import numpy as np
import ml_dtypes


def mxq(x, axis, fmt="e4m3"):
    dtype, down = {"e4m3": (ml_dtypes.float8_e4m3fn, 7), "e5m2": (ml_dtypes.float8_e5m2, 14)}[fmt]
    v = np.moveaxis(np.asarray(x, np.float32).astype(ml_dtypes.bfloat16).astype(np.float64), axis, -1)
    blocks = v.reshape(v.shape[:-1] + (-1, 32))
    amax = np.abs(blocks).max(-1, keepdims=True)
    byte = np.maximum(np.where(amax > 0, np.frexp(amax)[1] - 1 + 127, 0) - down, 1)
    scale = np.exp2(byte - 127.0)
    codes = (blocks / scale).astype(np.float32).astype(dtype).astype(np.float64)
    return np.moveaxis((codes * scale).reshape(v.shape), -1, axis)


WIDE = False


def mx_kscale(k):
    if not WIDE:
        return np.ones(k)
    levels = np.array([10, -10, 5, -5, 0])
    if k % 512:
        return np.exp2(np.random.permutation(np.resize(levels, k // 32))).repeat(32)
    a = np.empty((k // 512, 16))
    for p in range(k // 512):
        a[p, :8] = np.random.permutation(np.resize(levels, 8))
        for g in range(8):
            far = levels[np.abs(levels - a[p, g]) >= 10]
            a[p, g + 8] = far[np.random.randint(len(far))]
    return np.exp2(a.ravel()).repeat(32)


def f64(x):
    return np.asarray(x).astype(np.float64)


def striped(idx):
    return np.tile(idx.reshape(-1, 16).T, (8, 1)).astype(np.uint16)


def unstriped(offs):
    return offs[:16].T.reshape(-1).astype(np.int64)


E2M1 = np.array([0.0, 0.5, 1.0, 1.5, 2.0, 3.0, 4.0, 6.0, -0.0, -0.5, -1.0, -1.5, -2.0, -3.0, -4.0, -6.0])


def pack_weight(w, fmt):
    k, n = w.shape
    w = f64(np.asarray(w, np.float32).astype(ml_dtypes.bfloat16)).reshape(k // 32, 32, n)
    amax = np.abs(w).max(1)
    if fmt == "e4m3":
        byte = np.frexp(amax)[1] - 1 + 127 - 7
    else:
        mant, ex = np.frexp(amax / 6.0)
        byte = np.where(mant > 0.5, ex, ex - 1) + 127
    byte = np.clip(np.where(amax > 0, byte, 1), 1, 254)
    scaled = (w * np.exp2(127.0 - byte)[:, None, :]).reshape(k, n).astype(np.float32)
    by_word = np.ascontiguousarray(scaled.reshape(k // 512, 128, 4, n).transpose(0, 1, 3, 2))
    if fmt == "e4m3":
        words = by_word.astype(ml_dtypes.float8_e4m3fn).view(np.uint8)
    else:
        c = by_word.astype(ml_dtypes.float4_e2m1fn).view(np.uint8) & 0xF
        words = (c[..., 0::2] | (c[..., 1::2] << 4)).reshape(k // 512, 128, 2 * n)
    return np.ascontiguousarray(words), np.ascontiguousarray(byte.astype(np.uint8).reshape(k // 512, 16, n))


def unpack_weight(words, scales, fmt):
    g, _, n = scales.shape
    words = np.ascontiguousarray(words).reshape(g, 128, n, -1)
    if fmt == "e4m3":
        vals = words.view(ml_dtypes.float8_e4m3fn).astype(np.float64)
    else:
        nib = np.empty((g, 128, n, 4), np.uint8)
        nib[..., 0::2] = words & 0xF
        nib[..., 1::2] = words >> 4
        vals = E2M1[nib]
    vals = vals * np.repeat(np.exp2(scales.astype(np.float64) - 127.0), 8, axis=1)[..., None]
    return vals.transpose(0, 1, 3, 2).reshape(g * 512, n)


K, T, E1, C1, E2, C2, H = 512, 768, 6, 128, 3, 256, 512
N = 128


def by_expert(wq, xq, E, C):
    return np.concatenate([wq[e].T @ xq[:, e * C:(e + 1) * C] for e in range(E)], axis=1)


def setup_inputs():
    n = np.random.standard_normal
    s = mx_kscale(K)
    u = mx_kscale(H)
    slots1, slots2 = np.random.permutation(T), np.random.permutation(T)
    x = pack_weight(n((K, T)) * s[:, None], "e4m3")
    wa = [pack_weight(m, "e2m1") for m in n((E1, K, H)) / np.sqrt(K) / s[None, :, None]]
    wb = [pack_weight(m, "e2m1") for m in n((E2, K, H)) / np.sqrt(K) / s[None, :, None] * u]
    w2 = pack_weight(n((H, N)) / np.sqrt(H) / u[:, None], "e2m1")
    return {
        "x_words": x[0],
        "x_scales": x[1],
        "wa_words": np.stack([m[0] for m in wa]),
        "wa_scales": np.stack([m[1] for m in wa]),
        "wb_words": np.stack([m[0] for m in wb]),
        "wb_scales": np.stack([m[1] for m in wb]),
        "w2_words": w2[0],
        "w2_scales": w2[1],
        "offs": striped(slots1),
        "offs2": striped(slots2),
    }


def reference(x_words, x_scales, wa_words, wa_scales, wb_words, wb_scales, w2_words, w2_scales, offs, offs2):
    wa = np.stack([unpack_weight(wa_words[e], wa_scales[e], "e2m1") for e in range(E1)])
    wb = np.stack([unpack_weight(wb_words[e], wb_scales[e], "e2m1") for e in range(E2)])
    w2 = unpack_weight(w2_words, w2_scales, "e2m1")
    idx, idx2 = unstriped(offs), unstriped(offs2)
    x = unpack_weight(x_words, x_scales, "e4m3")
    a, c = np.zeros((H, T)), np.zeros((H, T))
    a[:, idx] = by_expert(wa, x[:, idx], E1, C1)
    c[:, idx2] = by_expert(wb, x[:, idx2], E2, C2)
    return w2.T @ mxq(a * c, 0, "e4m3")

@@ -1,0 +1,163 @@
+from contextlib import ExitStack
+
+import concourse.mybir as mybir
+from concourse.masks import make_identity
+
+K, T, E1, C1, E2, C2, H, N = 512, 768, 6, 128, 3, 256, 512, 128
+FLOPS = 2 * (2 * K * H * T) + 2 * H * N * T
+
+F32 = mybir.dt.float32
+BF16 = mybir.dt.bfloat16
+I32 = mybir.dt.int32
+U32 = mybir.dt.uint32
+U16 = mybir.dt.uint16
+U8 = mybir.dt.uint8
+FP8X4 = mybir.dt.float8_e4m3fn_x4
+FP4X4 = mybir.dt.float4_e2m1fn_x4
+MULT = mybir.AluOpType.mult
+
+P = 128
+PACK = 4
+GATHER = 256
+WINDOW = 1024
+HALF = T // 2
+CHUNK = 256
+
+
+def tile_moe_pool_none_kernel(
+    tc, x_words, x_scales, wa_words, wa_scales, wb_words, wb_scales, w2_words, w2_scales, offs, offs2, out
+):
+    nc = tc.nc
+    with ExitStack() as ctx:
+        keep = ctx.enter_context(tc.tile_pool(name="keep", bufs=1))
+        psum = ctx.enter_context(tc.psum_pool(name="psum", bufs=4))
+
+        list_a = keep.tile([P, T // 16], U16, name="list_a")
+        list_c = keep.tile([P, T // 16], U16, name="list_c")
+        xw = keep.tile([P, T], I32, name="xw", align_bytes=64)
+        xs = keep.tile([P, T], U8, name="xs", align_bytes=64)
+        wa_w = keep.tile([P, E1, 2 * H], U8, name="wa_w", align_bytes=64)
+        wa_s = keep.tile([P, E1, H], U8, name="wa_s", align_bytes=64)
+        wb_w = keep.tile([P, E2, 2 * H], U8, name="wb_w", align_bytes=64)
+        wb_s = keep.tile([P, E2, H], U8, name="wb_s", align_bytes=64)
+        w2_w = keep.tile([P, 2 * N], U8, name="w2_w", align_bytes=64)
+        w2_s = keep.tile([P, N], U8, name="w2_s", align_bytes=64)
+        ident = keep.tile([P, P], F32, name="ident")
+
+        nc.gpsimd.memset(xs[:].bitcast(I32), 0)
+        for plane in (wb_s, wa_s, w2_s):
+            nc.vector.memset(plane[:].bitcast(I32), 0)
+        make_identity(nc, ident[:])
+
+        def load_scales(queue, plane, rows):
+            for r in range(4):
+                queue.dma_start(out=plane[r:P:32].bitcast(I32), in_=rows[r:16:4].bitcast(I32))
+
+        nc.sync.dma_start(list_c[:], offs2)
+        load_scales(nc.scalar, xs, x_scales[0])
+        nc.sync.dma_start(out=xw[:], in_=x_words[0].rearrange("p t d -> p (t d)").bitcast(I32))
+        nc.sync.dma_start(out=wb_w[:].bitcast(I32), in_=wb_words[:, 0].rearrange("e p b -> p e b").bitcast(I32))
+        load_scales(nc.scalar, wb_s, wb_scales[:, 0].rearrange("e q i -> q e i"))
+        nc.sync.dma_start(list_a[:], offs)
+        load_scales(nc.sync, wa_s, wa_scales[:, 0].rearrange("e q i -> q e i"))
+        nc.sync.dma_start(out=wa_w[:].bitcast(I32), in_=wa_words[:, 0].rearrange("e p b -> p e b").bitcast(I32))
+        load_scales(nc.sync, w2_s, w2_scales[0])
+        nc.sync.dma_start(out=w2_w[:].bitcast(I32), in_=w2_words[0].bitcast(I32))
+
+        def experts(tag, offsets, w_words, w_scales, slots_per_expert):
+            gw = keep.tile([P, T], U32, name="gw_" + tag, align_bytes=64)
+            gs = keep.tile([P, T], U8, name="gs_" + tag, align_bytes=64)
+            by_slot = keep.tile([P, T // P, PACK, P], F32, name="by_slot_" + tag)
+            for g0 in range(0, T, GATHER):
+                cols = slice(g0, g0 + GATHER)
+                part = offsets[:, g0 // 16 : (g0 + GATHER) // 16]
+                nc.vector.tensor_copy(gw[:, cols], xw[:].bitcast(U32).indirect(part))
+                nc.vector.tensor_copy(gs[:, cols], xs[:].indirect(part))
+                for b in range(g0 // P, (g0 + GATHER) // P):
+                    e = b * P // slots_per_expert
+                    slots = slice(b * P, (b + 1) * P)
+                    acc = psum.tile([P, H], F32, name="acc")
+                    nc.tensor.matmul_mx(
+                        out=acc[:],
+                        lhsT=gw[:, slots].bitcast(FP8X4),
+                        lhsT_scale=gs[:, slots],
+                        rhs=w_words[:, e, :].bitcast(FP4X4),
+                        rhs_scale=w_scales[:, e, :],
+                        start=True,
+                        stop=True,
+                    )
+                    nc.scalar.copy(by_slot[:, b], acc[:].rearrange("p (m t) -> p t m", t=PACK))
+            return by_slot
+
+        def turn(tag, by_slot, t):
+            plane = keep.tile([P, T], F32, name="plane_%s%d" % (tag, t))
+            for h0 in range(0, T, HALF):
+                turned = psum.tile([P, HALF], F32, name="turned")
+                for b in range(h0 // P, (h0 + HALF) // P):
+                    nc.tensor.transpose(turned[:, b * P - h0 : (b + 1) * P - h0], by_slot[:, b, t, :], ident[:])
+                nc.scalar.copy(plane[:, h0 : h0 + HALF], turned[:])
+            return plane
+
+        def scatter(tag, plane, offsets, t):
+            window = keep.tile([P, WINDOW], F32, name="win_%s%d" % (tag, t))
+            if tag == "c" and t == 0:
+                for h0 in range(0, T, HALF):
+                    nc.vector.tensor_copy(window[:].indirect(offsets[:, h0 // 16 : (h0 + HALF) // 16]), plane[:, h0 : h0 + HALF])
+            else:
+                nc.vector.tensor_copy(window[:].indirect(offsets[:]), plane[:])
+            return window
+
+        c_slots = experts("c", list_c, wb_w, wb_s, C2)
+        c_planes = {t: turn("c", c_slots, t) for t in range(1)}
+        a_slots = experts("a", list_a, wa_w, wa_s, C1)
+
+        hb = keep.tile([P, PACK, T], BF16, name="hb", align_bytes=64)
+        n_chunks = T // CHUNK
+        hq = [keep.tile([P, CHUNK, PACK], BF16, name="hq%d" % j, align_bytes=64) for j in range(n_chunks)]
+        a_tok, c_tok, a_planes = {}, {}, {}
+
+        def product(t, cols):
+            nc.vector.tensor_tensor(hb[:, t, cols], a_tok[t][:, cols], c_tok[t][:, cols], MULT)
+
+        def place(t, j):
+            nc.scalar.copy(hq[j][:, :, t], hb[:, t, j * CHUNK : (j + 1) * CHUNK])
+
+        def finish(j, copy_out):
+            codes = keep.tile([P, CHUNK], U32, name="codes%d" % j, align_bytes=64)
+            scales = keep.tile([P, CHUNK], U8, name="scales%d" % j, align_bytes=64)
+            nc.vector.quantize_mx(out=codes[:].bitcast(FP8X4), scales=scales[:], in_=hq[j][:].rearrange("p c t -> p (c t)"))
+            acc = psum.tile([P, H], F32, name="acc")
+            nc.tensor.matmul_mx(
+                out=acc[:, :CHUNK],
+                lhsT=w2_w[:].bitcast(FP4X4),
+                lhsT_scale=w2_s[:],
+                rhs=codes[:].bitcast(FP8X4),
+                rhs_scale=scales[:],
+                start=True,
+                stop=True,
+            )
+            result = keep.tile([P, CHUNK], F32, name="result%d" % j)
+            copy_out(result[:], acc[:, :CHUNK])
+            nc.sync.dma_start(out=out[:, j * CHUNK : (j + 1) * CHUNK], in_=result[:])
+
+        order = ["c0", "c1", "a0", "a1", "h0", "c2", "h1", "a2", "c3", "h2", "a3"]
+        for step in order:
+            kind, t = step[0], int(step[1])
+            if kind == "c":
+                plane = c_planes[t] if t in c_planes else turn("c", c_slots, t)
+                c_tok[t] = scatter("c", plane, list_c, t)
+            elif kind == "a":
+                a_tok[t] = scatter("a", turn("a", a_slots, t), list_a, t)
+            else:
+                product(t, slice(0, T))
+                place(t, 0)
+                place(t, 1)
+        last = PACK - 1
+        for j in range(n_chunks):
+            product(last, slice(j * CHUNK, (j + 1) * CHUNK))
+            if j < 2:
+                place(last, j)
+        nc.vector.tensor_copy(hq[2][:], hb[:, :, 2 * CHUNK :].rearrange("p t c -> p c t"))
+        finish(0, nc.scalar.copy)
+        finish(2, nc.scalar.copy)
+        finish(1, nc.vector.tensor_copy)

@@ -18,10 +18,10 @@ MULT = mybir.AluOpType.mult
 
 P = 128
 PACK = 4
-GATHER = 256
+GATHER = 384
 WINDOW = 1024
 HALF = T // 2
-CHUNK = 256
+CHUNKS = [(0, 256, "scalar"), (256, 512, "vector"), (512, 640, "scalar"), (640, 768, "scalar")]
 
 
 def tile_moe_pool_none_kernel(
@@ -64,71 +64,79 @@ def tile_moe_pool_none_kernel(
         load_scales(nc.sync, w2_s, w2_scales[0])
         nc.sync.dma_start(out=w2_w[:].bitcast(I32), in_=w2_words[0].bitcast(I32))
 
-        def experts(tag, offsets, w_words, w_scales, slots_per_expert):
-            gw = keep.tile([P, T], U32, name="gw_" + tag, align_bytes=64)
-            gs = keep.tile([P, T], U8, name="gs_" + tag, align_bytes=64)
-            by_slot = keep.tile([P, T // P, PACK, P], F32, name="by_slot_" + tag)
-            for g0 in range(0, T, GATHER):
-                cols = slice(g0, g0 + GATHER)
-                part = offsets[:, g0 // 16 : (g0 + GATHER) // 16]
-                nc.vector.tensor_copy(gw[:, cols], xw[:].bitcast(U32).indirect(part))
-                nc.vector.tensor_copy(gs[:, cols], xs[:].indirect(part))
-                for b in range(g0 // P, (g0 + GATHER) // P):
-                    e = b * P // slots_per_expert
-                    slots = slice(b * P, (b + 1) * P)
-                    acc = psum.tile([P, H], F32, name="acc")
-                    nc.tensor.matmul_mx(
-                        out=acc[:],
-                        lhsT=gw[:, slots].bitcast(FP8X4),
-                        lhsT_scale=gs[:, slots],
-                        rhs=w_words[:, e, :].bitcast(FP4X4),
-                        rhs_scale=w_scales[:, e, :],
-                        start=True,
-                        stop=True,
-                    )
-                    nc.scalar.copy(by_slot[:, b], acc[:].rearrange("p (m t) -> p t m", t=PACK))
-            return by_slot
+        def experts(tag, offsets, w_words, w_scales, slots_per_expert, gathered, half):
+            gw, gs, by_slot = gathered
+            cols = slice(half * HALF, (half + 1) * HALF)
+            part = offsets[:, half * HALF // 16 : (half + 1) * HALF // 16]
+            nc.vector.tensor_copy(gs[:, cols], xs[:].indirect(part))
+            nc.vector.tensor_copy(gw[:, cols], xw[:].bitcast(U32).indirect(part))
+            for b in range(half * HALF // P, (half + 1) * HALF // P):
+                e = b * P // slots_per_expert
+                slots = slice(b * P, (b + 1) * P)
+                acc = psum.tile([P, H], F32, name="acc")
+                nc.tensor.matmul_mx(
+                    out=acc[:],
+                    lhsT=gw[:, slots].bitcast(FP8X4),
+                    lhsT_scale=gs[:, slots],
+                    rhs=w_words[:, e, :].bitcast(FP4X4),
+                    rhs_scale=w_scales[:, e, :],
+                    start=True,
+                    stop=True,
+                )
+                nc.scalar.copy(by_slot[:, b], acc[:].rearrange("p (m t) -> p t m", t=PACK))
 
-        def turn(tag, by_slot, t):
-            plane = keep.tile([P, T], F32, name="plane_%s%d" % (tag, t))
-            for h0 in range(0, T, HALF):
-                turned = psum.tile([P, HALF], F32, name="turned")
-                for b in range(h0 // P, (h0 + HALF) // P):
-                    nc.tensor.transpose(turned[:, b * P - h0 : (b + 1) * P - h0], by_slot[:, b, t, :], ident[:])
-                nc.scalar.copy(plane[:, h0 : h0 + HALF], turned[:])
-            return plane
+        def pool_tiles(tag):
+            return (
+                keep.tile([P, T], U32, name="gw_" + tag, align_bytes=64),
+                keep.tile([P, T], U8, name="gs_" + tag, align_bytes=64),
+                keep.tile([P, T // P, PACK, P], F32, name="by_slot_" + tag),
+            )
 
-        def scatter(tag, plane, offsets, t):
-            window = keep.tile([P, WINDOW], F32, name="win_%s%d" % (tag, t))
-            if tag == "c" and t == 0:
-                for h0 in range(0, T, HALF):
-                    nc.vector.tensor_copy(window[:].indirect(offsets[:, h0 // 16 : (h0 + HALF) // 16]), plane[:, h0 : h0 + HALF])
-            else:
-                nc.vector.tensor_copy(window[:].indirect(offsets[:]), plane[:])
-            return window
+        def turn(by_slot, t, plane, half):
+            h0 = half * HALF
+            turned = psum.tile([P, HALF], F32, name="turned")
+            for b in range(h0 // P, (h0 + HALF) // P):
+                nc.tensor.transpose(turned[:, b * P - h0 : (b + 1) * P - h0], by_slot[:, b, t, :], ident[:])
+            nc.scalar.copy(plane[:, h0 : h0 + HALF], turned[:])
 
-        c_slots = experts("c", list_c, wb_w, wb_s, C2)
-        c_planes = {t: turn("c", c_slots, t) for t in range(1)}
-        a_slots = experts("a", list_a, wa_w, wa_s, C1)
+        tiles = {"c": pool_tiles("c"), "a": pool_tiles("a")}
+        lists = {"c": list_c, "a": list_a}
+        planes = {(s, t): keep.tile([P, T], F32, name="plane_%s%d" % (s, t)) for s in "ca" for t in range(PACK)}
+        wins = {(s, t): keep.tile([P, WINDOW], F32, name="win_%s%d" % (s, t)) for s in "ca" for t in range(PACK)}
 
+        def scatter(s, t, lo, hi):
+            nc.vector.tensor_copy(wins[s, t][:].indirect(lists[s][:, lo // 16 : hi // 16]), planes[s, t][:, lo:hi])
+
+        for half in range(2):
+            experts("c", list_c, wb_w, wb_s, C2, tiles["c"], half)
+            for t in range(2):
+                turn(tiles["c"][2], t, planes["c", t], half)
+        for half in range(2):
+            experts("a", list_a, wa_w, wa_s, C1, tiles["a"], half)
+        for half in range(2):
+            for t in range(2):
+                scatter("c", t, half * HALF, (half + 1) * HALF)
+
+        chunks = CHUNKS
         hb = keep.tile([P, PACK, T], BF16, name="hb", align_bytes=64)
-        n_chunks = T // CHUNK
-        hq = [keep.tile([P, CHUNK, PACK], BF16, name="hq%d" % j, align_bytes=64) for j in range(n_chunks)]
-        a_tok, c_tok, a_planes = {}, {}, {}
+        hq = [keep.tile([P, hi - lo, PACK], BF16, name="hq%d" % j, align_bytes=64) for j, (lo, hi, who) in enumerate(chunks)]
 
-        def product(t, cols):
-            nc.vector.tensor_tensor(hb[:, t, cols], a_tok[t][:, cols], c_tok[t][:, cols], MULT)
+        def product(engine, t, lo, hi):
+            engine.tensor_tensor(hb[:, t, lo:hi], wins["a", t][:, lo:hi], wins["c", t][:, lo:hi], MULT)
 
         def place(t, j):
-            nc.scalar.copy(hq[j][:, :, t], hb[:, t, j * CHUNK : (j + 1) * CHUNK])
+            lo, hi, who = chunks[j]
+            if who == "scalar":
+                nc.scalar.copy(hq[j][:, :, t], hb[:, t, lo:hi])
 
         def finish(j, copy_out):
-            codes = keep.tile([P, CHUNK], U32, name="codes%d" % j, align_bytes=64)
-            scales = keep.tile([P, CHUNK], U8, name="scales%d" % j, align_bytes=64)
+            lo, hi, who = chunks[j]
+            codes = keep.tile([P, hi - lo], U32, name="codes%d" % j, align_bytes=64)
+            scales = keep.tile([P, hi - lo], U8, name="scales%d" % j, align_bytes=64)
             nc.vector.quantize_mx(out=codes[:].bitcast(FP8X4), scales=scales[:], in_=hq[j][:].rearrange("p c t -> p (c t)"))
             acc = psum.tile([P, H], F32, name="acc")
             nc.tensor.matmul_mx(
-                out=acc[:, :CHUNK],
+                out=acc[:, : hi - lo],
                 lhsT=w2_w[:].bitcast(FP4X4),
                 lhsT_scale=w2_s[:],
                 rhs=codes[:].bitcast(FP8X4),
@@ -136,28 +144,24 @@ def tile_moe_pool_none_kernel(
                 start=True,
                 stop=True,
             )
-            result = keep.tile([P, CHUNK], F32, name="result%d" % j)
-            copy_out(result[:], acc[:, :CHUNK])
-            nc.sync.dma_start(out=out[:, j * CHUNK : (j + 1) * CHUNK], in_=result[:])
+            result = keep.tile([P, hi - lo], F32, name="result%d" % j)
+            copy_out(result[:], acc[:, : hi - lo])
+            nc.sync.dma_start(out=out[:, lo:hi], in_=result[:])
 
-        order = ["c0", "c1", "a0", "a1", "h0", "c2", "h1", "a2", "c3", "h2", "a3"]
-        for step in order:
-            kind, t = step[0], int(step[1])
-            if kind == "c":
-                plane = c_planes[t] if t in c_planes else turn("c", c_slots, t)
-                c_tok[t] = scatter("c", plane, list_c, t)
-            elif kind == "a":
-                a_tok[t] = scatter("a", turn("a", a_slots, t), list_a, t)
-            else:
-                product(t, slice(0, T))
-                place(t, 0)
-                place(t, 1)
         last = PACK - 1
-        for j in range(n_chunks):
-            product(last, slice(j * CHUNK, (j + 1) * CHUNK))
-            if j < 2:
-                place(last, j)
-        nc.vector.tensor_copy(hq[2][:], hb[:, :, 2 * CHUNK :].rearrange("p t c -> p c t"))
-        finish(0, nc.scalar.copy)
-        finish(2, nc.scalar.copy)
-        finish(1, nc.vector.tensor_copy)
+        for s, t in [("a", 0), ("a", 1), ("c", 2), ("a", 2), ("c", 3), ("a", 3)]:
+            for half in range(2):
+                turn(tiles[s][2], t, planes[s, t], half)
+            scatter(s, t, 0, T)
+            if s == "a" and t < last:
+                product(nc.gpsimd, t, 0, T)
+                for j in range(len(chunks)):
+                    place(t, j)
+        for j, (lo, hi, who) in enumerate(chunks):
+            product(nc.vector, last, lo, hi)
+            place(last, j)
+        for j, (lo, hi, who) in enumerate(chunks):
+            if who == "vector":
+                nc.vector.tensor_copy(hq[j][:], hb[:, :, lo:hi].rearrange("p t c -> p c t"))
+        for j in range(len(chunks)):
+            finish(j, nc.vector.tensor_copy if j == len(chunks) - 1 else nc.scalar.copy)

@@ -3,7 +3,9 @@ from contextlib import ExitStack
 import concourse.mybir as mybir
 from concourse.masks import make_identity
 
-K, T, E1, C1, E2, C2, H, N = 512, 768, 6, 128, 3, 256, 512, 128
+K, T, H, N = 512, 768, 512, 128
+EXPERTS_A, SLOTS_A = 6, 128
+EXPERTS_C, SLOTS_C = 3, 256
 FLOPS = 2 * (2 * K * H * T) + 2 * H * N * T
 
 F32 = mybir.dt.float32
@@ -14,14 +16,15 @@ U16 = mybir.dt.uint16
 U8 = mybir.dt.uint8
 FP8X4 = mybir.dt.float8_e4m3fn_x4
 FP4X4 = mybir.dt.float4_e2m1fn_x4
-MULT = mybir.AluOpType.mult
 
 P = 128
 PACK = 4
-GATHER = 384
-WINDOW = 1024
+PER_COLUMN = 16
+BANK = 512
 HALF = T // 2
-CHUNKS = [(0, 256, "scalar"), (256, 512, "vector"), (512, 640, "scalar"), (640, 768, "scalar")]
+WINDOW = 1024
+PSUM_BUFS = 4
+RANGES = [(0, 256, "scalar"), (256, 512, "vector"), (512, 640, "scalar"), (640, 768, "scalar")]
 
 
 def tile_moe_pool_none_kernel(
@@ -30,138 +33,173 @@ def tile_moe_pool_none_kernel(
     nc = tc.nc
     with ExitStack() as ctx:
         keep = ctx.enter_context(tc.tile_pool(name="keep", bufs=1))
-        psum = ctx.enter_context(tc.psum_pool(name="psum", bufs=4))
+        psum = ctx.enter_context(tc.psum_pool(name="psum", bufs=PSUM_BUFS))
 
-        list_a = keep.tile([P, T // 16], U16, name="list_a")
-        list_c = keep.tile([P, T // 16], U16, name="list_c")
-        xw = keep.tile([P, T], I32, name="xw", align_bytes=64)
-        xs = keep.tile([P, T], U8, name="xs", align_bytes=64)
-        wa_w = keep.tile([P, E1, 2 * H], U8, name="wa_w", align_bytes=64)
-        wa_s = keep.tile([P, E1, H], U8, name="wa_s", align_bytes=64)
-        wb_w = keep.tile([P, E2, 2 * H], U8, name="wb_w", align_bytes=64)
-        wb_s = keep.tile([P, E2, H], U8, name="wb_s", align_bytes=64)
+        list_a = keep.tile([P, T // PER_COLUMN], U16, name="list_a")
+        list_c = keep.tile([P, T // PER_COLUMN], U16, name="list_c")
+        x_w = keep.tile([P, T], I32, name="x_w", align_bytes=64)
+        x_s = keep.tile([P, T], U8, name="x_s", align_bytes=64)
+        wa_w = keep.tile([P, EXPERTS_A, 2 * H], U8, name="wa_w", align_bytes=64)
+        wa_s = keep.tile([P, EXPERTS_A, H], U8, name="wa_s", align_bytes=64)
+        wb_w = keep.tile([P, EXPERTS_C, 2 * H], U8, name="wb_w", align_bytes=64)
+        wb_s = keep.tile([P, EXPERTS_C, H], U8, name="wb_s", align_bytes=64)
         w2_w = keep.tile([P, 2 * N], U8, name="w2_w", align_bytes=64)
         w2_s = keep.tile([P, N], U8, name="w2_s", align_bytes=64)
         ident = keep.tile([P, P], F32, name="ident")
 
-        nc.gpsimd.memset(xs[:].bitcast(I32), 0)
-        for plane in (wb_s, wa_s, w2_s):
-            nc.vector.memset(plane[:].bitcast(I32), 0)
+        nc.gpsimd.memset(x_s[:].bitcast(I32), 0)
+        for scale_tile in (wb_s, wa_s, w2_s):
+            nc.vector.memset(scale_tile[:].bitcast(I32), 0)
         make_identity(nc, ident[:])
 
-        def load_scales(queue, plane, rows):
+        def load_scales(queue, scale_tile, rows):
             for r in range(4):
-                queue.dma_start(out=plane[r:P:32].bitcast(I32), in_=rows[r:16:4].bitcast(I32))
+                queue.dma_start(out=scale_tile[r:P:32].bitcast(I32), in_=rows[r:16:4].bitcast(I32))
 
         nc.sync.dma_start(list_c[:], offs2)
-        load_scales(nc.scalar, xs, x_scales[0])
-        nc.sync.dma_start(out=xw[:], in_=x_words[0].rearrange("p t d -> p (t d)").bitcast(I32))
+        load_scales(nc.scalar, x_s, x_scales[0])
+        nc.sync.dma_start(out=x_w[:], in_=x_words[0].rearrange("p t d -> p (t d)").bitcast(I32))
         nc.sync.dma_start(out=wb_w[:].bitcast(I32), in_=wb_words[:, 0].rearrange("e p b -> p e b").bitcast(I32))
-        load_scales(nc.scalar, wb_s, wb_scales[:, 0].rearrange("e q i -> q e i"))
+        load_scales(nc.scalar, wb_s, wb_scales[:, 0].rearrange("e g i -> g e i"))
         nc.sync.dma_start(list_a[:], offs)
-        load_scales(nc.sync, wa_s, wa_scales[:, 0].rearrange("e q i -> q e i"))
+        load_scales(nc.sync, wa_s, wa_scales[:, 0].rearrange("e g i -> g e i"))
         nc.sync.dma_start(out=wa_w[:].bitcast(I32), in_=wa_words[:, 0].rearrange("e p b -> p e b").bitcast(I32))
         load_scales(nc.sync, w2_s, w2_scales[0])
         nc.sync.dma_start(out=w2_w[:].bitcast(I32), in_=w2_words[0].bitcast(I32))
 
-        def experts(tag, offsets, w_words, w_scales, slots_per_expert, gathered, half):
-            gw, gs, by_slot = gathered
-            cols = slice(half * HALF, (half + 1) * HALF)
-            part = offsets[:, half * HALF // 16 : (half + 1) * HALF // 16]
-            nc.vector.tensor_copy(gs[:, cols], xs[:].indirect(part))
-            nc.vector.tensor_copy(gw[:, cols], xw[:].bitcast(U32).indirect(part))
-            for b in range(half * HALF // P, (half + 1) * HALF // P):
-                e = b * P // slots_per_expert
-                slots = slice(b * P, (b + 1) * P)
-                acc = psum.tile([P, H], F32, name="acc")
-                nc.tensor.matmul_mx(
-                    out=acc[:],
-                    lhsT=gw[:, slots].bitcast(FP8X4),
-                    lhsT_scale=gs[:, slots],
-                    rhs=w_words[:, e, :].bitcast(FP4X4),
-                    rhs_scale=w_scales[:, e, :],
-                    start=True,
-                    stop=True,
-                )
-                nc.scalar.copy(by_slot[:, b], acc[:].rearrange("p (m t) -> p t m", t=PACK))
+        lists = {"a": list_a, "c": list_c}
+        weights = {"a": (wa_w, wa_s, SLOTS_A), "c": (wb_w, wb_s, SLOTS_C)}
+        slot_words, slot_scales, sums, in_slots, in_tokens = {}, {}, {}, {}, {}
+        for pool in "ca":
+            slot_words[pool] = keep.tile([P, T], U32, name="slot_words_" + pool, align_bytes=64)
+            slot_scales[pool] = keep.tile([P, T], U8, name="slot_scales_" + pool, align_bytes=64)
+            sums[pool] = keep.tile([P, T // P, PACK, P], F32, name="sums_" + pool)
+        for pool in "ca":
+            for t in range(PACK):
+                in_slots[pool, t] = keep.tile([P, T], F32, name="in_slots_%s%d" % (pool, t))
+        for pool in "ca":
+            for t in range(PACK):
+                in_tokens[pool, t] = keep.tile([P, WINDOW], F32, name="in_tokens_%s%d" % (pool, t))
+        block0 = keep.tile([P, PACK, P], F32, name="block0")
 
-        def pool_tiles(tag):
-            return (
-                keep.tile([P, T], U32, name="gw_" + tag, align_bytes=64),
-                keep.tile([P, T], U8, name="gs_" + tag, align_bytes=64),
-                keep.tile([P, T // P, PACK, P], F32, name="by_slot_" + tag),
-            )
+        def entries(pool, lo, hi):
+            return lists[pool][:, lo // PER_COLUMN : hi // PER_COLUMN]
 
-        def turn(by_slot, t, plane, half):
-            h0 = half * HALF
-            turned = psum.tile([P, HALF], F32, name="turned")
-            for b in range(h0 // P, (h0 + HALF) // P):
-                nc.tensor.transpose(turned[:, b * P - h0 : (b + 1) * P - h0], by_slot[:, b, t, :], ident[:])
-            nc.scalar.copy(plane[:, h0 : h0 + HALF], turned[:])
+        def gather(pool, lo, hi):
+            nc.vector.tensor_copy(slot_words[pool][:, lo:hi], x_w[:].bitcast(U32).indirect(entries(pool, lo, hi)))
+            nc.vector.tensor_copy(slot_scales[pool][:, lo:hi], x_s[:].indirect(entries(pool, lo, hi)))
 
-        tiles = {"c": pool_tiles("c"), "a": pool_tiles("a")}
-        lists = {"c": list_c, "a": list_a}
-        planes = {(s, t): keep.tile([P, T], F32, name="plane_%s%d" % (s, t)) for s in "ca" for t in range(PACK)}
-        wins = {(s, t): keep.tile([P, WINDOW], F32, name="win_%s%d" % (s, t)) for s in "ca" for t in range(PACK)}
-
-        def scatter(s, t, lo, hi):
-            nc.vector.tensor_copy(wins[s, t][:].indirect(lists[s][:, lo // 16 : hi // 16]), planes[s, t][:, lo:hi])
-
-        for half in range(2):
-            experts("c", list_c, wb_w, wb_s, C2, tiles["c"], half)
-            for t in range(2):
-                turn(tiles["c"][2], t, planes["c", t], half)
-        for half in range(2):
-            experts("a", list_a, wa_w, wa_s, C1, tiles["a"], half)
-        for half in range(2):
-            for t in range(2):
-                scatter("c", t, half * HALF, (half + 1) * HALF)
-
-        chunks = CHUNKS
-        hb = keep.tile([P, PACK, T], BF16, name="hb", align_bytes=64)
-        hq = [keep.tile([P, hi - lo, PACK], BF16, name="hq%d" % j, align_bytes=64) for j, (lo, hi, who) in enumerate(chunks)]
-
-        def product(engine, t, lo, hi):
-            engine.tensor_tensor(hb[:, t, lo:hi], wins["a", t][:, lo:hi], wins["c", t][:, lo:hi], MULT)
-
-        def place(t, j):
-            lo, hi, who = chunks[j]
-            if who == "scalar":
-                nc.scalar.copy(hq[j][:, :, t], hb[:, t, lo:hi])
-
-        def finish(j, copy_out):
-            lo, hi, who = chunks[j]
-            codes = keep.tile([P, hi - lo], U32, name="codes%d" % j, align_bytes=64)
-            scales = keep.tile([P, hi - lo], U8, name="scales%d" % j, align_bytes=64)
-            nc.vector.quantize_mx(out=codes[:].bitcast(FP8X4), scales=scales[:], in_=hq[j][:].rearrange("p c t -> p (c t)"))
-            acc = psum.tile([P, H], F32, name="acc")
+        def expert_sums(pool, b):
+            w_words, w_scales, slots_per_expert = weights[pool]
+            e = b * P // slots_per_expert
+            slots = slice(b * P, (b + 1) * P)
+            acc = psum.tile([P, BANK], F32, name="acc")
             nc.tensor.matmul_mx(
-                out=acc[:, : hi - lo],
-                lhsT=w2_w[:].bitcast(FP4X4),
-                lhsT_scale=w2_s[:],
-                rhs=codes[:].bitcast(FP8X4),
-                rhs_scale=scales[:],
+                out=acc[:],
+                lhsT=slot_words[pool][:, slots].bitcast(FP8X4),
+                lhsT_scale=slot_scales[pool][:, slots],
+                rhs=w_words[:, e, :].bitcast(FP4X4),
+                rhs_scale=w_scales[:, e, :],
                 start=True,
                 stop=True,
             )
-            result = keep.tile([P, hi - lo], F32, name="result%d" % j)
-            copy_out(result[:], acc[:, : hi - lo])
-            nc.sync.dma_start(out=out[:, lo:hi], in_=result[:])
+            nc.scalar.copy(sums[pool][:, b], acc[:].rearrange("u (m t) -> u t m", t=PACK))
+
+        def turn(pool, t, lo, hi):
+            turned = psum.tile([P, BANK], F32, name="turned")
+            for b in range(lo // P, hi // P):
+                nc.tensor.transpose(turned[:, b * P - lo : (b + 1) * P - lo], sums[pool][:, b, t, :], ident[:])
+            nc.scalar.copy(in_slots[pool, t][:, lo:hi], turned[:, : hi - lo])
+
+        def turn_block0():
+            turned = psum.tile([P, BANK], F32, name="turned")
+            for t in range(PACK):
+                nc.tensor.transpose(turned[:, t * P : (t + 1) * P], sums["c"][:, 0, t, :], ident[:])
+            nc.scalar.copy(block0[:].rearrange("p t u -> p (t u)"), turned[:])
+
+        def turn_from(pool, t, lo):
+            turn(pool, t, lo, BANK)
+            turn(pool, t, BANK, T)
+
+        def scatter(pool, t, lo, hi, values):
+            nc.vector.tensor_copy(in_tokens[pool, t][:].indirect(entries(pool, lo, hi)), values)
+
+        for lo in range(0, T, HALF):
+            gather("c", lo, lo + HALF)
+            for b in range(lo // P, (lo + HALF) // P):
+                expert_sums("c", b)
+                if b == 0:
+                    turn_block0()
+        early_parts = range(2)
+        for t in early_parts:
+            turn_from("c", t, P)
+        for lo in range(0, T, HALF):
+            gather("a", lo, lo + HALF)
+            for b in range(lo // P, (lo + HALF) // P):
+                expert_sums("a", b)
+        for t in range(PACK):
+            scatter("c", t, 0, P, block0[:, t, :])
+        for t in early_parts:
+            scatter("c", t, P, T, in_slots["c", t][:, P:])
+
+        h_parts = keep.tile([P, PACK, T], BF16, name="h_parts", align_bytes=64)
+        h_words = [
+            keep.tile([P, hi - lo, PACK], BF16, name="h_words%d" % j, align_bytes=64)
+            for j, (lo, hi, layer) in enumerate(RANGES)
+        ]
+
+        def multiply(engine, t, lo, hi):
+            engine.tensor_tensor(
+                h_parts[:, t, lo:hi], in_tokens["a", t][:, lo:hi], in_tokens["c", t][:, lo:hi], mybir.AluOpType.mult
+            )
+
+        def lay_part_on_scalar(t, j):
+            lo, hi, layer = RANGES[j]
+            if layer == "scalar":
+                nc.scalar.copy(h_words[j][:, :, t], h_parts[:, t, lo:hi])
+
+        def project(j):
+            lo, hi, layer = RANGES[j]
+            width = hi - lo
+            h_codes = keep.tile([P, width], U32, name="h_codes%d" % j, align_bytes=64)
+            h_scales = keep.tile([P, width], U8, name="h_scales%d" % j, align_bytes=64)
+            nc.vector.quantize_mx(
+                out=h_codes[:].bitcast(FP8X4), scales=h_scales[:], in_=h_words[j][:].rearrange("p c t -> p (c t)")
+            )
+            acc = psum.tile([P, BANK], F32, name="acc")
+            nc.tensor.matmul_mx(
+                out=acc[:, :width],
+                lhsT=w2_w[:].bitcast(FP4X4),
+                lhsT_scale=w2_s[:],
+                rhs=h_codes[:].bitcast(FP8X4),
+                rhs_scale=h_scales[:],
+                start=True,
+                stop=True,
+            )
+            result = keep.tile([P, width], F32, name="result%d" % j)
+            copy_out = nc.vector.tensor_copy if j == len(RANGES) - 1 else nc.scalar.copy
+            copy_out(result[:], acc[:, :width])
+            queue = nc.scalar if j == len(RANGES) - 2 else nc.sync
+            queue.dma_start(out=out[:, lo:hi], in_=result[:])
 
         last = PACK - 1
-        for s, t in [("a", 0), ("a", 1), ("c", 2), ("a", 2), ("c", 3), ("a", 3)]:
-            for half in range(2):
-                turn(tiles[s][2], t, planes[s, t], half)
-            scatter(s, t, 0, T)
-            if s == "a" and t < last:
-                product(nc.gpsimd, t, 0, T)
-                for j in range(len(chunks)):
-                    place(t, j)
-        for j, (lo, hi, who) in enumerate(chunks):
-            product(nc.vector, last, lo, hi)
-            place(last, j)
-        for j, (lo, hi, who) in enumerate(chunks):
-            if who == "vector":
-                nc.vector.tensor_copy(hq[j][:], hb[:, :, lo:hi].rearrange("p t c -> p c t"))
-        for j in range(len(chunks)):
-            finish(j, nc.vector.tensor_copy if j == len(chunks) - 1 else nc.scalar.copy)
+        for pool, t in [("a", 0), ("a", 1), ("c", 2), ("a", 2), ("c", 3), ("a", 3)]:
+            lo = P if pool == "c" else 0
+            turn_from(pool, t, lo)
+            scatter(pool, t, lo, T, in_slots[pool, t][:, lo:])
+            if pool == "a" and t < last:
+                multiply(nc.gpsimd, t, 0, T)
+                for j in range(len(RANGES)):
+                    lay_part_on_scalar(t, j)
+
+        for j, (lo, hi, layer) in enumerate(RANGES):
+            multiply(nc.vector, last, lo, hi)
+            lay_part_on_scalar(last, j)
+        for j, (lo, hi, layer) in enumerate(RANGES):
+            if layer == "vector":
+                nc.vector.tensor_copy(
+                    h_words[j][:].rearrange("p (c i) t -> p c t i", i=PACK),
+                    h_parts[:, :, lo:hi].rearrange("p t (c i) -> p c t i", i=PACK),
+                )
+        for j in range(len(RANGES)):
+            project(j)

@@ -21,9 +21,8 @@ P = 128
 PACK = 4
 PER_COLUMN = 16
 BANK = 512
-HALF = T // 2
+FIRST = SLOTS_C
 WINDOW = 1024
-PSUM_BUFS = 4
 RANGES = [(0, 256, "scalar"), (256, 512, "vector"), (512, 640, "scalar"), (640, 768, "scalar")]
 
 
@@ -33,17 +32,19 @@ def tile_moe_pool_none_kernel(
     nc = tc.nc
     with ExitStack() as ctx:
         keep = ctx.enter_context(tc.tile_pool(name="keep", bufs=1))
-        psum = ctx.enter_context(tc.psum_pool(name="psum", bufs=PSUM_BUFS))
+        psum = ctx.enter_context(tc.psum_pool(name="psum", bufs=1))
+
+        def bank(n):
+            return psum.tile([P, BANK], F32, name="bank%d" % n)
+
 
         list_a = keep.tile([P, T // PER_COLUMN], U16, name="list_a")
         list_c = keep.tile([P, T // PER_COLUMN], U16, name="list_c")
-        x_w = keep.tile([P, T], I32, name="x_w", align_bytes=64)
-        x_s = keep.tile([P, T], U8, name="x_s", align_bytes=64)
-        wa_w = keep.tile([P, EXPERTS_A, 2 * H], U8, name="wa_w", align_bytes=64)
+        x_w = keep.tile([P, WINDOW], I32, name="x_w", align_bytes=64)
+        x_s = keep.tile([P, WINDOW], U8, name="x_s", align_bytes=64)
+        wb_w = keep.tile([P, EXPERTS_C, 2 * H], U8, name="wb_w", tag="expert_words", align_bytes=64)
+        wb_s = keep.tile([P, EXPERTS_C, H], U8, name="wb_s", tag="wb_s", align_bytes=64)
         wa_s = keep.tile([P, EXPERTS_A, H], U8, name="wa_s", align_bytes=64)
-        wb_w = keep.tile([P, EXPERTS_C, 2 * H], U8, name="wb_w", align_bytes=64)
-        wb_s = keep.tile([P, EXPERTS_C, H], U8, name="wb_s", align_bytes=64)
-        w2_w = keep.tile([P, 2 * N], U8, name="w2_w", align_bytes=64)
         w2_s = keep.tile([P, N], U8, name="w2_s", align_bytes=64)
         ident = keep.tile([P, P], F32, name="ident")
 
@@ -57,43 +58,39 @@ def tile_moe_pool_none_kernel(
                 queue.dma_start(out=scale_tile[r:P:32].bitcast(I32), in_=rows[r:16:4].bitcast(I32))
 
         nc.sync.dma_start(list_c[:], offs2)
-        load_scales(nc.scalar, x_s, x_scales[0])
-        nc.sync.dma_start(out=x_w[:], in_=x_words[0].rearrange("p t d -> p (t d)").bitcast(I32))
+        load_scales(nc.scalar, x_s[:, :T], x_scales[0])
+        nc.sync.dma_start(out=x_w[:, :T], in_=x_words[0].rearrange("p t d -> p (t d)").bitcast(I32))
         nc.sync.dma_start(out=wb_w[:].bitcast(I32), in_=wb_words[:, 0].rearrange("e p b -> p e b").bitcast(I32))
-        load_scales(nc.scalar, wb_s, wb_scales[:, 0].rearrange("e g i -> g e i"))
         nc.sync.dma_start(list_a[:], offs)
+        load_scales(nc.sync, wb_s, wb_scales[:, 0].rearrange("e g i -> g e i"))
         load_scales(nc.sync, wa_s, wa_scales[:, 0].rearrange("e g i -> g e i"))
-        nc.sync.dma_start(out=wa_w[:].bitcast(I32), in_=wa_words[:, 0].rearrange("e p b -> p e b").bitcast(I32))
         load_scales(nc.sync, w2_s, w2_scales[0])
-        nc.sync.dma_start(out=w2_w[:].bitcast(I32), in_=w2_words[0].bitcast(I32))
 
         lists = {"a": list_a, "c": list_c}
-        weights = {"a": (wa_w, wa_s, SLOTS_A), "c": (wb_w, wb_s, SLOTS_C)}
+        weights = {"c": (wb_w, wb_s, SLOTS_C)}
         slot_words, slot_scales, sums, in_slots, in_tokens = {}, {}, {}, {}, {}
         for pool in "ca":
             slot_words[pool] = keep.tile([P, T], U32, name="slot_words_" + pool, align_bytes=64)
             slot_scales[pool] = keep.tile([P, T], U8, name="slot_scales_" + pool, align_bytes=64)
-            sums[pool] = keep.tile([P, T // P, PACK, P], F32, name="sums_" + pool)
+            sums[pool] = keep.tile([P, T // P, PACK, P], F32, name="sums_" + pool, align_bytes=64)
         for pool in "ca":
             for t in range(PACK):
                 in_slots[pool, t] = keep.tile([P, T], F32, name="in_slots_%s%d" % (pool, t))
-        for pool in "ca":
-            for t in range(PACK):
-                in_tokens[pool, t] = keep.tile([P, WINDOW], F32, name="in_tokens_%s%d" % (pool, t))
-        block0 = keep.tile([P, PACK, P], F32, name="block0")
 
         def entries(pool, lo, hi):
             return lists[pool][:, lo // PER_COLUMN : hi // PER_COLUMN]
 
-        def gather(pool, lo, hi):
+        def gather_words(pool, lo, hi):
             nc.vector.tensor_copy(slot_words[pool][:, lo:hi], x_w[:].bitcast(U32).indirect(entries(pool, lo, hi)))
+
+        def gather_scales(pool, lo, hi):
             nc.vector.tensor_copy(slot_scales[pool][:, lo:hi], x_s[:].indirect(entries(pool, lo, hi)))
 
-        def expert_sums(pool, b):
+        def expert_product(pool, b, n):
             w_words, w_scales, slots_per_expert = weights[pool]
             e = b * P // slots_per_expert
             slots = slice(b * P, (b + 1) * P)
-            acc = psum.tile([P, BANK], F32, name="acc")
+            acc = bank(n)
             nc.tensor.matmul_mx(
                 out=acc[:],
                 lhsT=slot_words[pool][:, slots].bitcast(FP8X4),
@@ -103,44 +100,68 @@ def tile_moe_pool_none_kernel(
                 start=True,
                 stop=True,
             )
-            nc.scalar.copy(sums[pool][:, b], acc[:].rearrange("u (m t) -> u t m", t=PACK))
+            return acc
 
-        def turn(pool, t, lo, hi):
-            turned = psum.tile([P, BANK], F32, name="turned")
+        def empty(pool, b, acc, t_lo, t_hi):
+            nc.scalar.copy(sums[pool][:, b, t_lo:t_hi], acc[:].rearrange("u (m t) -> u t m", t=PACK)[:, t_lo:t_hi])
+
+        def expert_sums(pool, b, n):
+            empty(pool, b, expert_product(pool, b, n), 0, PACK)
+
+        def turn(pool, t, lo, hi, n):
+            turned = bank(n)
             for b in range(lo // P, hi // P):
                 nc.tensor.transpose(turned[:, b * P - lo : (b + 1) * P - lo], sums[pool][:, b, t, :], ident[:])
             nc.scalar.copy(in_slots[pool, t][:, lo:hi], turned[:, : hi - lo])
 
-        def turn_block0():
-            turned = psum.tile([P, BANK], F32, name="turned")
-            for t in range(PACK):
-                nc.tensor.transpose(turned[:, t * P : (t + 1) * P], sums["c"][:, 0, t, :], ident[:])
-            nc.scalar.copy(block0[:].rearrange("p t u -> p (t u)"), turned[:])
-
-        def turn_from(pool, t, lo):
-            turn(pool, t, lo, BANK)
-            turn(pool, t, BANK, T)
+        def turn_whole(pool, t, n):
+            turn(pool, t, 0, BANK, n)
+            turn(pool, t, BANK, T, n + 1)
 
         def scatter(pool, t, lo, hi, values):
+            if lo == 0:
+                place = min(t, PACK - 2) if pool == "a" else t
+                in_tokens[pool, t] = keep.tile([P, WINDOW], F32, name="in_tokens_%s%d" % (pool, place))
             nc.vector.tensor_copy(in_tokens[pool, t][:].indirect(entries(pool, lo, hi)), values)
 
-        for lo in range(0, T, HALF):
-            gather("c", lo, lo + HALF)
-            for b in range(lo // P, (lo + HALF) // P):
-                expert_sums("c", b)
-                if b == 0:
-                    turn_block0()
-        early_parts = range(2)
+        for pool in "ca":
+            gather_words(pool, 0, T)
+            gather_scales(pool, 0, T)
+        early = 2
+        early_parts = range(early)
+        first_blocks = range(FIRST // P)
+        first = keep.tile([P, early, FIRST], F32, name="first")
+        accs = [expert_product("c", b, b) for b in first_blocks]
+        for b in first_blocks:
+            empty("c", b, accs[b], 0, early)
+        turned = bank(2)
+        for b in first_blocks:
+            for t in early_parts:
+                nc.tensor.transpose(turned[:, t * FIRST + b * P : t * FIRST + (b + 1) * P], sums["c"][:, b, t, :], ident[:])
+        nc.scalar.copy(first[:].rearrange("p t u -> p (t u)"), turned[:])
+        for b in first_blocks:
+            empty("c", b, accs[b], early, PACK)
+        for b in range(FIRST // P, T // P):
+            expert_sums("c", b, (b - FIRST // P) % 3)
+        wa_w = keep.tile([P, EXPERTS_A, 2 * H], U8, name="wa_w", tag="expert_words", align_bytes=64)
+        nc.sync.dma_start(out=wa_w[:].bitcast(I32), in_=wa_words[:, 0].rearrange("e p b -> p e b").bitcast(I32))
+        weights["a"] = (wa_w, wa_s, SLOTS_A)
+        w2_w = keep.tile([P, 2 * N], U8, name="w2_w", tag="wb_s", align_bytes=64)
+        nc.sync.dma_start(out=w2_w[:].bitcast(I32), in_=w2_words[0].bitcast(I32))
         for t in early_parts:
-            turn_from("c", t, P)
-        for lo in range(0, T, HALF):
-            gather("a", lo, lo + HALF)
-            for b in range(lo // P, (lo + HALF) // P):
-                expert_sums("a", b)
-        for t in range(PACK):
-            scatter("c", t, 0, P, block0[:, t, :])
+            turn("c", t, FIRST, T, 3 + t)
+        turn_whole("c", 2, 3)
+        for b in range(T // P):
+            expert_sums("a", b, (b + 1) % 3)
         for t in early_parts:
-            scatter("c", t, P, T, in_slots["c", t][:, P:])
+            scatter("c", t, 0, FIRST, first[:, t, :])
+        for t in early_parts:
+            scatter("c", t, FIRST, T, in_slots["c", t][:, FIRST:])
+
+        scatter("c", 2, 0, T, in_slots["c", 2][:])
+        later = [("a", 0), ("a", 1), ("a", 2), ("c", 3), ("a", 3)]
+        for (pool, t), n in zip(later, (5, 3, 5, 5, 3)):
+            turn_whole(pool, t, n)
 
         h_parts = keep.tile([P, PACK, T], BF16, name="h_parts", align_bytes=64)
         h_words = [
@@ -153,10 +174,9 @@ def tile_moe_pool_none_kernel(
                 h_parts[:, t, lo:hi], in_tokens["a", t][:, lo:hi], in_tokens["c", t][:, lo:hi], mybir.AluOpType.mult
             )
 
-        def lay_part_on_scalar(t, j):
+        def lay_on_scalar(t, j):
             lo, hi, layer = RANGES[j]
-            if layer == "scalar":
-                nc.scalar.copy(h_words[j][:, :, t], h_parts[:, t, lo:hi])
+            nc.scalar.copy(h_words[j][:, :, t], h_parts[:, t, lo:hi])
 
         def project(j):
             lo, hi, layer = RANGES[j]
@@ -166,7 +186,7 @@ def tile_moe_pool_none_kernel(
             nc.vector.quantize_mx(
                 out=h_codes[:].bitcast(FP8X4), scales=h_scales[:], in_=h_words[j][:].rearrange("p c t -> p (c t)")
             )
-            acc = psum.tile([P, BANK], F32, name="acc")
+            acc = bank((7, 0, 1, 2)[j])
             nc.tensor.matmul_mx(
                 out=acc[:, :width],
                 lhsT=w2_w[:].bitcast(FP4X4),
@@ -183,23 +203,24 @@ def tile_moe_pool_none_kernel(
             queue.dma_start(out=out[:, lo:hi], in_=result[:])
 
         last = PACK - 1
-        for pool, t in [("a", 0), ("a", 1), ("c", 2), ("a", 2), ("c", 3), ("a", 3)]:
-            lo = P if pool == "c" else 0
-            turn_from(pool, t, lo)
-            scatter(pool, t, lo, T, in_slots[pool, t][:, lo:])
+        for pool, t in later:
+            scatter(pool, t, 0, T, in_slots[pool, t][:])
             if pool == "a" and t < last:
                 multiply(nc.gpsimd, t, 0, T)
-                for j in range(len(RANGES)):
-                    lay_part_on_scalar(t, j)
+                for j, (lo, hi, layer) in enumerate(RANGES):
+                    if layer == "scalar" or t < last - 1:
+                        lay_on_scalar(t, j)
 
+        third = T // 3
+        for lo in range(0, T, third):
+            multiply(nc.vector, last, lo, lo + third)
         for j, (lo, hi, layer) in enumerate(RANGES):
-            multiply(nc.vector, last, lo, hi)
-            lay_part_on_scalar(last, j)
-        for j, (lo, hi, layer) in enumerate(RANGES):
-            if layer == "vector":
+            if layer == "scalar":
+                lay_on_scalar(last, j)
+            else:
                 nc.vector.tensor_copy(
-                    h_words[j][:].rearrange("p (c i) t -> p c t i", i=PACK),
-                    h_parts[:, :, lo:hi].rearrange("p t (c i) -> p c t i", i=PACK),
+                    h_words[j][:, :, last - 1 :].rearrange("p (c i) t -> p c t i", i=PACK),
+                    h_parts[:, last - 1 :, lo:hi].rearrange("p t (c i) -> p c t i", i=PACK),
                 )
         for j in range(len(RANGES)):
             project(j)

@@ -23,7 +23,7 @@ PER_COLUMN = 16
 BANK = 512
 FIRST = SLOTS_C
 WINDOW = 1024
-RANGES = [(0, 256, "scalar"), (256, 512, "vector"), (512, 640, "scalar"), (640, 768, "scalar")]
+RANGES = [(0, 128), (128, 384), (384, 640), (640, 768)]
 
 
 def tile_moe_pool_none_kernel(
@@ -57,9 +57,9 @@ def tile_moe_pool_none_kernel(
             for r in range(4):
                 queue.dma_start(out=scale_tile[r:P:32].bitcast(I32), in_=rows[r:16:4].bitcast(I32))
 
-        nc.sync.dma_start(list_c[:], offs2)
-        load_scales(nc.scalar, x_s[:, :T], x_scales[0])
         nc.sync.dma_start(out=x_w[:, :T], in_=x_words[0].rearrange("p t d -> p (t d)").bitcast(I32))
+        nc.sync.dma_start(list_c[:], offs2)
+        load_scales(nc.sync, x_s[:, :T], x_scales[0])
         nc.sync.dma_start(out=wb_w[:].bitcast(I32), in_=wb_words[:, 0].rearrange("e p b -> p e b").bitcast(I32))
         nc.sync.dma_start(list_a[:], offs)
         load_scales(nc.sync, wb_s, wb_scales[:, 0].rearrange("e g i -> g e i"))
@@ -124,103 +124,103 @@ def tile_moe_pool_none_kernel(
                 in_tokens[pool, t] = keep.tile([P, WINDOW], F32, name="in_tokens_%s%d" % (pool, place))
             nc.vector.tensor_copy(in_tokens[pool, t][:].indirect(entries(pool, lo, hi)), values)
 
-        for pool in "ca":
-            gather_words(pool, 0, T)
-            gather_scales(pool, 0, T)
+        gather_words("c", 0, T)
+        gather_scales("c", 0, FIRST)
+        gather_scales("c", FIRST, T)
+        gather_words("a", 0, T)
+        gather_scales("a", 0, T)
         early = 2
-        early_parts = range(early)
-        first_blocks = range(FIRST // P)
-        first = keep.tile([P, early, FIRST], F32, name="first")
-        accs = [expert_product("c", b, b) for b in first_blocks]
-        for b in first_blocks:
+        blocks = range(T // P)
+        accs = []
+        for b in blocks:
+            accs.append(expert_product("c", b, b))
             empty("c", b, accs[b], 0, early)
-        turned = bank(2)
-        for b in first_blocks:
-            for t in early_parts:
-                nc.tensor.transpose(turned[:, t * FIRST + b * P : t * FIRST + (b + 1) * P], sums["c"][:, b, t, :], ident[:])
-        nc.scalar.copy(first[:].rearrange("p t u -> p (t u)"), turned[:])
-        for b in first_blocks:
+            if (b + 1) * P == FIRST:
+                turn("c", 0, 0, FIRST, 6)
+        turn("c", 1, 0, BANK, 7)
+        turn("c", 1, BANK, T, 6)
+        turn("c", 0, FIRST, T, 7)
+        for b in blocks:
             empty("c", b, accs[b], early, PACK)
-        for b in range(FIRST // P, T // P):
-            expert_sums("c", b, (b - FIRST // P) % 3)
         wa_w = keep.tile([P, EXPERTS_A, 2 * H], U8, name="wa_w", tag="expert_words", align_bytes=64)
         nc.sync.dma_start(out=wa_w[:].bitcast(I32), in_=wa_words[:, 0].rearrange("e p b -> p e b").bitcast(I32))
         weights["a"] = (wa_w, wa_s, SLOTS_A)
         w2_w = keep.tile([P, 2 * N], U8, name="w2_w", tag="wb_s", align_bytes=64)
         nc.sync.dma_start(out=w2_w[:].bitcast(I32), in_=w2_words[0].bitcast(I32))
-        for t in early_parts:
-            turn("c", t, FIRST, T, 3 + t)
-        turn_whole("c", 2, 3)
+        turn_whole("c", 2, 6)
         for b in range(T // P):
-            expert_sums("a", b, (b + 1) % 3)
-        for t in early_parts:
-            scatter("c", t, 0, FIRST, first[:, t, :])
-        for t in early_parts:
-            scatter("c", t, FIRST, T, in_slots["c", t][:, FIRST:])
+            expert_sums("a", b, b % 3)
+        scatter("c", 0, 0, FIRST, in_slots["c", 0][:, :FIRST])
+        scatter("c", 1, 0, T, in_slots["c", 1][:])
+        scatter("c", 0, FIRST, T, in_slots["c", 0][:, FIRST:])
 
         scatter("c", 2, 0, T, in_slots["c", 2][:])
         later = [("a", 0), ("a", 1), ("a", 2), ("c", 3), ("a", 3)]
-        for (pool, t), n in zip(later, (5, 3, 5, 5, 3)):
+        for (pool, t), n in zip(later, (3, 6, 3, 3, 6)):
             turn_whole(pool, t, n)
 
-        h_parts = keep.tile([P, PACK, T], BF16, name="h_parts", align_bytes=64)
+        h_pairs = [keep.tile([P, 2, hi - lo, 2], BF16, name="h_pairs%d" % j) for j, (lo, hi) in enumerate(RANGES)]
         h_words = [
             keep.tile([P, hi - lo, PACK], BF16, name="h_words%d" % j, align_bytes=64)
-            for j, (lo, hi, layer) in enumerate(RANGES)
+            for j, (lo, hi) in enumerate(RANGES)
         ]
 
-        def multiply(engine, t, lo, hi):
+        def multiply(engine, t, j):
+            lo, hi = RANGES[j]
             engine.tensor_tensor(
-                h_parts[:, t, lo:hi], in_tokens["a", t][:, lo:hi], in_tokens["c", t][:, lo:hi], mybir.AluOpType.mult
+                h_pairs[j][:, t // 2, :, t % 2],
+                in_tokens["a", t][:, lo:hi],
+                in_tokens["c", t][:, lo:hi],
+                mybir.AluOpType.mult,
             )
 
-        def lay_on_scalar(t, j):
-            lo, hi, layer = RANGES[j]
-            nc.scalar.copy(h_words[j][:, :, t], h_parts[:, t, lo:hi])
+        def weave(j):
+            on_vector = j == len(RANGES) - 1
+            copy, word = (nc.vector.tensor_copy, I32) if on_vector else (nc.scalar.copy, U32)
+            copy(
+                h_words[j][:].rearrange("p c t -> p (c t)").bitcast(word).rearrange("p (c w) -> p c w", w=2),
+                h_pairs[j][:].rearrange("p w c e -> p w (c e)").bitcast(word).rearrange("p w c -> p c w"),
+            )
 
         def project(j):
-            lo, hi, layer = RANGES[j]
+            lo, hi = RANGES[j]
             width = hi - lo
             h_codes = keep.tile([P, width], U32, name="h_codes%d" % j, align_bytes=64)
             h_scales = keep.tile([P, width], U8, name="h_scales%d" % j, align_bytes=64)
             nc.vector.quantize_mx(
                 out=h_codes[:].bitcast(FP8X4), scales=h_scales[:], in_=h_words[j][:].rearrange("p c t -> p (c t)")
             )
-            acc = bank((7, 0, 1, 2)[j])
-            nc.tensor.matmul_mx(
-                out=acc[:, :width],
-                lhsT=w2_w[:].bitcast(FP4X4),
-                lhsT_scale=w2_s[:],
-                rhs=h_codes[:].bitcast(FP8X4),
-                rhs_scale=h_scales[:],
-                start=True,
-                stop=True,
-            )
-            result = keep.tile([P, width], F32, name="result%d" % j)
-            copy_out = nc.vector.tensor_copy if j == len(RANGES) - 1 else nc.scalar.copy
-            copy_out(result[:], acc[:, :width])
-            queue = nc.scalar if j == len(RANGES) - 2 else nc.sync
-            queue.dma_start(out=out[:, lo:hi], in_=result[:])
+            for first, count, n, copy_out, queue in PIECES[j]:
+                acc = bank(n)
+                nc.tensor.matmul_mx(
+                    out=acc[:, :count],
+                    lhsT=w2_w[:].bitcast(FP4X4),
+                    lhsT_scale=w2_s[:],
+                    rhs=h_codes[:, first : first + count].bitcast(FP8X4),
+                    rhs_scale=h_scales[:, first : first + count],
+                    start=True,
+                    stop=True,
+                )
+                result = keep.tile([P, count], F32, name="result%d" % n)
+                copy_out(result[:], acc[:, :count])
+                queue.dma_start(out=out[:, lo + first : lo + first + count], in_=result[:])
+
+        PIECES = [
+            [(0, 128, 5, nc.scalar.copy, nc.sync)],
+            [(0, 256, 0, nc.scalar.copy, nc.sync)],
+            [(0, 128, 1, nc.scalar.copy, nc.scalar), (128, 128, 3, nc.vector.tensor_copy, nc.sync)],
+            [(0, 128, 2, nc.vector.tensor_copy, nc.sync)],
+        ]
 
         last = PACK - 1
         for pool, t in later:
             scatter(pool, t, 0, T, in_slots[pool, t][:])
             if pool == "a" and t < last:
-                multiply(nc.gpsimd, t, 0, T)
-                for j, (lo, hi, layer) in enumerate(RANGES):
-                    if layer == "scalar" or t < last - 1:
-                        lay_on_scalar(t, j)
+                for j in range(len(RANGES)):
+                    multiply(nc.gpsimd, t, j)
 
-        third = T // 3
-        for lo in range(0, T, third):
-            multiply(nc.vector, last, lo, lo + third)
-        for j, (lo, hi, layer) in enumerate(RANGES):
-            if layer == "scalar":
-                lay_on_scalar(last, j)
-            else:
-                nc.vector.tensor_copy(
-                    h_words[j][:, :, last - 1 :].rearrange("p (c i) t -> p c t i", i=PACK),
-                    h_parts[:, last - 1 :, lo:hi].rearrange("p t (c i) -> p c t i", i=PACK),
-                )
+        for j in range(len(RANGES)):
+            multiply(nc.vector, last, j)
+            weave(j)
         for j in range(len(RANGES)):
             project(j)

@@ -43,14 +43,11 @@ def tile_moe_pool_none_kernel(
         x_w = keep.tile([P, WINDOW], I32, name="x_w", align_bytes=64)
         x_s = keep.tile([P, WINDOW], U8, name="x_s", align_bytes=64)
         wb_w = keep.tile([P, EXPERTS_C, 2 * H], U8, name="wb_w", tag="expert_words", align_bytes=64)
-        wb_s = keep.tile([P, EXPERTS_C, H], U8, name="wb_s", tag="wb_s", align_bytes=64)
-        wa_s = keep.tile([P, EXPERTS_A, H], U8, name="wa_s", align_bytes=64)
-        w2_s = keep.tile([P, N], U8, name="w2_s", align_bytes=64)
+        wb_s = keep.tile([P, EXPERTS_C, H], U8, name="wb_s", tag="weight_scales", align_bytes=64)
         ident = keep.tile([P, P], F32, name="ident")
 
         nc.gpsimd.memset(x_s[:].bitcast(I32), 0)
-        for scale_tile in (wb_s, wa_s, w2_s):
-            nc.vector.memset(scale_tile[:].bitcast(I32), 0)
+        nc.vector.memset(wb_s[:].bitcast(I32), 0)
         make_identity(nc, ident[:])
 
         def load_scales(queue, scale_tile, rows):
@@ -59,12 +56,10 @@ def tile_moe_pool_none_kernel(
 
         nc.sync.dma_start(out=x_w[:, :T], in_=x_words[0].rearrange("p t d -> p (t d)").bitcast(I32))
         nc.sync.dma_start(list_c[:], offs2)
-        load_scales(nc.sync, x_s[:, :T], x_scales[0])
+        load_scales(nc.scalar, x_s[:, :T], x_scales[0])
         nc.sync.dma_start(out=wb_w[:].bitcast(I32), in_=wb_words[:, 0].rearrange("e p b -> p e b").bitcast(I32))
         nc.sync.dma_start(list_a[:], offs)
-        load_scales(nc.sync, wb_s, wb_scales[:, 0].rearrange("e g i -> g e i"))
-        load_scales(nc.sync, wa_s, wa_scales[:, 0].rearrange("e g i -> g e i"))
-        load_scales(nc.sync, w2_s, w2_scales[0])
+        load_scales(nc.scalar, wb_s, wb_scales[:, 0].rearrange("e g i -> g e i"))
 
         lists = {"a": list_a, "c": list_c}
         weights = {"c": (wb_w, wb_s, SLOTS_C)}
@@ -136,23 +131,29 @@ def tile_moe_pool_none_kernel(
             accs.append(expert_product("c", b, b))
             empty("c", b, accs[b], 0, early)
             if (b + 1) * P == FIRST:
-                turn("c", 0, 0, FIRST, 6)
-        turn("c", 1, 0, BANK, 7)
-        turn("c", 1, BANK, T, 6)
-        turn("c", 0, FIRST, T, 7)
+                for t in range(early):
+                    turn("c", t, 0, FIRST, 6 + t)
+        for t in range(early):
+            turn("c", t, FIRST, T, 6 + t)
         for b in blocks:
             empty("c", b, accs[b], early, PACK)
         wa_w = keep.tile([P, EXPERTS_A, 2 * H], U8, name="wa_w", tag="expert_words", align_bytes=64)
         nc.sync.dma_start(out=wa_w[:].bitcast(I32), in_=wa_words[:, 0].rearrange("e p b -> p e b").bitcast(I32))
+        wa_s = keep.tile([P, EXPERTS_A, H], U8, name="wa_s", tag="weight_scales", align_bytes=64)
+        nc.gpsimd.memset(wa_s[:].bitcast(I32), 0)
+        load_scales(nc.sync, wa_s, wa_scales[:, 0].rearrange("e g i -> g e i"))
         weights["a"] = (wa_w, wa_s, SLOTS_A)
-        w2_w = keep.tile([P, 2 * N], U8, name="w2_w", tag="wb_s", align_bytes=64)
-        nc.sync.dma_start(out=w2_w[:].bitcast(I32), in_=w2_words[0].bitcast(I32))
         turn_whole("c", 2, 6)
         for b in range(T // P):
             expert_sums("a", b, b % 3)
-        scatter("c", 0, 0, FIRST, in_slots["c", 0][:, :FIRST])
-        scatter("c", 1, 0, T, in_slots["c", 1][:])
-        scatter("c", 0, FIRST, T, in_slots["c", 0][:, FIRST:])
+        w2_w = keep.tile([P, 2 * N], U8, name="w2_w", tag="expert_words", align_bytes=64)
+        nc.sync.dma_start(out=w2_w[:].bitcast(I32), in_=w2_words[0].bitcast(I32))
+        w2_s = keep.tile([P, N], U8, name="w2_s", tag="weight_scales", align_bytes=64)
+        nc.gpsimd.memset(w2_s[:].bitcast(I32), 0)
+        load_scales(nc.sync, w2_s, w2_scales[0])
+        for lo, hi in ((0, FIRST), (FIRST, T)):
+            for t in range(early):
+                scatter("c", t, lo, hi, in_slots["c", t][:, lo:hi])
 
         scatter("c", 2, 0, T, in_slots["c", 2][:])
         later = [("a", 0), ("a", 1), ("a", 2), ("c", 3), ("a", 3)]

@@ -23,7 +23,7 @@ PER_COLUMN = 16
 BANK = 512
 FIRST = SLOTS_C
 WINDOW = 1024
-RANGES = [(0, 128), (128, 384), (384, 640), (640, 768)]
+RANGES = [(0, 128), (128, 384), (384, 512), (512, 768)]
 
 
 def tile_moe_pool_none_kernel(
@@ -161,21 +161,20 @@ def tile_moe_pool_none_kernel(
             turn_whole(pool, t, n)
 
         h_pairs = [keep.tile([P, 2, hi - lo, 2], BF16, name="h_pairs%d" % j) for j, (lo, hi) in enumerate(RANGES)]
-        h_words = [
-            keep.tile([P, hi - lo, PACK], BF16, name="h_words%d" % j, align_bytes=64)
-            for j, (lo, hi) in enumerate(RANGES)
-        ]
+        h_words = {}
 
-        def multiply(engine, t, j):
+        def multiply(engine, t, j, c_part):
             lo, hi = RANGES[j]
             engine.tensor_tensor(
                 h_pairs[j][:, t // 2, :, t % 2],
                 in_tokens["a", t][:, lo:hi],
-                in_tokens["c", t][:, lo:hi],
+                c_part[:, lo:hi],
                 mybir.AluOpType.mult,
             )
 
         def weave(j):
+            lo, hi = RANGES[j]
+            h_words[j] = keep.tile([P, hi - lo, PACK], BF16, name="h_words%d" % j, align_bytes=64)
             on_vector = j == len(RANGES) - 1
             copy, word = (nc.vector.tensor_copy, I32) if on_vector else (nc.scalar.copy, U32)
             copy(
@@ -208,9 +207,9 @@ def tile_moe_pool_none_kernel(
 
         PIECES = [
             [(0, 128, 5, nc.scalar.copy, nc.sync)],
-            [(0, 256, 0, nc.scalar.copy, nc.sync)],
-            [(0, 128, 1, nc.scalar.copy, nc.scalar), (128, 128, 3, nc.vector.tensor_copy, nc.sync)],
-            [(0, 128, 2, nc.vector.tensor_copy, nc.sync)],
+            [(0, 128, 0, nc.vector.tensor_copy, nc.sync), (128, 128, 3, nc.vector.tensor_copy, nc.sync)],
+            [(0, 128, 2, nc.scalar.copy, nc.scalar)],
+            [(0, 256, 1, nc.scalar.copy, nc.sync)],
         ]
 
         last = PACK - 1
@@ -218,10 +217,22 @@ def tile_moe_pool_none_kernel(
             scatter(pool, t, 0, T, in_slots[pool, t][:])
             if pool == "a" and t < last:
                 for j in range(len(RANGES)):
-                    multiply(nc.gpsimd, t, j)
+                    multiply(nc.gpsimd, t, j, in_tokens["c", t])
+            if (pool, t) == ("c", last):
+                there, back = bank(6), bank(7)
+                between = keep.tile([P, BANK], F32, name="h_words%d" % (len(RANGES) - 1), align_bytes=64)
+                for b in range(BANK // P):
+                    cols = slice(b * P, (b + 1) * P)
+                    nc.tensor.transpose(there[:, cols], in_tokens[pool, t][:, cols], ident[:])
+                nc.scalar.copy(between[:], there[:])
+                for b in range(BANK // P):
+                    cols = slice(b * P, (b + 1) * P)
+                    nc.tensor.transpose(back[:, cols], between[:, cols], ident[:])
 
-        for j in range(len(RANGES)):
-            multiply(nc.vector, last, j)
+        multiply(nc.gpsimd, last, 3, in_tokens["c", last])
+        for j in range(3):
+            multiply(nc.vector, last, j, back)
+        for j in range(4):
             weave(j)
-        for j in range(len(RANGES)):
+        for j in (0, 3, 1, 2):
             project(j)

@@ -22,6 +22,7 @@ PACK = 4
 PER_COLUMN = 16
 BANK = 512
 FIRST = SLOTS_C
+WARM_UPS = 3
 WINDOW = 1024
 RANGES = [(0, 128), (128, 384), (384, 512), (512, 768)]
 
@@ -146,8 +147,6 @@ def tile_moe_pool_none_kernel(
         turn_whole("c", 2, 6)
         for b in range(T // P):
             expert_sums("a", b, b % 3)
-        w2_w = keep.tile([P, 2 * N], U8, name="w2_w", tag="expert_words", align_bytes=64)
-        nc.sync.dma_start(out=w2_w[:].bitcast(I32), in_=w2_words[0].bitcast(I32))
         w2_s = keep.tile([P, N], U8, name="w2_s", tag="weight_scales", align_bytes=64)
         nc.gpsimd.memset(w2_s[:].bitcast(I32), 0)
         load_scales(nc.sync, w2_s, w2_scales[0])
@@ -220,14 +219,28 @@ def tile_moe_pool_none_kernel(
                     multiply(nc.gpsimd, t, j, in_tokens["c", t])
             if (pool, t) == ("c", last):
                 there, back = bank(6), bank(7)
-                between = keep.tile([P, BANK], F32, name="h_words%d" % (len(RANGES) - 1), align_bytes=64)
                 for b in range(BANK // P):
                     cols = slice(b * P, (b + 1) * P)
                     nc.tensor.transpose(there[:, cols], in_tokens[pool, t][:, cols], ident[:])
-                nc.scalar.copy(between[:], there[:])
-                for b in range(BANK // P):
-                    cols = slice(b * P, (b + 1) * P)
-                    nc.tensor.transpose(back[:, cols], between[:, cols], ident[:])
+                for half, place in enumerate(("w2_w", "h_words%d" % (len(RANGES) - 1))):
+                    between = keep.tile([P, 2, P], F32, name=place, align_bytes=64)
+                    nc.scalar.copy(between[:], there[:].rearrange("u (b m) -> u b m", m=P)[:, 2 * half : 2 * half + 2])
+                    for b in range(2):
+                        cols = slice((2 * half + b) * P, (2 * half + b + 1) * P)
+                        nc.tensor.transpose(back[:, cols], between[:, b, :], ident[:])
+
+        w2_w = keep.tile([P, 2 * N], U8, name="w2_w", align_bytes=64)
+        nc.sync.dma_start(out=w2_w[:].bitcast(I32), in_=w2_words[0].bitcast(I32))
+        for n in range(WARM_UPS):
+            nc.tensor.matmul_mx(
+                out=bank(4 + 2 * (n % 2))[:],
+                lhsT=w2_w[:].bitcast(FP4X4),
+                lhsT_scale=w2_s[:],
+                rhs=slot_words["a"][:, :BANK].bitcast(FP8X4),
+                rhs_scale=slot_scales["a"][:, :BANK],
+                start=True,
+                stop=True,
+            )
 
         multiply(nc.gpsimd, last, 3, in_tokens["c", last])
         for j in range(3):

@@ -47,7 +47,6 @@ def tile_moe_pool_none_kernel(
         wb_s = keep.tile([P, EXPERTS_C, H], U8, name="wb_s", tag="weight_scales", align_bytes=64)
         ident = keep.tile([P, P], F32, name="ident")
 
-        nc.gpsimd.memset(x_s[:].bitcast(I32), 0)
         nc.vector.memset(wb_s[:].bitcast(I32), 0)
         make_identity(nc, ident[:])
 
@@ -55,12 +54,17 @@ def tile_moe_pool_none_kernel(
             for r in range(4):
                 queue.dma_start(out=scale_tile[r:P:32].bitcast(I32), in_=rows[r:16:4].bitcast(I32))
 
-        nc.sync.dma_start(out=x_w[:, :T], in_=x_words[0].rearrange("p t d -> p (t d)").bitcast(I32))
+        def load_token_scales(queue, q):
+            rows = x_scales[0, 4 * q : 4 * q + 4].bitcast(I32)
+            queue.dma_start(out=x_s[32 * q : 32 * q + 32, :T].bitcast(I32), in_=rows.partition_broadcast(8))
+
         nc.sync.dma_start(list_c[:], offs2)
-        load_scales(nc.scalar, x_s[:, :T], x_scales[0])
+        for q in range(4):
+            load_token_scales(nc.sync if q < 2 else nc.scalar, q)
+        nc.sync.dma_start(out=x_w[:, :T], in_=x_words[0].rearrange("p t d -> p (t d)").bitcast(I32))
         nc.sync.dma_start(out=wb_w[:].bitcast(I32), in_=wb_words[:, 0].rearrange("e p b -> p e b").bitcast(I32))
         nc.sync.dma_start(list_a[:], offs)
-        load_scales(nc.scalar, wb_s, wb_scales[:, 0].rearrange("e g i -> g e i"))
+        load_scales(nc.sync, wb_s, wb_scales[:, 0].rearrange("e g i -> g e i"))
 
         lists = {"a": list_a, "c": list_c}
         weights = {"c": (wb_w, wb_s, SLOTS_C)}
@@ -120,9 +124,9 @@ def tile_moe_pool_none_kernel(
                 in_tokens[pool, t] = keep.tile([P, WINDOW], F32, name="in_tokens_%s%d" % (pool, place))
             nc.vector.tensor_copy(in_tokens[pool, t][:].indirect(entries(pool, lo, hi)), values)
 
-        gather_words("c", 0, T)
-        gather_scales("c", 0, FIRST)
-        gather_scales("c", FIRST, T)
+        gather_scales("c", 0, T)
+        gather_words("c", 0, FIRST)
+        gather_words("c", FIRST, T)
         gather_words("a", 0, T)
         gather_scales("a", 0, T)
         early = 2

@@ -22,7 +22,7 @@ PACK = 4
 PER_COLUMN = 16
 BANK = 512
 FIRST = SLOTS_C
-WARM_UPS = 3
+WARM_UPS = (512, 512, 512, 128)
 WINDOW = 1024
 RANGES = [(0, 128), (128, 384), (384, 512), (512, 768)]
 
@@ -75,7 +75,7 @@ def tile_moe_pool_none_kernel(
             sums[pool] = keep.tile([P, T // P, PACK, P], F32, name="sums_" + pool, align_bytes=64)
         for pool in "ca":
             for t in range(PACK):
-                in_slots[pool, t] = keep.tile([P, T], F32, name="in_slots_%s%d" % (pool, t))
+                in_slots[pool, t] = keep.tile([P, T], F32, name="in_slots_%s%d" % (pool, t), align_bytes=64)
 
         def entries(pool, lo, hi):
             return lists[pool][:, lo // PER_COLUMN : hi // PER_COLUMN]
@@ -151,9 +151,8 @@ def tile_moe_pool_none_kernel(
         turn_whole("c", 2, 6)
         for b in range(T // P):
             expert_sums("a", b, b % 3)
-        w2_s = keep.tile([P, N], U8, name="w2_s", tag="weight_scales", align_bytes=64)
-        nc.gpsimd.memset(w2_s[:].bitcast(I32), 0)
-        load_scales(nc.sync, w2_s, w2_scales[0])
+        w2_w = keep.tile([P, 2 * N], U8, name="w2_w", tag="expert_words", align_bytes=64)
+        nc.sync.dma_start(out=w2_w[:].bitcast(I32), in_=w2_words[0].bitcast(I32))
         for lo, hi in ((0, FIRST), (FIRST, T)):
             for t in range(early):
                 scatter("c", t, lo, hi, in_slots["c", t][:, lo:hi])
@@ -226,22 +225,23 @@ def tile_moe_pool_none_kernel(
                 for b in range(BANK // P):
                     cols = slice(b * P, (b + 1) * P)
                     nc.tensor.transpose(there[:, cols], in_tokens[pool, t][:, cols], ident[:])
-                for half, place in enumerate(("w2_w", "h_words%d" % (len(RANGES) - 1))):
+                for half, place in enumerate(("between", "h_words%d" % (len(RANGES) - 1))):
                     between = keep.tile([P, 2, P], F32, name=place, align_bytes=64)
                     nc.scalar.copy(between[:], there[:].rearrange("u (b m) -> u b m", m=P)[:, 2 * half : 2 * half + 2])
                     for b in range(2):
                         cols = slice((2 * half + b) * P, (2 * half + b + 1) * P)
                         nc.tensor.transpose(back[:, cols], between[:, b, :], ident[:])
 
-        w2_w = keep.tile([P, 2 * N], U8, name="w2_w", align_bytes=64)
-        nc.sync.dma_start(out=w2_w[:].bitcast(I32), in_=w2_words[0].bitcast(I32))
-        for n in range(WARM_UPS):
+        w2_s = keep.tile([P, N], U8, name="in_slots_c%d" % last, align_bytes=64)
+        nc.gpsimd.memset(w2_s[:].bitcast(I32), 0)
+        load_scales(nc.sync, w2_s, w2_scales[0])
+        for n, count in enumerate(WARM_UPS):
             nc.tensor.matmul_mx(
-                out=bank(4 + 2 * (n % 2))[:],
+                out=bank(4 + 2 * (n % 2))[:, :count],
                 lhsT=w2_w[:].bitcast(FP4X4),
                 lhsT_scale=w2_s[:],
-                rhs=slot_words["a"][:, :BANK].bitcast(FP8X4),
-                rhs_scale=slot_scales["a"][:, :BANK],
+                rhs=slot_words["a"][:, :count].bitcast(FP8X4),
+                rhs_scale=slot_scales["a"][:, :count],
                 start=True,
                 stop=True,
             )

@@ -1,11 +1,10 @@
 from contextlib import ExitStack
 
 import concourse.mybir as mybir
-from concourse.masks import make_identity
 
 K, T, H, N = 512, 768, 512, 128
-EXPERTS_A, SLOTS_A = 6, 128
-EXPERTS_C, SLOTS_C = 3, 256
+EXPERTS = {"a": 6, "c": 3}
+SLOTS = {"a": 128, "c": 256}
 FLOPS = 2 * (2 * K * H * T) + 2 * H * N * T
 
 F32 = mybir.dt.float32
@@ -16,15 +15,16 @@ U16 = mybir.dt.uint16
 U8 = mybir.dt.uint8
 FP8X4 = mybir.dt.float8_e4m3fn_x4
 FP4X4 = mybir.dt.float4_e2m1fn_x4
+COPY = mybir.ActivationFunctionType.Copy
 
 P = 128
 PACK = 4
 PER_COLUMN = 16
 BANK = 512
-FIRST = SLOTS_C
-WARM_UPS = (512, 512, 512, 128)
 WINDOW = 1024
-RANGES = [(0, 128), (128, 384), (384, 512), (512, 768)]
+HALF = T // 2
+ORDER = (2, 0, 1, 3)
+RANGES = [(0, 128), (128, 384), (384, 640), (640, 768)]
 
 
 def tile_moe_pool_none_kernel(
@@ -38,44 +38,51 @@ def tile_moe_pool_none_kernel(
         def bank(n):
             return psum.tile([P, BANK], F32, name="bank%d" % n)
 
+        def sbuf(name, shape, dtype):
+            return keep.tile(shape, dtype, name=name, align_bytes=64)
 
-        list_a = keep.tile([P, T // PER_COLUMN], U16, name="list_a")
-        list_c = keep.tile([P, T // PER_COLUMN], U16, name="list_c")
-        x_w = keep.tile([P, WINDOW], I32, name="x_w", align_bytes=64)
-        x_s = keep.tile([P, WINDOW], U8, name="x_s", align_bytes=64)
-        wb_w = keep.tile([P, EXPERTS_C, 2 * H], U8, name="wb_w", tag="expert_words", align_bytes=64)
-        wb_s = keep.tile([P, EXPERTS_C, H], U8, name="wb_s", tag="weight_scales", align_bytes=64)
-        ident = keep.tile([P, P], F32, name="ident")
+        lists = {pool: keep.tile([P, T // PER_COLUMN], U16, name="list_" + pool) for pool in "ca"}
+        x_w = sbuf("x_w", [P, WINDOW], I32)
+        x_s = sbuf("x_s", [P, WINDOW], U8)
+        raw_words = {pool: sbuf("raw_words_" + pool, [P, EXPERTS[pool], 2 * H], U8) for pool in "ca"}
+        raw_scales = {pool: sbuf("raw_scales_" + pool, [P, EXPERTS[pool], H], U8) for pool in "ca"}
+        w2_w = sbuf("w2_w", [P, 2 * N], U8)
+        w2_s = sbuf("w2_s", [P, N], U8)
 
-        nc.vector.memset(wb_s[:].bitcast(I32), 0)
-        make_identity(nc, ident[:])
+        for scale_tile in (raw_scales["c"], raw_scales["a"], w2_s):
+            nc.gpsimd.memset(scale_tile[:].bitcast(I32), 0)
 
-        def load_scales(queue, scale_tile, rows):
+        def load_scales(scale_tile, rows):
             for r in range(4):
-                queue.dma_start(out=scale_tile[r:P:32].bitcast(I32), in_=rows[r:16:4].bitcast(I32))
+                nc.sync.dma_start(out=scale_tile[r:P:32].bitcast(I32), in_=rows[r:16:4].bitcast(I32))
 
         def load_token_scales(queue, q):
             rows = x_scales[0, 4 * q : 4 * q + 4].bitcast(I32)
             queue.dma_start(out=x_s[32 * q : 32 * q + 32, :T].bitcast(I32), in_=rows.partition_broadcast(8))
 
-        nc.sync.dma_start(list_c[:], offs2)
+        def load_words(pool, words):
+            nc.sync.dma_start(
+                out=raw_words[pool][:].bitcast(I32), in_=words[:, 0].rearrange("e p b -> p e b").bitcast(I32)
+            )
+
+        nc.sync.dma_start(lists["c"][:], offs2)
         for q in range(4):
             load_token_scales(nc.sync if q < 2 else nc.scalar, q)
+        load_words("c", wb_words)
         nc.sync.dma_start(out=x_w[:, :T], in_=x_words[0].rearrange("p t d -> p (t d)").bitcast(I32))
-        nc.sync.dma_start(out=wb_w[:].bitcast(I32), in_=wb_words[:, 0].rearrange("e p b -> p e b").bitcast(I32))
-        nc.sync.dma_start(list_a[:], offs)
-        load_scales(nc.sync, wb_s, wb_scales[:, 0].rearrange("e g i -> g e i"))
+        load_scales(raw_scales["c"], wb_scales[:, 0].rearrange("e g i -> g e i"))
+        nc.sync.dma_start(lists["a"][:], offs)
+        load_words("a", wa_words)
+        load_scales(raw_scales["a"], wa_scales[:, 0].rearrange("e g i -> g e i"))
+        nc.sync.dma_start(out=w2_w[:].bitcast(I32), in_=w2_words[0].bitcast(I32))
+        load_scales(w2_s, w2_scales[0])
 
-        lists = {"a": list_a, "c": list_c}
-        weights = {"c": (wb_w, wb_s, SLOTS_C)}
-        slot_words, slot_scales, sums, in_slots, in_tokens = {}, {}, {}, {}, {}
-        for pool in "ca":
-            slot_words[pool] = keep.tile([P, T], U32, name="slot_words_" + pool, align_bytes=64)
-            slot_scales[pool] = keep.tile([P, T], U8, name="slot_scales_" + pool, align_bytes=64)
-            sums[pool] = keep.tile([P, T // P, PACK, P], F32, name="sums_" + pool, align_bytes=64)
+        slot_words = {pool: sbuf("slot_words_" + pool, [P, T], U32) for pool in "ca"}
+        slot_scales = {pool: sbuf("slot_scales_" + pool, [P, T], U8) for pool in "ca"}
+        part_words, part_scales, in_slots, in_tokens = {}, {}, {}, {}
         for pool in "ca":
             for t in range(PACK):
-                in_slots[pool, t] = keep.tile([P, T], F32, name="in_slots_%s%d" % (pool, t), align_bytes=64)
+                part_scales[pool, t] = sbuf("part_scales_%s%d" % (pool, t), [P, EXPERTS[pool], P], U8)
 
         def entries(pool, lo, hi):
             return lists[pool][:, lo // PER_COLUMN : hi // PER_COLUMN]
@@ -86,170 +93,141 @@ def tile_moe_pool_none_kernel(
         def gather_scales(pool, lo, hi):
             nc.vector.tensor_copy(slot_scales[pool][:, lo:hi], x_s[:].indirect(entries(pool, lo, hi)))
 
-        def expert_product(pool, b, n):
-            w_words, w_scales, slots_per_expert = weights[pool]
-            e = b * P // slots_per_expert
-            slots = slice(b * P, (b + 1) * P)
+        def pick_words(copy, pool, t, place):
+            part_words[pool, t] = sbuf(place, [P, EXPERTS[pool], 2 * P], U8)
+            columns = raw_words[pool][:].bitcast(U16).rearrange("p e (m t) -> p e m t", t=PACK)
+            copy(part_words[pool, t][:].bitcast(U16), columns[:, :, :, t])
+
+        def pick_scales(pool, t):
+            columns = raw_scales[pool][:].rearrange("p e (m t) -> p e m t", t=PACK)
+            nc.gpsimd.tensor_copy(part_scales[pool, t][:], columns[:, :, :, t])
+
+        def products(pool, t, lo, hi, n):
             acc = bank(n)
-            nc.tensor.matmul_mx(
-                out=acc[:],
-                lhsT=slot_words[pool][:, slots].bitcast(FP8X4),
-                lhsT_scale=slot_scales[pool][:, slots],
-                rhs=w_words[:, e, :].bitcast(FP4X4),
-                rhs_scale=w_scales[:, e, :],
-                start=True,
-                stop=True,
-            )
+            width = SLOTS[pool]
+            for e in range(lo // width, (hi - 1) // width + 1):
+                slots = slice(max(lo, e * width), min(hi, (e + 1) * width))
+                nc.tensor.matmul_mx(
+                    out=acc[:, slots.start - lo : slots.stop - lo],
+                    lhsT=part_words[pool, t][:, e, :].bitcast(FP4X4),
+                    lhsT_scale=part_scales[pool, t][:, e, :],
+                    rhs=slot_words[pool][:, slots].bitcast(FP8X4),
+                    rhs_scale=slot_scales[pool][:, slots],
+                    start=True,
+                    stop=True,
+                )
             return acc
 
-        def empty(pool, b, acc, t_lo, t_hi):
-            nc.scalar.copy(sums[pool][:, b, t_lo:t_hi], acc[:].rearrange("u (m t) -> u t m", t=PACK)[:, t_lo:t_hi])
+        def sums_a(copy, t, banks):
+            in_slots["a", t] = sbuf("in_slots_a%d" % t, [P, T], F32)
+            for (lo, hi), n in zip(((0, BANK), (BANK, T)), banks):
+                copy(in_slots["a", t][:, lo:hi], products("a", t, lo, hi, n)[:, : hi - lo])
 
-        def expert_sums(pool, b, n):
-            empty(pool, b, expert_product(pool, b, n), 0, PACK)
+        def sums_c(t, half, n, place=None):
+            in_slots["c", t, half] = sbuf(place or "in_slots_c%d_%d" % (t, half), [P, HALF], F32)
+            acc = products("c", t, half * HALF, (half + 1) * HALF, n)
+            nc.scalar.copy(in_slots["c", t, half][:], acc[:, :HALF])
 
-        def turn(pool, t, lo, hi, n):
-            turned = bank(n)
-            for b in range(lo // P, hi // P):
-                nc.tensor.transpose(turned[:, b * P - lo : (b + 1) * P - lo], sums[pool][:, b, t, :], ident[:])
-            nc.scalar.copy(in_slots[pool, t][:, lo:hi], turned[:, : hi - lo])
+        def scatter_a(t, place=None):
+            in_tokens["a", t] = sbuf(place or "in_tokens_a%d" % t, [P, WINDOW], F32)
+            nc.vector.tensor_copy(in_tokens["a", t][:].indirect(entries("a", 0, T)), in_slots["a", t][:])
 
-        def turn_whole(pool, t, n):
-            turn(pool, t, 0, BANK, n)
-            turn(pool, t, BANK, T, n + 1)
+        def scatter_c(t, half, place=None):
+            if half == 0:
+                in_tokens["c", t] = sbuf(place or "in_tokens_c%d" % t, [P, T], F32)
+            window = in_tokens["c", t][:].indirect(entries("c", half * HALF, (half + 1) * HALF))
+            nc.scalar.activation(window, in_slots["c", t, half][:], COPY)
 
-        def scatter(pool, t, lo, hi, values):
-            if lo == 0:
-                place = min(t, PACK - 2) if pool == "a" else t
-                in_tokens[pool, t] = keep.tile([P, WINDOW], F32, name="in_tokens_%s%d" % (pool, place))
-            nc.vector.tensor_copy(in_tokens[pool, t][:].indirect(entries(pool, lo, hi)), values)
+        h_pairs = [sbuf("h_pairs%d" % j, [P, 2, hi - lo, 2], BF16) for j, (lo, hi) in enumerate(RANGES)]
 
+        def multiply(engine, t):
+            for j, (lo, hi) in enumerate(RANGES):
+                engine.tensor_tensor(
+                    h_pairs[j][:, t // 2, :, t % 2],
+                    in_tokens["a", t][:, lo:hi],
+                    in_tokens["c", t][:, lo:hi],
+                    mybir.AluOpType.mult,
+                )
+
+        t0, t1, t2, t3 = ORDER
         gather_scales("c", 0, T)
-        gather_words("c", 0, FIRST)
-        gather_words("c", FIRST, T)
+        gather_words("c", 0, HALF)
+        gather_words("c", HALF, T)
         gather_words("a", 0, T)
         gather_scales("a", 0, T)
-        early = 2
-        blocks = range(T // P)
-        accs = []
-        for b in blocks:
-            accs.append(expert_product("c", b, b))
-            empty("c", b, accs[b], 0, early)
-            if (b + 1) * P == FIRST:
-                for t in range(early):
-                    turn("c", t, 0, FIRST, 6 + t)
-        for t in range(early):
-            turn("c", t, FIRST, T, 6 + t)
-        for b in blocks:
-            empty("c", b, accs[b], early, PACK)
-        wa_w = keep.tile([P, EXPERTS_A, 2 * H], U8, name="wa_w", tag="expert_words", align_bytes=64)
-        nc.sync.dma_start(out=wa_w[:].bitcast(I32), in_=wa_words[:, 0].rearrange("e p b -> p e b").bitcast(I32))
-        wa_s = keep.tile([P, EXPERTS_A, H], U8, name="wa_s", tag="weight_scales", align_bytes=64)
-        nc.gpsimd.memset(wa_s[:].bitcast(I32), 0)
-        load_scales(nc.sync, wa_s, wa_scales[:, 0].rearrange("e g i -> g e i"))
-        weights["a"] = (wa_w, wa_s, SLOTS_A)
-        turn_whole("c", 2, 6)
-        for b in range(T // P):
-            expert_sums("a", b, b % 3)
-        w2_w = keep.tile([P, 2 * N], U8, name="w2_w", tag="expert_words", align_bytes=64)
-        nc.sync.dma_start(out=w2_w[:].bitcast(I32), in_=w2_words[0].bitcast(I32))
-        for lo, hi in ((0, FIRST), (FIRST, T)):
-            for t in range(early):
-                scatter("c", t, lo, hi, in_slots["c", t][:, lo:hi])
+        for t in ORDER:
+            pick_words(nc.scalar.copy, "c", t, "part_words_c%d" % t)
+        for pool, t in [("c", t0), ("c", t1), ("a", t0), ("a", t1), ("c", t2), ("a", t2), ("c", t3), ("a", t3)]:
+            pick_scales(pool, t)
+        for t in ORDER[:-1]:
+            pick_words(nc.vector.tensor_copy, "a", t, "part_words_a%d" % t)
 
-        scatter("c", 2, 0, T, in_slots["c", 2][:])
-        later = [("a", 0), ("a", 1), ("a", 2), ("c", 3), ("a", 3)]
-        for (pool, t), n in zip(later, (3, 6, 3, 3, 6)):
-            turn_whole(pool, t, n)
+        sums_c(t0, 0, 0)
+        sums_c(t1, 0, 2)
+        scatter_c(t0, 0)
+        sums_c(t0, 1, 1)
+        scatter_c(t1, 0)
+        sums_a(nc.vector.tensor_copy, t0, (3, 4))
+        pick_words(nc.vector.tensor_copy, "a", t3, "part_words_a%d" % t0)
+        scatter_a(t0)
+        scatter_c(t0, 1)
+        multiply(nc.gpsimd, t0)
+        sums_c(t2, 0, 7)
+        sums_a(nc.scalar.copy, t1, (5, 6))
+        scatter_c(t2, 0, "part_words_a%d" % t1)
+        scatter_a(t1)
+        sums_c(t3, 0, 2)
+        acc = products("c", t1, HALF, T, 0)
+        sums_a(nc.scalar.copy, t2, (3, 4))
+        in_slots["c", t1, 1] = sbuf("part_words_a%d" % t2, [P, HALF], F32)
+        nc.scalar.copy(in_slots["c", t1, 1][:], acc[:, :HALF])
+        sums_c(t2, 1, 1)
+        scatter_c(t1, 1)
+        multiply(nc.gpsimd, t1)
+        scatter_a(t2)
+        sums_c(t3, 1, 5)
+        sums_a(nc.scalar.copy, t3, (3, 6))
+        scatter_c(t3, 0, "part_words_a%d" % t0)
+        scatter_c(t2, 1)
+        multiply(nc.gpsimd, t2)
+        scatter_a(t3, "in_tokens_a%d" % t0)
+        scatter_c(t3, 1)
 
-        h_pairs = [keep.tile([P, 2, hi - lo, 2], BF16, name="h_pairs%d" % j) for j, (lo, hi) in enumerate(RANGES)]
         h_words = {}
-
-        def multiply(engine, t, j, c_part):
-            lo, hi = RANGES[j]
-            engine.tensor_tensor(
-                h_pairs[j][:, t // 2, :, t % 2],
-                in_tokens["a", t][:, lo:hi],
-                c_part[:, lo:hi],
-                mybir.AluOpType.mult,
-            )
 
         def weave(j):
             lo, hi = RANGES[j]
-            h_words[j] = keep.tile([P, hi - lo, PACK], BF16, name="h_words%d" % j, align_bytes=64)
-            on_vector = j == len(RANGES) - 1
-            copy, word = (nc.vector.tensor_copy, I32) if on_vector else (nc.scalar.copy, U32)
-            copy(
-                h_words[j][:].rearrange("p c t -> p (c t)").bitcast(word).rearrange("p (c w) -> p c w", w=2),
-                h_pairs[j][:].rearrange("p w c e -> p w (c e)").bitcast(word).rearrange("p w c -> p c w"),
+            h_words[j] = sbuf("h_words%d" % j, [P, hi - lo, PACK], BF16)
+            nc.scalar.copy(
+                h_words[j][:].rearrange("p c t -> p (c t)").bitcast(U32).rearrange("p (c w) -> p c w", w=2),
+                h_pairs[j][:].rearrange("p w c e -> p w (c e)").bitcast(U32).rearrange("p w c -> p c w"),
             )
 
         def project(j):
             lo, hi = RANGES[j]
             width = hi - lo
-            h_codes = keep.tile([P, width], U32, name="h_codes%d" % j, align_bytes=64)
-            h_scales = keep.tile([P, width], U8, name="h_scales%d" % j, align_bytes=64)
+            h_codes = sbuf("h_codes%d" % j, [P, width], U32)
+            h_scales = sbuf("h_scales%d" % j, [P, width], U8)
             nc.vector.quantize_mx(
                 out=h_codes[:].bitcast(FP8X4), scales=h_scales[:], in_=h_words[j][:].rearrange("p c t -> p (c t)")
             )
-            for first, count, n, copy_out, queue in PIECES[j]:
-                acc = bank(n)
-                nc.tensor.matmul_mx(
-                    out=acc[:, :count],
-                    lhsT=w2_w[:].bitcast(FP4X4),
-                    lhsT_scale=w2_s[:],
-                    rhs=h_codes[:, first : first + count].bitcast(FP8X4),
-                    rhs_scale=h_scales[:, first : first + count],
-                    start=True,
-                    stop=True,
-                )
-                result = keep.tile([P, count], F32, name="result%d" % n)
-                copy_out(result[:], acc[:, :count])
-                queue.dma_start(out=out[:, lo + first : lo + first + count], in_=result[:])
-
-        PIECES = [
-            [(0, 128, 5, nc.scalar.copy, nc.sync)],
-            [(0, 128, 0, nc.vector.tensor_copy, nc.sync), (128, 128, 3, nc.vector.tensor_copy, nc.sync)],
-            [(0, 128, 2, nc.scalar.copy, nc.scalar)],
-            [(0, 256, 1, nc.scalar.copy, nc.sync)],
-        ]
-
-        last = PACK - 1
-        for pool, t in later:
-            scatter(pool, t, 0, T, in_slots[pool, t][:])
-            if pool == "a" and t < last:
-                for j in range(len(RANGES)):
-                    multiply(nc.gpsimd, t, j, in_tokens["c", t])
-            if (pool, t) == ("c", last):
-                there, back = bank(6), bank(7)
-                for b in range(BANK // P):
-                    cols = slice(b * P, (b + 1) * P)
-                    nc.tensor.transpose(there[:, cols], in_tokens[pool, t][:, cols], ident[:])
-                for half, place in enumerate(("between", "h_words%d" % (len(RANGES) - 1))):
-                    between = keep.tile([P, 2, P], F32, name=place, align_bytes=64)
-                    nc.scalar.copy(between[:], there[:].rearrange("u (b m) -> u b m", m=P)[:, 2 * half : 2 * half + 2])
-                    for b in range(2):
-                        cols = slice((2 * half + b) * P, (2 * half + b + 1) * P)
-                        nc.tensor.transpose(back[:, cols], between[:, b, :], ident[:])
-
-        w2_s = keep.tile([P, N], U8, name="in_slots_c%d" % last, align_bytes=64)
-        nc.gpsimd.memset(w2_s[:].bitcast(I32), 0)
-        load_scales(nc.sync, w2_s, w2_scales[0])
-        for n, count in enumerate(WARM_UPS):
+            acc = bank(j)
             nc.tensor.matmul_mx(
-                out=bank(4 + 2 * (n % 2))[:, :count],
+                out=acc[:, :width],
                 lhsT=w2_w[:].bitcast(FP4X4),
                 lhsT_scale=w2_s[:],
-                rhs=slot_words["a"][:, :count].bitcast(FP8X4),
-                rhs_scale=slot_scales["a"][:, :count],
+                rhs=h_codes[:].bitcast(FP8X4),
+                rhs_scale=h_scales[:],
                 start=True,
                 stop=True,
             )
+            result = sbuf("result%d" % j, [P, width], F32)
+            copy_out = nc.vector.tensor_copy if j < 2 else nc.scalar.copy
+            copy_out(result[:], acc[:, :width])
+            nc.sync.dma_start(out=out[:, lo:hi], in_=result[:])
 
-        multiply(nc.gpsimd, last, 3, in_tokens["c", last])
-        for j in range(3):
-            multiply(nc.vector, last, j, back)
-        for j in range(4):
+        multiply(nc.vector, t3)
+        for j in range(len(RANGES)):
             weave(j)
-        for j in (0, 3, 1, 2):
+        for j in range(len(RANGES)):
             project(j)

@@ -23,7 +23,7 @@ PER_COLUMN = 16
 BANK = 512
 WINDOW = 1024
 HALF = T // 2
-ORDER = (2, 0, 1, 3)
+ORDER = (0, 2, 1, 3)
 RANGES = [(0, 128), (128, 384), (384, 640), (640, 768)]
 
 
@@ -118,25 +118,29 @@ def tile_moe_pool_none_kernel(
                 )
             return acc
 
-        def sums_a(copy, t, banks):
-            in_slots["a", t] = sbuf("in_slots_a%d" % t, [P, T], F32)
-            for (lo, hi), n in zip(((0, BANK), (BANK, T)), banks):
-                copy(in_slots["a", t][:, lo:hi], products("a", t, lo, hi, n)[:, : hi - lo])
+        def half_slots(half):
+            return half * HALF, (half + 1) * HALF
 
-        def sums_c(t, half, n, place=None):
-            in_slots["c", t, half] = sbuf(place or "in_slots_c%d_%d" % (t, half), [P, HALF], F32)
-            acc = products("c", t, half * HALF, (half + 1) * HALF, n)
-            nc.scalar.copy(in_slots["c", t, half][:], acc[:, :HALF])
+        def sums_for_scalar(copy, pool, t, half, n, place=None):
+            acc = products(pool, t, *half_slots(half), n)
+            in_slots[pool, t, half] = sbuf(place or "in_slots_%s%d_%d" % (pool, t, half), [P, HALF], F32)
+            copy(in_slots[pool, t, half][:], acc[:, :HALF])
 
-        def scatter_a(t, place=None):
-            in_tokens["a", t] = sbuf(place or "in_tokens_a%d" % t, [P, WINDOW], F32)
-            nc.vector.tensor_copy(in_tokens["a", t][:].indirect(entries("a", 0, T)), in_slots["a", t][:])
-
-        def scatter_c(t, half, place=None):
+        def sums_for_vector(copy, pool, t, half, n):
             if half == 0:
-                in_tokens["c", t] = sbuf(place or "in_tokens_c%d" % t, [P, T], F32)
-            window = in_tokens["c", t][:].indirect(entries("c", half * HALF, (half + 1) * HALF))
-            nc.scalar.activation(window, in_slots["c", t, half][:], COPY)
+                in_slots[pool, t] = sbuf("in_slots_%s%d" % (pool, t), [P, T], F32)
+            lo, hi = half_slots(half)
+            copy(in_slots[pool, t][:, lo:hi], products(pool, t, lo, hi, n)[:, :HALF])
+
+        def scatter_on_vector(pool, t, place=None):
+            in_tokens[pool, t] = sbuf(place or "in_tokens_%s%d" % (pool, t), [P, WINDOW], F32)
+            nc.vector.tensor_copy(in_tokens[pool, t][:].indirect(entries(pool, 0, T)), in_slots[pool, t][:])
+
+        def scatter_on_scalar(pool, t, half, place=None):
+            if half == 0:
+                in_tokens[pool, t] = sbuf(place or "in_tokens_%s%d" % (pool, t), [P, T], F32)
+            window = in_tokens[pool, t][:].indirect(entries(pool, *half_slots(half)))
+            nc.scalar.activation(window, in_slots[pool, t, half][:], COPY)
 
         h_pairs = [sbuf("h_pairs%d" % j, [P, 2, hi - lo, 2], BF16) for j, (lo, hi) in enumerate(RANGES)]
 
@@ -149,49 +153,59 @@ def tile_moe_pool_none_kernel(
                     mybir.AluOpType.mult,
                 )
 
+        on_scalar, on_vector = nc.scalar.copy, nc.vector.tensor_copy
         t0, t1, t2, t3 = ORDER
         gather_scales("c", 0, T)
         gather_words("c", 0, HALF)
         gather_words("c", HALF, T)
         gather_words("a", 0, T)
-        gather_scales("a", 0, T)
         for t in ORDER:
-            pick_words(nc.scalar.copy, "c", t, "part_words_c%d" % t)
-        for pool, t in [("c", t0), ("c", t1), ("a", t0), ("a", t1), ("c", t2), ("a", t2), ("c", t3), ("a", t3)]:
-            pick_scales(pool, t)
+            pick_words(on_scalar, "c", t, "part_words_c%d" % t)
         for t in ORDER[:-1]:
-            pick_words(nc.vector.tensor_copy, "a", t, "part_words_a%d" % t)
+            pick_scales("c", t)
+        for t in ORDER:
+            pick_words(nc.gpsimd.tensor_copy, "a", t, "part_words_a%d" % t)
+            pick_scales("a", t)
+            if t == t1:
+                pick_scales("c", t3)
 
-        sums_c(t0, 0, 0)
-        sums_c(t1, 0, 2)
-        scatter_c(t0, 0)
-        sums_c(t0, 1, 1)
-        scatter_c(t1, 0)
-        sums_a(nc.vector.tensor_copy, t0, (3, 4))
-        pick_words(nc.vector.tensor_copy, "a", t3, "part_words_a%d" % t0)
-        scatter_a(t0)
-        scatter_c(t0, 1)
-        multiply(nc.gpsimd, t0)
-        sums_c(t2, 0, 7)
-        sums_a(nc.scalar.copy, t1, (5, 6))
-        scatter_c(t2, 0, "part_words_a%d" % t1)
-        scatter_a(t1)
-        sums_c(t3, 0, 2)
-        acc = products("c", t1, HALF, T, 0)
-        sums_a(nc.scalar.copy, t2, (3, 4))
-        in_slots["c", t1, 1] = sbuf("part_words_a%d" % t2, [P, HALF], F32)
-        nc.scalar.copy(in_slots["c", t1, 1][:], acc[:, :HALF])
-        sums_c(t2, 1, 1)
-        scatter_c(t1, 1)
+        sums_for_scalar(on_scalar, "c", t0, 0, 0)
+        sums_for_vector(on_scalar, "c", t1, 0, 1)
+        sums_for_scalar(on_scalar, "c", t0, 1, 2)
+        sums_for_vector(on_vector, "c", t1, 1, 3)
+        gather_scales("a", 0, T)
+        scatter_on_scalar("c", t0, 0)
+        sums_for_scalar(on_scalar, "c", t2, 0, 4)
+        scatter_on_scalar("c", t0, 1)
+        scatter_on_vector("c", t1)
+        sums_for_scalar(on_vector, "c", t3, 0, 1)
+        sums_for_scalar(on_vector, "c", t3, 1, 2)
+        sums_for_scalar(on_scalar, "a", t0, 0, 5)
+        sums_for_vector(on_scalar, "a", t1, 0, 6)
+        sums_for_vector(on_scalar, "a", t1, 1, 7)
+        scatter_on_scalar("a", t0, 0, "part_scales_a%d" % t1)
+        scatter_on_scalar("c", t2, 0, "part_words_a%d" % t1)
+        scatter_on_vector("a", t1)
         multiply(nc.gpsimd, t1)
-        scatter_a(t2)
-        sums_c(t3, 1, 5)
-        sums_a(nc.scalar.copy, t3, (3, 6))
-        scatter_c(t3, 0, "part_words_a%d" % t0)
-        scatter_c(t2, 1)
+        held = products("a", t0, *half_slots(1), 0)
+        first_half = products("a", t2, *half_slots(0), 3)
+        second_half = products("a", t2, *half_slots(1), 4)
+        in_slots["a", t0, 1] = sbuf("part_words_a%d" % t2, [P, HALF], F32)
+        on_scalar(in_slots["a", t0, 1][:], held[:, :HALF])
+        in_slots["a", t2] = sbuf("in_slots_a%d" % t2, [P, T], F32)
+        on_scalar(in_slots["a", t2][:, :HALF], first_half[:, :HALF])
+        on_scalar(in_slots["a", t2][:, HALF:], second_half[:, :HALF])
+        scatter_on_scalar("a", t0, 1)
+        multiply(nc.gpsimd, t0)
+        scatter_on_vector("a", t2)
+        sums_for_vector(on_scalar, "a", t3, 0, 5)
+        sums_for_vector(on_scalar, "a", t3, 1, 7)
+        sums_for_scalar(on_vector, "c", t2, 1, 6, "part_scales_a%d" % t3)
+        scatter_on_scalar("c", t3, 0, "part_words_a%d" % t3)
+        scatter_on_scalar("c", t2, 1)
         multiply(nc.gpsimd, t2)
-        scatter_a(t3, "in_tokens_a%d" % t0)
-        scatter_c(t3, 1)
+        scatter_on_vector("a", t3, "in_tokens_a%d" % t1)
+        scatter_on_scalar("c", t3, 1)
 
         h_words = {}
 

@@ -24,7 +24,7 @@ BANK = 512
 WINDOW = 1024
 HALF = T // 2
 ORDER = (0, 2, 1, 3)
-RANGES = [(0, 128), (128, 384), (384, 640), (640, 768)]
+RANGES = [(0, 128), (128, 384), (384, 512), (512, 768)]
 
 
 def tile_moe_pool_none_kernel(
@@ -46,7 +46,6 @@ def tile_moe_pool_none_kernel(
         x_s = sbuf("x_s", [P, WINDOW], U8)
         raw_words = {pool: sbuf("raw_words_" + pool, [P, EXPERTS[pool], 2 * H], U8) for pool in "ca"}
         raw_scales = {pool: sbuf("raw_scales_" + pool, [P, EXPERTS[pool], H], U8) for pool in "ca"}
-        w2_w = sbuf("w2_w", [P, 2 * N], U8)
         w2_s = sbuf("w2_s", [P, N], U8)
 
         for scale_tile in (raw_scales["c"], raw_scales["a"], w2_s):
@@ -74,7 +73,6 @@ def tile_moe_pool_none_kernel(
         nc.sync.dma_start(lists["a"][:], offs)
         load_words("a", wa_words)
         load_scales(raw_scales["a"], wa_scales[:, 0].rearrange("e g i -> g e i"))
-        nc.sync.dma_start(out=w2_w[:].bitcast(I32), in_=w2_words[0].bitcast(I32))
         load_scales(w2_s, w2_scales[0])
 
         slot_words = {pool: sbuf("slot_words_" + pool, [P, T], U32) for pool in "ca"}
@@ -170,7 +168,7 @@ def tile_moe_pool_none_kernel(
                 pick_scales("c", t3)
 
         sums_for_scalar(on_scalar, "c", t0, 0, 0)
-        sums_for_vector(on_scalar, "c", t1, 0, 1)
+        sums_for_vector(on_vector, "c", t1, 0, 1)
         sums_for_scalar(on_scalar, "c", t0, 1, 2)
         sums_for_vector(on_vector, "c", t1, 1, 3)
         gather_scales("a", 0, T)
@@ -203,21 +201,23 @@ def tile_moe_pool_none_kernel(
         sums_for_scalar(on_vector, "c", t2, 1, 6, "part_scales_a%d" % t3)
         scatter_on_scalar("c", t3, 0, "part_words_a%d" % t3)
         scatter_on_scalar("c", t2, 1)
+        w2_w = sbuf("part_scales_a%d" % t3, [P, 2 * N], U8)
+        nc.sync.dma_start(out=w2_w[:].bitcast(I32), in_=w2_words[0].bitcast(I32))
         multiply(nc.gpsimd, t2)
         scatter_on_vector("a", t3, "in_tokens_a%d" % t1)
         scatter_on_scalar("c", t3, 1)
 
         h_words = {}
 
-        def weave(j):
+        def weave(j, copy, word):
             lo, hi = RANGES[j]
             h_words[j] = sbuf("h_words%d" % j, [P, hi - lo, PACK], BF16)
-            nc.scalar.copy(
-                h_words[j][:].rearrange("p c t -> p (c t)").bitcast(U32).rearrange("p (c w) -> p c w", w=2),
-                h_pairs[j][:].rearrange("p w c e -> p w (c e)").bitcast(U32).rearrange("p w c -> p c w"),
+            copy(
+                h_words[j][:].rearrange("p c t -> p (c t)").bitcast(word).rearrange("p (c w) -> p c w", w=2),
+                h_pairs[j][:].rearrange("p w c e -> p w (c e)").bitcast(word).rearrange("p w c -> p c w"),
             )
 
-        def project(j):
+        def project(j, pieces, copy_out, queue):
             lo, hi = RANGES[j]
             width = hi - lo
             h_codes = sbuf("h_codes%d" % j, [P, width], U32)
@@ -225,23 +225,28 @@ def tile_moe_pool_none_kernel(
             nc.vector.quantize_mx(
                 out=h_codes[:].bitcast(FP8X4), scales=h_scales[:], in_=h_words[j][:].rearrange("p c t -> p (c t)")
             )
-            acc = bank(j)
-            nc.tensor.matmul_mx(
-                out=acc[:, :width],
-                lhsT=w2_w[:].bitcast(FP4X4),
-                lhsT_scale=w2_s[:],
-                rhs=h_codes[:].bitcast(FP8X4),
-                rhs_scale=h_scales[:],
-                start=True,
-                stop=True,
-            )
-            result = sbuf("result%d" % j, [P, width], F32)
-            copy_out = nc.vector.tensor_copy if j < 2 else nc.scalar.copy
-            copy_out(result[:], acc[:, :width])
-            nc.sync.dma_start(out=out[:, lo:hi], in_=result[:])
+            count = width // pieces
+            for first in range(0, width, count):
+                n = (lo + first) // P
+                acc = bank(n)
+                nc.tensor.matmul_mx(
+                    out=acc[:, :count],
+                    lhsT=w2_w[:].bitcast(FP4X4),
+                    lhsT_scale=w2_s[:],
+                    rhs=h_codes[:, first : first + count].bitcast(FP8X4),
+                    rhs_scale=h_scales[:, first : first + count],
+                    start=True,
+                    stop=True,
+                )
+                result = sbuf("result%d" % n, [P, count], F32)
+                copy_out(result[:], acc[:, :count])
+                queue.dma_start(out=out[:, lo + first : lo + first + count], in_=result[:])
 
         multiply(nc.vector, t3)
-        for j in range(len(RANGES)):
-            weave(j)
-        for j in range(len(RANGES)):
-            project(j)
+        for j in range(3):
+            weave(j, on_scalar, U32)
+        weave(3, on_vector, I32)
+        project(0, 1, on_scalar, nc.sync)
+        project(1, 1, on_scalar, nc.sync)
+        project(3, 2, on_vector, nc.sync)
+        project(2, 1, on_scalar, nc.scalar)

@@ -23,6 +23,7 @@ PER_COLUMN = 16
 BANK = 512
 WINDOW = 1024
 HALF = T // 2
+WARM_UPS = (512, 512, 512, 128)
 ORDER = (0, 2, 1, 3)
 RANGES = [(0, 128), (128, 384), (384, 512), (512, 768)]
 
@@ -203,6 +204,16 @@ def tile_moe_pool_none_kernel(
         scatter_on_scalar("c", t2, 1)
         w2_w = sbuf("part_scales_a%d" % t3, [P, 2 * N], U8)
         nc.sync.dma_start(out=w2_w[:].bitcast(I32), in_=w2_words[0].bitcast(I32))
+        for n, count in enumerate(WARM_UPS):
+            nc.tensor.matmul_mx(
+                out=bank(6 + n % 2)[:, :count],
+                lhsT=w2_w[:].bitcast(FP4X4),
+                lhsT_scale=w2_s[:],
+                rhs=slot_words["a"][:, :count].bitcast(FP8X4),
+                rhs_scale=slot_scales["a"][:, :count],
+                start=True,
+                stop=True,
+            )
         multiply(nc.gpsimd, t2)
         scatter_on_vector("a", t3, "in_tokens_a%d" % t1)
         scatter_on_scalar("c", t3, 1)

@@ -169,7 +169,7 @@ def tile_moe_pool_none_kernel(
                 pick_scales("c", t3)
 
         sums_for_scalar(on_scalar, "c", t0, 0, 0)
-        sums_for_vector(on_vector, "c", t1, 0, 1)
+        sums_for_vector(on_scalar, "c", t1, 0, 1)
         sums_for_scalar(on_scalar, "c", t0, 1, 2)
         sums_for_vector(on_vector, "c", t1, 1, 3)
         gather_scales("a", 0, T)

@@ -22,7 +22,7 @@ PACK = 4
 PER_COLUMN = 16
 BANK = 512
 WINDOW = 1024
-HALF = T // 2
+HALVES = ((0, T // 2), (T // 2, T))
 WARM_UPS = (512, 512, 512, 128)
 ORDER = (0, 2, 1, 3)
 RANGES = [(0, 128), (128, 384), (384, 512), (512, 768)]
@@ -76,7 +76,7 @@ def tile_moe_pool_none_kernel(
         load_scales(raw_scales["a"], wa_scales[:, 0].rearrange("e g i -> g e i"))
         load_scales(w2_s, w2_scales[0])
 
-        slot_words = {pool: sbuf("slot_words_" + pool, [P, T], U32) for pool in "ca"}
+        slot_words = {}
         slot_scales = {pool: sbuf("slot_scales_" + pool, [P, T], U8) for pool in "ca"}
         part_words, part_scales, in_slots, in_tokens = {}, {}, {}, {}
         for pool in "ca":
@@ -87,7 +87,10 @@ def tile_moe_pool_none_kernel(
             return lists[pool][:, lo // PER_COLUMN : hi // PER_COLUMN]
 
         def gather_words(pool, lo, hi):
-            nc.vector.tensor_copy(slot_words[pool][:, lo:hi], x_w[:].bitcast(U32).indirect(entries(pool, lo, hi)))
+            gathered = sbuf("slot_words_%s%d" % (pool, lo), [P, hi - lo], U32)
+            nc.vector.tensor_copy(gathered[:], x_w[:].bitcast(U32).indirect(entries(pool, lo, hi)))
+            for first in range(lo, hi, P):
+                slot_words[pool, first] = gathered[:, first - lo :]
 
         def gather_scales(pool, lo, hi):
             nc.vector.tensor_copy(slot_scales[pool][:, lo:hi], x_s[:].indirect(entries(pool, lo, hi)))
@@ -97,9 +100,9 @@ def tile_moe_pool_none_kernel(
             columns = raw_words[pool][:].bitcast(U16).rearrange("p e (m t) -> p e m t", t=PACK)
             copy(part_words[pool, t][:].bitcast(U16), columns[:, :, :, t])
 
-        def pick_scales(pool, t):
+        def pick_scales(pool, t, experts=slice(None)):
             columns = raw_scales[pool][:].rearrange("p e (m t) -> p e m t", t=PACK)
-            nc.gpsimd.tensor_copy(part_scales[pool, t][:], columns[:, :, :, t])
+            nc.gpsimd.tensor_copy(part_scales[pool, t][:, experts], columns[:, experts, :, t])
 
         def products(pool, t, lo, hi, n):
             acc = bank(n)
@@ -110,36 +113,34 @@ def tile_moe_pool_none_kernel(
                     out=acc[:, slots.start - lo : slots.stop - lo],
                     lhsT=part_words[pool, t][:, e, :].bitcast(FP4X4),
                     lhsT_scale=part_scales[pool, t][:, e, :],
-                    rhs=slot_words[pool][:, slots].bitcast(FP8X4),
+                    rhs=slot_words[pool, slots.start][:, : slots.stop - slots.start].bitcast(FP8X4),
                     rhs_scale=slot_scales[pool][:, slots],
                     start=True,
                     stop=True,
                 )
-            return acc
+            return acc[:, : hi - lo]
 
-        def half_slots(half):
-            return half * HALF, (half + 1) * HALF
+        def empty_piece(copy, sums, pool, t, lo, hi, place=None):
+            in_slots[pool, t, lo] = sbuf(place or "in_slots_%s%d_%d" % (pool, t, lo), [P, hi - lo], F32)
+            copy(in_slots[pool, t, lo][:], sums)
 
-        def sums_for_scalar(copy, pool, t, half, n, place=None):
-            acc = products(pool, t, *half_slots(half), n)
-            in_slots[pool, t, half] = sbuf(place or "in_slots_%s%d_%d" % (pool, t, half), [P, HALF], F32)
-            copy(in_slots[pool, t, half][:], acc[:, :HALF])
+        def empty_whole(copy, halves, pool, t):
+            in_slots[pool, t] = sbuf("in_slots_%s%d" % (pool, t), [P, T], F32)
+            for (lo, hi), sums in zip(HALVES, halves):
+                copy(in_slots[pool, t][:, lo:hi], sums)
 
-        def sums_for_vector(copy, pool, t, half, n):
-            if half == 0:
-                in_slots[pool, t] = sbuf("in_slots_%s%d" % (pool, t), [P, T], F32)
-            lo, hi = half_slots(half)
-            copy(in_slots[pool, t][:, lo:hi], products(pool, t, lo, hi, n)[:, :HALF])
+        def both_halves(pool, t, banks):
+            return [products(pool, t, lo, hi, n) for (lo, hi), n in zip(HALVES, banks)]
 
-        def scatter_on_vector(pool, t, place=None):
+        def scatter_whole(pool, t, place=None):
             in_tokens[pool, t] = sbuf(place or "in_tokens_%s%d" % (pool, t), [P, WINDOW], F32)
             nc.vector.tensor_copy(in_tokens[pool, t][:].indirect(entries(pool, 0, T)), in_slots[pool, t][:])
 
-        def scatter_on_scalar(pool, t, half, place=None):
-            if half == 0:
+        def scatter_piece(pool, t, lo, hi, place=None):
+            if lo == 0:
                 in_tokens[pool, t] = sbuf(place or "in_tokens_%s%d" % (pool, t), [P, T], F32)
-            window = in_tokens[pool, t][:].indirect(entries(pool, *half_slots(half)))
-            nc.scalar.activation(window, in_slots[pool, t, half][:], COPY)
+            window = in_tokens[pool, t][:].indirect(entries(pool, lo, hi))
+            nc.scalar.activation(window, in_slots[pool, t, lo][:], COPY)
 
         h_pairs = [sbuf("h_pairs%d" % j, [P, 2, hi - lo, 2], BF16) for j, (lo, hi) in enumerate(RANGES)]
 
@@ -154,54 +155,72 @@ def tile_moe_pool_none_kernel(
 
         on_scalar, on_vector = nc.scalar.copy, nc.vector.tensor_copy
         t0, t1, t2, t3 = ORDER
+        e0, e1, e2 = [(e * SLOTS["c"], (e + 1) * SLOTS["c"]) for e in range(EXPERTS["c"])]
+        first, second = HALVES
         gather_scales("c", 0, T)
-        gather_words("c", 0, HALF)
-        gather_words("c", HALF, T)
+        gather_words("c", *e0)
+        gather_words("c", e0[1], T)
         gather_words("a", 0, T)
-        for t in ORDER:
-            pick_words(on_scalar, "c", t, "part_words_c%d" % t)
-        for t in ORDER[:-1]:
-            pick_scales("c", t)
-        for t in ORDER:
-            pick_words(nc.gpsimd.tensor_copy, "a", t, "part_words_a%d" % t)
-            pick_scales("a", t)
-            if t == t1:
-                pick_scales("c", t3)
-
-        sums_for_scalar(on_scalar, "c", t0, 0, 0)
-        sums_for_vector(on_scalar, "c", t1, 0, 1)
-        sums_for_scalar(on_scalar, "c", t0, 1, 2)
-        sums_for_vector(on_vector, "c", t1, 1, 3)
         gather_scales("a", 0, T)
-        scatter_on_scalar("c", t0, 0)
-        sums_for_scalar(on_scalar, "c", t2, 0, 4)
-        scatter_on_scalar("c", t0, 1)
-        scatter_on_vector("c", t1)
-        sums_for_scalar(on_vector, "c", t3, 0, 1)
-        sums_for_scalar(on_vector, "c", t3, 1, 2)
-        sums_for_scalar(on_scalar, "a", t0, 0, 5)
-        sums_for_vector(on_scalar, "a", t1, 0, 6)
-        sums_for_vector(on_scalar, "a", t1, 1, 7)
-        scatter_on_scalar("a", t0, 0, "part_scales_a%d" % t1)
-        scatter_on_scalar("c", t2, 0, "part_words_a%d" % t1)
-        scatter_on_vector("a", t1)
+        for t in (t0, t2, t1, t3):
+            pick_words(on_scalar, "c", t, "part_words_c%d" % t)
+        for experts in (slice(0, 1), slice(1, None)):
+            for t in (t0, t2):
+                pick_scales("c", t, experts)
+        for t in (t1, t3):
+            pick_scales("c", t)
+        words_place = {
+            t1: "part_words_a%d" % t1,
+            t0: "part_words_a%d" % t0,
+            t2: "part_words_c%d" % t3,
+            t3: "part_scales_c%d" % t3,
+        }
+
+        def pick_a(t):
+            pick_words(nc.gpsimd.tensor_copy, "a", t, words_place[t])
+            pick_scales("a", t)
+
+        pick_a(t1)
+        pick_a(t0)
+        width = SLOTS["c"]
+        empty_piece(on_scalar, products("c", t0, *e0, 0), "c", t0, *e0)
+        empty_piece(on_scalar, products("c", t2, *e0, 1), "c", t2, *e0)
+        scatter_piece("c", t0, *e0)
+        rest = {t: products("c", t, e1[0], T, n) for t, n in ((t0, 0), (t2, 7))}
+        empty_piece(on_scalar, rest[t0][:, :width], "c", t0, *e1)
+        empty_piece(on_vector, rest[t2][:, :width], "c", t2, *e1)
+        scatter_piece("c", t2, *e0)
+        scatter_piece("c", t0, *e1)
+        scatter_piece("c", t2, *e1)
+        empty_whole(on_vector, both_halves("c", t1, (3, 4)), "c", t1)
+        halves = both_halves("c", t3, (5, 6))
+        empty_piece(on_vector, halves[0], "c", t3, *first)
+        empty_piece(on_scalar, halves[1], "c", t3, *second)
+        scatter_whole("c", t1)
+        pick_a(t2)
+        pick_a(t3)
+
+        halves = both_halves("a", t1, (2, 1))
+        empty_piece(on_scalar, rest[t0][:, width:], "c", t0, *e2, words_place[t1])
+        empty_piece(on_scalar, rest[t2][:, width:], "c", t2, *e2, "part_scales_a%d" % t1)
+        empty_whole(on_scalar, halves, "a", t1)
+        scatter_piece("c", t0, *e2)
+        scatter_piece("c", t2, *e2)
+        scatter_whole("a", t1)
         multiply(nc.gpsimd, t1)
-        held = products("a", t0, *half_slots(1), 0)
-        first_half = products("a", t2, *half_slots(0), 3)
-        second_half = products("a", t2, *half_slots(1), 4)
-        in_slots["a", t0, 1] = sbuf("part_words_a%d" % t2, [P, HALF], F32)
-        on_scalar(in_slots["a", t0, 1][:], held[:, :HALF])
-        in_slots["a", t2] = sbuf("in_slots_a%d" % t2, [P, T], F32)
-        on_scalar(in_slots["a", t2][:, :HALF], first_half[:, :HALF])
-        on_scalar(in_slots["a", t2][:, HALF:], second_half[:, :HALF])
-        scatter_on_scalar("a", t0, 1)
-        multiply(nc.gpsimd, t0)
-        scatter_on_vector("a", t2)
-        sums_for_vector(on_scalar, "a", t3, 0, 5)
-        sums_for_vector(on_scalar, "a", t3, 1, 7)
-        sums_for_scalar(on_vector, "c", t2, 1, 6, "part_scales_a%d" % t3)
-        scatter_on_scalar("c", t3, 0, "part_words_a%d" % t3)
-        scatter_on_scalar("c", t2, 1)
+
+        halves_t0 = both_halves("a", t0, (3, 4))
+        empty_piece(on_scalar, halves_t0[0], "a", t0, *first)
+        empty_whole(on_scalar, both_halves("a", t2, (5, 6)), "a", t2)
+        scatter_piece("a", t0, *first, words_place[t2])
+        scatter_whole("a", t2)
+        multiply(nc.gpsimd, t2)
+
+        halves = both_halves("a", t3, (0, 1))
+        empty_piece(on_scalar, halves_t0[1], "a", t0, *second, "part_scales_a%d" % t3)
+        empty_whole(on_scalar, halves, "a", t3)
+        scatter_piece("c", t3, *first, words_place[t3])
+        scatter_piece("a", t0, *second)
         w2_w = sbuf("part_scales_a%d" % t3, [P, 2 * N], U8)
         nc.sync.dma_start(out=w2_w[:].bitcast(I32), in_=w2_words[0].bitcast(I32))
         for n, count in enumerate(WARM_UPS):
@@ -209,14 +228,14 @@ def tile_moe_pool_none_kernel(
                 out=bank(6 + n % 2)[:, :count],
                 lhsT=w2_w[:].bitcast(FP4X4),
                 lhsT_scale=w2_s[:],
-                rhs=slot_words["a"][:, :count].bitcast(FP8X4),
+                rhs=slot_words["a", 0][:, :count].bitcast(FP8X4),
                 rhs_scale=slot_scales["a"][:, :count],
                 start=True,
                 stop=True,
             )
-        multiply(nc.gpsimd, t2)
-        scatter_on_vector("a", t3, "in_tokens_a%d" % t1)
-        scatter_on_scalar("c", t3, 1)
+        multiply(nc.gpsimd, t0)
+        scatter_whole("a", t3, "in_tokens_a%d" % t1)
+        scatter_piece("c", t3, *second)
 
         h_words = {}
 

@@ -25,7 +25,7 @@ WINDOW = 1024
 HALVES = ((0, T // 2), (T // 2, T))
 WARM_UPS = (512, 512, 512, 128)
 ORDER = (0, 2, 1, 3)
-RANGES = [(0, 128), (128, 384), (384, 512), (512, 768)]
+RANGES = [(0, 128), (128, 384), (384, 640), (640, 768)]
 
 
 def tile_moe_pool_none_kernel(
@@ -200,27 +200,28 @@ def tile_moe_pool_none_kernel(
         pick_a(t2)
         pick_a(t3)
 
-        halves = both_halves("a", t1, (2, 1))
-        empty_piece(on_scalar, rest[t0][:, width:], "c", t0, *e2, words_place[t1])
-        empty_piece(on_scalar, rest[t2][:, width:], "c", t2, *e2, "part_scales_a%d" % t1)
-        empty_whole(on_scalar, halves, "a", t1)
-        scatter_piece("c", t0, *e2)
-        scatter_piece("c", t2, *e2)
+        empty_whole(on_scalar, both_halves("a", t1, (2, 1)), "a", t1)
         scatter_whole("a", t1)
         multiply(nc.gpsimd, t1)
 
         halves_t0 = both_halves("a", t0, (3, 4))
         empty_piece(on_scalar, halves_t0[0], "a", t0, *first)
-        empty_whole(on_scalar, both_halves("a", t2, (5, 6)), "a", t2)
-        scatter_piece("a", t0, *first, words_place[t2])
+        empty_piece(on_scalar, rest[t0][:, width:], "c", t0, *e2, words_place[t0])
+        scatter_piece("a", t0, *first)
+        scatter_piece("c", t0, *e2)
+
+        halves = both_halves("a", t2, (5, 6))
+        empty_piece(on_scalar, halves_t0[1], "a", t0, *second, words_place[t2])
+        empty_whole(on_scalar, halves, "a", t2)
+        scatter_piece("a", t0, *second)
+        multiply(nc.gpsimd, t0)
         scatter_whole("a", t2)
-        multiply(nc.gpsimd, t2)
 
         halves = both_halves("a", t3, (0, 1))
-        empty_piece(on_scalar, halves_t0[1], "a", t0, *second, "part_scales_a%d" % t3)
+        empty_piece(on_scalar, rest[t2][:, width:], "c", t2, *e2, "part_scales_a%d" % t3)
         empty_whole(on_scalar, halves, "a", t3)
         scatter_piece("c", t3, *first, words_place[t3])
-        scatter_piece("a", t0, *second)
+        scatter_piece("c", t2, *e2)
         w2_w = sbuf("part_scales_a%d" % t3, [P, 2 * N], U8)
         nc.sync.dma_start(out=w2_w[:].bitcast(I32), in_=w2_words[0].bitcast(I32))
         for n, count in enumerate(WARM_UPS):
@@ -233,7 +234,7 @@ def tile_moe_pool_none_kernel(
                 start=True,
                 stop=True,
             )
-        multiply(nc.gpsimd, t0)
+        multiply(nc.gpsimd, t2)
         scatter_whole("a", t3, "in_tokens_a%d" % t1)
         scatter_piece("c", t3, *second)
 
@@ -247,7 +248,7 @@ def tile_moe_pool_none_kernel(
                 h_pairs[j][:].rearrange("p w c e -> p w (c e)").bitcast(word).rearrange("p w c -> p c w"),
             )
 
-        def project(j, pieces, copy_out, queue):
+        def project(j, ways_out):
             lo, hi = RANGES[j]
             width = hi - lo
             h_codes = sbuf("h_codes%d" % j, [P, width], U32)
@@ -255,8 +256,8 @@ def tile_moe_pool_none_kernel(
             nc.vector.quantize_mx(
                 out=h_codes[:].bitcast(FP8X4), scales=h_scales[:], in_=h_words[j][:].rearrange("p c t -> p (c t)")
             )
-            count = width // pieces
-            for first in range(0, width, count):
+            count = width // len(ways_out)
+            for first, (copy_out, queue) in zip(range(0, width, count), ways_out):
                 n = (lo + first) // P
                 acc = bank(n)
                 nc.tensor.matmul_mx(
@@ -276,7 +277,7 @@ def tile_moe_pool_none_kernel(
         for j in range(3):
             weave(j, on_scalar, U32)
         weave(3, on_vector, I32)
-        project(0, 1, on_scalar, nc.sync)
-        project(1, 1, on_scalar, nc.sync)
-        project(3, 2, on_vector, nc.sync)
-        project(2, 1, on_scalar, nc.scalar)
+        project(0, [(on_scalar, nc.sync)])
+        project(1, [(on_scalar, nc.sync)])
+        project(3, [(on_vector, nc.sync)])
+        project(2, [(on_vector, nc.sync), (on_scalar, nc.scalar)])

@@ -47,9 +47,9 @@ def tile_moe_pool_none_kernel(
         x_s = sbuf("x_s", [P, WINDOW], U8)
         raw_words = {pool: sbuf("raw_words_" + pool, [P, EXPERTS[pool], 2 * H], U8) for pool in "ca"}
         raw_scales = {pool: sbuf("raw_scales_" + pool, [P, EXPERTS[pool], H], U8) for pool in "ca"}
-        w2_s = sbuf("w2_s", [P, N], U8)
+        w2_w = sbuf("w2_w", [P, 2 * N], U8)
 
-        for scale_tile in (raw_scales["c"], raw_scales["a"], w2_s):
+        for scale_tile in (raw_scales["c"], raw_scales["a"]):
             nc.gpsimd.memset(scale_tile[:].bitcast(I32), 0)
 
         def load_scales(scale_tile, rows):
@@ -74,7 +74,7 @@ def tile_moe_pool_none_kernel(
         nc.sync.dma_start(lists["a"][:], offs)
         load_words("a", wa_words)
         load_scales(raw_scales["a"], wa_scales[:, 0].rearrange("e g i -> g e i"))
-        load_scales(w2_s, w2_scales[0])
+        nc.sync.dma_start(out=w2_w[:].bitcast(I32), in_=w2_words[0].bitcast(I32))
 
         slot_words = {}
         slot_scales = {pool: sbuf("slot_scales_" + pool, [P, T], U8) for pool in "ca"}
@@ -222,8 +222,9 @@ def tile_moe_pool_none_kernel(
         empty_whole(on_scalar, halves, "a", t3)
         scatter_piece("c", t3, *first, words_place[t3])
         scatter_piece("c", t2, *e2)
-        w2_w = sbuf("part_scales_a%d" % t3, [P, 2 * N], U8)
-        nc.sync.dma_start(out=w2_w[:].bitcast(I32), in_=w2_words[0].bitcast(I32))
+        w2_s = sbuf("in_slots_c%d_0" % t3, [P, N], U8)
+        nc.gpsimd.memset(w2_s[:].bitcast(I32), 0)
+        load_scales(w2_s, w2_scales[0])
         for n, count in enumerate(WARM_UPS):
             nc.tensor.matmul_mx(
                 out=bank(6 + n % 2)[:, :count],

@@ -182,20 +182,20 @@ def tile_moe_pool_none_kernel(
 
         pick_a(t1)
         pick_a(t0)
-        width = SLOTS["c"]
         empty_piece(on_scalar, products("c", t0, *e0, 0), "c", t0, *e0)
         empty_piece(on_scalar, products("c", t2, *e0, 1), "c", t2, *e0)
         scatter_piece("c", t0, *e0)
         rest = {t: products("c", t, e1[0], T, n) for t, n in ((t0, 0), (t2, 7))}
-        empty_piece(on_scalar, rest[t0][:, :width], "c", t0, *e1)
-        empty_piece(on_vector, rest[t2][:, :width], "c", t2, *e1)
+        short = (e1[0], second[0])
+        empty_piece(on_scalar, rest[t0][:, :P], "c", t0, *short)
+        middle, last = (e1[0], T - P), (T - P, T)
+        empty_piece(on_vector, rest[t2][:, : BANK - P], "c", t2, *middle)
         scatter_piece("c", t2, *e0)
-        scatter_piece("c", t0, *e1)
-        scatter_piece("c", t2, *e1)
+        scatter_piece("c", t0, *short)
+        scatter_piece("c", t2, *middle)
         empty_whole(on_vector, both_halves("c", t1, (3, 4)), "c", t1)
-        halves = both_halves("c", t3, (5, 6))
-        empty_piece(on_vector, halves[0], "c", t3, *first)
-        empty_piece(on_scalar, halves[1], "c", t3, *second)
+        halves_c3 = both_halves("c", t3, (5, 6))
+        empty_piece(on_vector, halves_c3[0], "c", t3, *first)
         scatter_whole("c", t1)
         pick_a(t2)
         pick_a(t3)
@@ -206,22 +206,23 @@ def tile_moe_pool_none_kernel(
 
         halves_t0 = both_halves("a", t0, (3, 4))
         empty_piece(on_scalar, halves_t0[0], "a", t0, *first)
-        empty_piece(on_scalar, rest[t0][:, width:], "c", t0, *e2, words_place[t0])
+        empty_piece(on_scalar, halves_c3[1], "c", t3, *second, words_place[t0])
         scatter_piece("a", t0, *first)
-        scatter_piece("c", t0, *e2)
 
-        halves = both_halves("a", t2, (5, 6))
+        halves = both_halves("a", t2, (5, 2))
+        empty_piece(on_scalar, rest[t0][:, P:], "c", t0, *second, "part_scales_a%d" % t2)
         empty_piece(on_scalar, halves_t0[1], "a", t0, *second, words_place[t2])
         empty_whole(on_scalar, halves, "a", t2)
+        scatter_piece("c", t0, *second)
         scatter_piece("a", t0, *second)
         multiply(nc.gpsimd, t0)
         scatter_whole("a", t2)
 
-        halves = both_halves("a", t3, (0, 1))
-        empty_piece(on_scalar, rest[t2][:, width:], "c", t2, *e2, "part_scales_a%d" % t3)
+        halves = both_halves("a", t3, (3, 1))
+        empty_piece(on_scalar, rest[t2][:, BANK - P :], "c", t2, *last, "part_scales_a%d" % t3)
         empty_whole(on_scalar, halves, "a", t3)
         scatter_piece("c", t3, *first, words_place[t3])
-        scatter_piece("c", t2, *e2)
+        scatter_piece("c", t2, *last)
         w2_s = sbuf("in_slots_c%d_0" % t3, [P, N], U8)
         nc.gpsimd.memset(w2_s[:].bitcast(I32), 0)
         load_scales(w2_s, w2_scales[0])

@@ -25,7 +25,7 @@ WINDOW = 1024
 HALVES = ((0, T // 2), (T // 2, T))
 WARM_UPS = (512, 512, 512, 128)
 ORDER = (0, 2, 1, 3)
-RANGES = [(0, 128), (128, 384), (384, 640), (640, 768)]
+RANGES = [(0, 256), (256, 512), (512, 768)]
 
 
 def tile_moe_pool_none_kernel(
@@ -240,17 +240,15 @@ def tile_moe_pool_none_kernel(
         scatter_whole("a", t3, "in_tokens_a%d" % t1)
         scatter_piece("c", t3, *second)
 
-        h_words = {}
+        h_words = [sbuf("h_words%d" % j, [P, hi - lo, PACK], BF16) for j, (lo, hi) in enumerate(RANGES)]
 
-        def weave(j, copy, word):
-            lo, hi = RANGES[j]
-            h_words[j] = sbuf("h_words%d" % j, [P, hi - lo, PACK], BF16)
+        def weave(j, copy, word, tokens=slice(None)):
             copy(
-                h_words[j][:].rearrange("p c t -> p (c t)").bitcast(word).rearrange("p (c w) -> p c w", w=2),
-                h_pairs[j][:].rearrange("p w c e -> p w (c e)").bitcast(word).rearrange("p w c -> p c w"),
+                h_words[j][:, tokens].rearrange("p c t -> p (c t)").bitcast(word).rearrange("p (c w) -> p c w", w=2),
+                h_pairs[j][:, :, tokens].rearrange("p w c e -> p w (c e)").bitcast(word).rearrange("p w c -> p c w"),
             )
 
-        def project(j, ways_out):
+        def project(j, copy_out, queue):
             lo, hi = RANGES[j]
             width = hi - lo
             h_codes = sbuf("h_codes%d" % j, [P, width], U32)
@@ -258,28 +256,25 @@ def tile_moe_pool_none_kernel(
             nc.vector.quantize_mx(
                 out=h_codes[:].bitcast(FP8X4), scales=h_scales[:], in_=h_words[j][:].rearrange("p c t -> p (c t)")
             )
-            count = width // len(ways_out)
-            for first, (copy_out, queue) in zip(range(0, width, count), ways_out):
-                n = (lo + first) // P
-                acc = bank(n)
-                nc.tensor.matmul_mx(
-                    out=acc[:, :count],
-                    lhsT=w2_w[:].bitcast(FP4X4),
-                    lhsT_scale=w2_s[:],
-                    rhs=h_codes[:, first : first + count].bitcast(FP8X4),
-                    rhs_scale=h_scales[:, first : first + count],
-                    start=True,
-                    stop=True,
-                )
-                result = sbuf("result%d" % n, [P, count], F32)
-                copy_out(result[:], acc[:, :count])
-                queue.dma_start(out=out[:, lo + first : lo + first + count], in_=result[:])
+            acc = bank(j)
+            nc.tensor.matmul_mx(
+                out=acc[:, :width],
+                lhsT=w2_w[:].bitcast(FP4X4),
+                lhsT_scale=w2_s[:],
+                rhs=h_codes[:].bitcast(FP8X4),
+                rhs_scale=h_scales[:],
+                start=True,
+                stop=True,
+            )
+            result = sbuf("result%d" % j, [P, width], F32)
+            copy_out(result[:], acc[:, :width])
+            queue.dma_start(out=out[:, lo:hi], in_=result[:])
 
         multiply(nc.vector, t3)
-        for j in range(3):
-            weave(j, on_scalar, U32)
-        weave(3, on_vector, I32)
-        project(0, [(on_scalar, nc.sync)])
-        project(1, [(on_scalar, nc.sync)])
-        project(3, [(on_vector, nc.sync)])
-        project(2, [(on_vector, nc.sync), (on_scalar, nc.scalar)])
+        weave(0, on_scalar, U32)
+        weave(1, on_scalar, U32)
+        weave(2, on_scalar, U32, slice(0, P))
+        weave(2, on_vector, I32, slice(P, 2 * P))
+        project(0, on_scalar, nc.sync)
+        project(1, on_vector, nc.sync)
+        project(2, on_scalar, nc.scalar)

@@ -23,7 +23,6 @@ PER_COLUMN = 16
 BANK = 512
 WINDOW = 1024
 HALVES = ((0, T // 2), (T // 2, T))
-WARM_UPS = (512, 512, 512, 128)
 ORDER = (0, 2, 1, 3)
 RANGES = [(0, 256), (256, 512), (512, 768)]
 
@@ -226,16 +225,6 @@ def tile_moe_pool_none_kernel(
         w2_s = sbuf("in_slots_c%d_0" % t3, [P, N], U8)
         nc.gpsimd.memset(w2_s[:].bitcast(I32), 0)
         load_scales(w2_s, w2_scales[0])
-        for n, count in enumerate(WARM_UPS):
-            nc.tensor.matmul_mx(
-                out=bank(6 + n % 2)[:, :count],
-                lhsT=w2_w[:].bitcast(FP4X4),
-                lhsT_scale=w2_s[:],
-                rhs=slot_words["a", 0][:, :count].bitcast(FP8X4),
-                rhs_scale=slot_scales["a"][:, :count],
-                start=True,
-                stop=True,
-            )
         multiply(nc.gpsimd, t2)
         scatter_whole("a", t3, "in_tokens_a%d" % t1)
         scatter_piece("c", t3, *second)

@@ -38,8 +38,8 @@ def tile_moe_pool_none_kernel(
         def bank(n):
             return psum.tile([P, BANK], F32, name="bank%d" % n)
 
-        def sbuf(name, shape, dtype):
-            return keep.tile(shape, dtype, name=name, align_bytes=64)
+        def sbuf(place, shape, dtype):
+            return keep.tile(shape, dtype, name=place, align_bytes=64)
 
         lists = {pool: keep.tile([P, T // PER_COLUMN], U16, name="list_" + pool) for pool in "ca"}
         x_w = sbuf("x_w", [P, WINDOW], I32)
@@ -75,9 +75,8 @@ def tile_moe_pool_none_kernel(
         load_scales(raw_scales["a"], wa_scales[:, 0].rearrange("e g i -> g e i"))
         nc.sync.dma_start(out=w2_w[:].bitcast(I32), in_=w2_words[0].bitcast(I32))
 
-        slot_words = {}
         slot_scales = {pool: sbuf("slot_scales_" + pool, [P, T], U8) for pool in "ca"}
-        part_words, part_scales, in_slots, in_tokens = {}, {}, {}, {}
+        slot_words, part_words, part_scales, in_slots, in_tokens = {}, {}, {}, {}, {}
         for pool in "ca":
             for t in range(PACK):
                 part_scales[pool, t] = sbuf("part_scales_%s%d" % (pool, t), [P, EXPERTS[pool], P], U8)
@@ -88,11 +87,11 @@ def tile_moe_pool_none_kernel(
         def gather_words(pool, lo, hi):
             gathered = sbuf("slot_words_%s%d" % (pool, lo), [P, hi - lo], U32)
             nc.vector.tensor_copy(gathered[:], x_w[:].bitcast(U32).indirect(entries(pool, lo, hi)))
-            for first in range(lo, hi, P):
-                slot_words[pool, first] = gathered[:, first - lo :]
+            for slot in range(lo, hi, P):
+                slot_words[pool, slot] = gathered[:, slot - lo :]
 
-        def gather_scales(pool, lo, hi):
-            nc.vector.tensor_copy(slot_scales[pool][:, lo:hi], x_s[:].indirect(entries(pool, lo, hi)))
+        def gather_scales(pool):
+            nc.vector.tensor_copy(slot_scales[pool][:], x_s[:].indirect(entries(pool, 0, T)))
 
         def pick_words(copy, pool, t, place):
             part_words[pool, t] = sbuf(place, [P, EXPERTS[pool], 2 * P], U8)
@@ -119,17 +118,17 @@ def tile_moe_pool_none_kernel(
                 )
             return acc[:, : hi - lo]
 
+        def in_two_banks(pool, t, banks, cuts=HALVES):
+            return [products(pool, t, lo, hi, n) for (lo, hi), n in zip(cuts, banks)]
+
         def empty_piece(copy, sums, pool, t, lo, hi, place=None):
-            in_slots[pool, t, lo] = sbuf(place or "in_slots_%s%d_%d" % (pool, t, lo), [P, hi - lo], F32)
-            copy(in_slots[pool, t, lo][:], sums)
+            in_slots[pool, t, lo] = sbuf(place or "in_slots_%s%d_%d" % (pool, t, lo), [P, hi - lo], F32)[:]
+            copy(in_slots[pool, t, lo], sums)
 
-        def empty_whole(copy, halves, pool, t):
+        def empty_whole(copies, sums, pool, t, cuts=HALVES):
             in_slots[pool, t] = sbuf("in_slots_%s%d" % (pool, t), [P, T], F32)
-            for (lo, hi), sums in zip(HALVES, halves):
-                copy(in_slots[pool, t][:, lo:hi], sums)
-
-        def both_halves(pool, t, banks):
-            return [products(pool, t, lo, hi, n) for (lo, hi), n in zip(HALVES, banks)]
+            for copy, (lo, hi), some in zip(copies, cuts, sums):
+                copy(in_slots[pool, t][:, lo:hi], some)
 
         def scatter_whole(pool, t, place=None):
             in_tokens[pool, t] = sbuf(place or "in_tokens_%s%d" % (pool, t), [P, WINDOW], F32)
@@ -139,9 +138,10 @@ def tile_moe_pool_none_kernel(
             if lo == 0:
                 in_tokens[pool, t] = sbuf(place or "in_tokens_%s%d" % (pool, t), [P, T], F32)
             window = in_tokens[pool, t][:].indirect(entries(pool, lo, hi))
-            nc.scalar.activation(window, in_slots[pool, t, lo][:], COPY)
+            nc.scalar.activation(window, in_slots[pool, t, lo], COPY)
 
         h_pairs = [sbuf("h_pairs%d" % j, [P, 2, hi - lo, 2], BF16) for j, (lo, hi) in enumerate(RANGES)]
+        h_words = [sbuf("h_words%d" % j, [P, hi - lo, PACK], BF16) for j, (lo, hi) in enumerate(RANGES)]
 
         def multiply(engine, t):
             for j, (lo, hi) in enumerate(RANGES):
@@ -156,18 +156,22 @@ def tile_moe_pool_none_kernel(
         t0, t1, t2, t3 = ORDER
         e0, e1, e2 = [(e * SLOTS["c"], (e + 1) * SLOTS["c"]) for e in range(EXPERTS["c"])]
         first, second = HALVES
-        gather_scales("c", 0, T)
+        by_bank = ((0, BANK), (BANK, T))
+        width = SLOTS["c"]
+
+        gather_scales("c")
         gather_words("c", *e0)
         gather_words("c", e0[1], T)
         gather_words("a", 0, T)
-        gather_scales("a", 0, T)
+        gather_scales("a")
         for t in (t0, t2, t1, t3):
             pick_words(on_scalar, "c", t, "part_words_c%d" % t)
-        for experts in (slice(0, 1), slice(1, None)):
-            for t in (t0, t2):
-                pick_scales("c", t, experts)
-        for t in (t1, t3):
-            pick_scales("c", t)
+        pick_scales("c", t0, slice(0, 1))
+        pick_scales("c", t2, slice(0, 1))
+        pick_scales("c", t0, slice(1, None))
+        pick_scales("c", t1)
+        pick_scales("c", t2, slice(1, None))
+        pick_scales("c", t3)
         words_place = {
             t1: "part_words_a%d" % t1,
             t0: "part_words_a%d" % t0,
@@ -184,52 +188,49 @@ def tile_moe_pool_none_kernel(
         empty_piece(on_scalar, products("c", t0, *e0, 0), "c", t0, *e0)
         empty_piece(on_scalar, products("c", t2, *e0, 1), "c", t2, *e0)
         scatter_piece("c", t0, *e0)
-        rest = {t: products("c", t, e1[0], T, n) for t, n in ((t0, 0), (t2, 7))}
-        short = (e1[0], second[0])
-        empty_piece(on_scalar, rest[t0][:, :P], "c", t0, *short)
-        middle, last = (e1[0], T - P), (T - P, T)
-        empty_piece(on_vector, rest[t2][:, : BANK - P], "c", t2, *middle)
+        rest_t0 = products("c", t0, e1[0], T, 0)
+        empty_piece(on_scalar, rest_t0[:, :width], "c", t0, *e1)
+        empty_whole([on_vector, on_vector], in_two_banks("c", t1, (3, 4), by_bank), "c", t1, by_bank)
+        rest_t2 = products("c", t2, e1[0], T, 7)
+        empty_piece(on_vector, rest_t2[:, :width], "c", t2, *e1)
         scatter_piece("c", t2, *e0)
-        scatter_piece("c", t0, *short)
-        scatter_piece("c", t2, *middle)
-        empty_whole(on_vector, both_halves("c", t1, (3, 4)), "c", t1)
-        halves_c3 = both_halves("c", t3, (5, 6))
-        empty_piece(on_vector, halves_c3[0], "c", t3, *first)
+        scatter_piece("c", t0, *e1)
+        scatter_piece("c", t2, *e1)
+        empty_whole([on_vector, on_scalar], in_two_banks("c", t3, (5, 6), by_bank), "c", t3, by_bank)
+        for lo, hi in HALVES:
+            in_slots["c", t3, lo] = in_slots["c", t3][:, lo:hi]
         scatter_whole("c", t1)
         pick_a(t2)
         pick_a(t3)
 
-        empty_whole(on_scalar, both_halves("a", t1, (2, 1)), "a", t1)
+        empty_whole([on_scalar, on_scalar], in_two_banks("a", t1, (2, 1)), "a", t1)
         scatter_whole("a", t1)
         multiply(nc.gpsimd, t1)
 
-        halves_t0 = both_halves("a", t0, (3, 4))
+        halves_t0 = in_two_banks("a", t0, (3, 4))
         empty_piece(on_scalar, halves_t0[0], "a", t0, *first)
-        empty_piece(on_scalar, halves_c3[1], "c", t3, *second, words_place[t0])
+        empty_piece(on_scalar, rest_t0[:, width:], "c", t0, *e2, words_place[t0])
         scatter_piece("a", t0, *first)
+        scatter_piece("c", t0, *e2)
 
-        halves = both_halves("a", t2, (5, 2))
-        empty_piece(on_scalar, rest[t0][:, P:], "c", t0, *second, "part_scales_a%d" % t2)
+        halves = in_two_banks("a", t2, (5, 6))
         empty_piece(on_scalar, halves_t0[1], "a", t0, *second, words_place[t2])
-        empty_whole(on_scalar, halves, "a", t2)
-        scatter_piece("c", t0, *second)
+        empty_whole([on_scalar, on_scalar], halves, "a", t2)
         scatter_piece("a", t0, *second)
+        w2_s = sbuf(words_place[t2], [P, N], U8)
+        nc.gpsimd.memset(w2_s[:].bitcast(I32), 0)
+        load_scales(w2_s, w2_scales[0])
         multiply(nc.gpsimd, t0)
         scatter_whole("a", t2)
 
-        halves = both_halves("a", t3, (3, 1))
-        empty_piece(on_scalar, rest[t2][:, BANK - P :], "c", t2, *last, "part_scales_a%d" % t3)
-        empty_whole(on_scalar, halves, "a", t3)
+        halves = in_two_banks("a", t3, (0, 1))
+        empty_piece(on_scalar, rest_t2[:, width:], "c", t2, *e2, "part_scales_a%d" % t3)
+        empty_whole([on_scalar, on_scalar], halves, "a", t3)
         scatter_piece("c", t3, *first, words_place[t3])
-        scatter_piece("c", t2, *last)
-        w2_s = sbuf("in_slots_c%d_0" % t3, [P, N], U8)
-        nc.gpsimd.memset(w2_s[:].bitcast(I32), 0)
-        load_scales(w2_s, w2_scales[0])
+        scatter_piece("c", t2, *e2)
         multiply(nc.gpsimd, t2)
         scatter_whole("a", t3, "in_tokens_a%d" % t1)
         scatter_piece("c", t3, *second)
-
-        h_words = [sbuf("h_words%d" % j, [P, hi - lo, PACK], BF16) for j, (lo, hi) in enumerate(RANGES)]
 
         def weave(j, copy, word, tokens=slice(None)):
             copy(

@@ -67,12 +67,12 @@ def tile_moe_pool_none_kernel(
         nc.sync.dma_start(lists["c"][:], offs2)
         for q in range(4):
             load_token_scales(nc.sync if q < 2 else nc.scalar, q)
-        load_words("c", wb_words)
         nc.sync.dma_start(out=x_w[:, :T], in_=x_words[0].rearrange("p t d -> p (t d)").bitcast(I32))
+        load_words("c", wb_words)
         load_scales(raw_scales["c"], wb_scales[:, 0].rearrange("e g i -> g e i"))
         nc.sync.dma_start(lists["a"][:], offs)
-        load_words("a", wa_words)
         load_scales(raw_scales["a"], wa_scales[:, 0].rearrange("e g i -> g e i"))
+        load_words("a", wa_words)
         nc.sync.dma_start(out=w2_w[:].bitcast(I32), in_=w2_words[0].bitcast(I32))
 
         slot_scales = {pool: sbuf("slot_scales_" + pool, [P, T], U8) for pool in "ca"}
@@ -93,10 +93,13 @@ def tile_moe_pool_none_kernel(
         def gather_scales(pool):
             nc.vector.tensor_copy(slot_scales[pool][:], x_s[:].indirect(entries(pool, 0, T)))
 
-        def pick_words(copy, pool, t, place):
-            part_words[pool, t] = sbuf(place, [P, EXPERTS[pool], 2 * P], U8)
+        def pick_words(copy, pool, t, place, lo=0, hi=None):
+            hi = hi or EXPERTS[pool]
+            picked = sbuf(place, [P, hi - lo, 2 * P], U8)
             columns = raw_words[pool][:].bitcast(U16).rearrange("p e (m t) -> p e m t", t=PACK)
-            copy(part_words[pool, t][:].bitcast(U16), columns[:, :, :, t])
+            copy(picked[:].bitcast(U16), columns[:, lo:hi, :, t])
+            for e in range(lo, hi):
+                part_words[pool, t, e] = picked[:, e - lo, :]
 
         def pick_scales(pool, t, experts=slice(None)):
             columns = raw_scales[pool][:].rearrange("p e (m t) -> p e m t", t=PACK)
@@ -109,7 +112,7 @@ def tile_moe_pool_none_kernel(
                 slots = slice(max(lo, e * width), min(hi, (e + 1) * width))
                 nc.tensor.matmul_mx(
                     out=acc[:, slots.start - lo : slots.stop - lo],
-                    lhsT=part_words[pool, t][:, e, :].bitcast(FP4X4),
+                    lhsT=part_words[pool, t, e].bitcast(FP4X4),
                     lhsT_scale=part_scales[pool, t][:, e, :],
                     rhs=slot_words[pool, slots.start][:, : slots.stop - slots.start].bitcast(FP8X4),
                     rhs_scale=slot_scales[pool][:, slots],
@@ -164,18 +167,17 @@ def tile_moe_pool_none_kernel(
         gather_words("c", e0[1], T)
         gather_words("a", 0, T)
         gather_scales("a")
-        for t in (t0, t2, t1, t3):
-            pick_words(on_scalar, "c", t, "part_words_c%d" % t)
+        for t in (t0, t2):
+            pick_words(on_scalar, "c", t, "first_words_c%d" % t, 0, 1)
+        for t in (t0, t2):
+            pick_words(on_scalar, "c", t, "part_words_c%d" % t, 1)
         pick_scales("c", t0, slice(0, 1))
         pick_scales("c", t2, slice(0, 1))
         pick_scales("c", t0, slice(1, None))
-        pick_scales("c", t1)
-        pick_scales("c", t2, slice(1, None))
-        pick_scales("c", t3)
         words_place = {
             t1: "part_words_a%d" % t1,
             t0: "part_words_a%d" % t0,
-            t2: "part_words_c%d" % t3,
+            t2: "first_words_c%d" % t2,
             t3: "part_scales_c%d" % t3,
         }
 
@@ -183,10 +185,15 @@ def tile_moe_pool_none_kernel(
             pick_words(nc.gpsimd.tensor_copy, "a", t, words_place[t])
             pick_scales("a", t)
 
-        pick_a(t1)
-        pick_a(t0)
         empty_piece(on_scalar, products("c", t0, *e0, 0), "c", t0, *e0)
         empty_piece(on_scalar, products("c", t2, *e0, 1), "c", t2, *e0)
+        pick_scales("c", t1)
+        pick_words(nc.gpsimd.tensor_copy, "c", t1, "first_words_c%d" % t0)
+        pick_scales("c", t2, slice(1, None))
+        pick_scales("c", t3)
+        pick_words(nc.gpsimd.tensor_copy, "c", t3, "first_words_c%d" % t2)
+        pick_a(t1)
+        pick_a(t0)
         scatter_piece("c", t0, *e0)
         rest_t0 = products("c", t0, e1[0], T, 0)
         empty_piece(on_scalar, rest_t0[:, :width], "c", t0, *e1)

@@ -245,15 +245,21 @@ def tile_moe_pool_none_kernel(
                 h_pairs[j][:, :, tokens].rearrange("p w c e -> p w (c e)").bitcast(word).rearrange("p w c -> p c w"),
             )
 
-        def project(j, copy_out, queue):
-            lo, hi = RANGES[j]
-            width = hi - lo
-            h_codes = sbuf("h_codes%d" % j, [P, width], U32)
-            h_scales = sbuf("h_scales%d" % j, [P, width], U8)
+        result = sbuf("result", [P, T], F32)
+
+        def store(queue, lo, hi):
+            queue.dma_start(out=out[:, lo:hi], in_=result[:, lo:hi])
+
+        def project(j, n, copy_out, tokens=slice(0, 2 * P)):
+            lo, width = RANGES[j][0] + tokens.start, tokens.stop - tokens.start
+            h_codes = sbuf("h_codes%d" % n, [P, width], U32)
+            h_scales = sbuf("h_scales%d" % n, [P, width], U8)
             nc.vector.quantize_mx(
-                out=h_codes[:].bitcast(FP8X4), scales=h_scales[:], in_=h_words[j][:].rearrange("p c t -> p (c t)")
+                out=h_codes[:].bitcast(FP8X4),
+                scales=h_scales[:],
+                in_=h_words[j][:, tokens].rearrange("p c t -> p (c t)"),
             )
-            acc = bank(j)
+            acc = bank(n)
             nc.tensor.matmul_mx(
                 out=acc[:, :width],
                 lhsT=w2_w[:].bitcast(FP4X4),
@@ -263,15 +269,17 @@ def tile_moe_pool_none_kernel(
                 start=True,
                 stop=True,
             )
-            result = sbuf("result%d" % j, [P, width], F32)
-            copy_out(result[:], acc[:, :width])
-            queue.dma_start(out=out[:, lo:hi], in_=result[:])
+            copy_out(result[:, lo : lo + width], acc[:, :width])
 
         multiply(nc.vector, t3)
         weave(0, on_scalar, U32)
-        weave(1, on_scalar, U32)
+        weave(1, on_vector, I32)
         weave(2, on_scalar, U32, slice(0, P))
-        weave(2, on_vector, I32, slice(P, 2 * P))
-        project(0, on_scalar, nc.sync)
-        project(1, on_vector, nc.sync)
-        project(2, on_scalar, nc.scalar)
+        weave(2, on_scalar, U32, slice(P, 2 * P))
+        project(0, 0, on_scalar)
+        store(nc.sync, 0, 2 * P)
+        project(1, 1, on_scalar)
+        project(2, 2, on_scalar, slice(0, P))
+        store(nc.scalar, 2 * P, T - P)
+        project(2, 3, on_vector, slice(P, 2 * P))
+        store(nc.sync, T - P, T)

@@ -22,7 +22,6 @@ PACK = 4
 PER_COLUMN = 16
 BANK = 512
 WINDOW = 1024
-HALVES = ((0, T // 2), (T // 2, T))
 ORDER = (0, 2, 1, 3)
 RANGES = [(0, 256), (256, 512), (512, 768)]
 
@@ -44,12 +43,16 @@ def tile_moe_pool_none_kernel(
         lists = {pool: keep.tile([P, T // PER_COLUMN], U16, name="list_" + pool) for pool in "ca"}
         x_w = sbuf("x_w", [P, WINDOW], I32)
         x_s = sbuf("x_s", [P, WINDOW], U8)
-        raw_words = {pool: sbuf("raw_words_" + pool, [P, EXPERTS[pool], 2 * H], U8) for pool in "ca"}
+        raw_first = sbuf("raw_first", [P, 1, 2 * H], U8)
+        raw_rest = sbuf("raw_rest", [P, EXPERTS["c"] - 1, 2 * H], U8)
+        raw_a = sbuf("raw_a", [P, EXPERTS["a"], 2 * H], U8)
         raw_scales = {pool: sbuf("raw_scales_" + pool, [P, EXPERTS[pool], H], U8) for pool in "ca"}
         w2_w = sbuf("w2_w", [P, 2 * N], U8)
+        ones = sbuf("ones", [P, 1], F32)
 
         for scale_tile in (raw_scales["c"], raw_scales["a"]):
             nc.gpsimd.memset(scale_tile[:].bitcast(I32), 0)
+        nc.gpsimd.memset(ones[:], 1.0)
 
         def load_scales(scale_tile, rows):
             for r in range(4):
@@ -59,89 +62,56 @@ def tile_moe_pool_none_kernel(
             rows = x_scales[0, 4 * q : 4 * q + 4].bitcast(I32)
             queue.dma_start(out=x_s[32 * q : 32 * q + 32, :T].bitcast(I32), in_=rows.partition_broadcast(8))
 
-        def load_words(pool, words):
-            nc.sync.dma_start(
-                out=raw_words[pool][:].bitcast(I32), in_=words[:, 0].rearrange("e p b -> p e b").bitcast(I32)
-            )
+        def load_words(raw, words):
+            nc.sync.dma_start(out=raw[:].bitcast(I32), in_=words[:, 0].rearrange("e p b -> p e b").bitcast(I32))
 
         nc.sync.dma_start(lists["c"][:], offs2)
         for q in range(4):
             load_token_scales(nc.sync if q < 2 else nc.scalar, q)
         nc.sync.dma_start(out=x_w[:, :T], in_=x_words[0].rearrange("p t d -> p (t d)").bitcast(I32))
-        load_words("c", wb_words)
+        load_words(raw_first, wb_words[:1])
         load_scales(raw_scales["c"], wb_scales[:, 0].rearrange("e g i -> g e i"))
+        load_words(raw_rest, wb_words[1:])
         nc.sync.dma_start(lists["a"][:], offs)
         load_scales(raw_scales["a"], wa_scales[:, 0].rearrange("e g i -> g e i"))
-        load_words("a", wa_words)
-        nc.sync.dma_start(out=w2_w[:].bitcast(I32), in_=w2_words[0].bitcast(I32))
+        load_words(raw_a, wa_words)
+        nc.gpsimd.dma_start(out=w2_w[:].bitcast(I32), in_=w2_words[0].bitcast(I32))
 
-        slot_scales = {pool: sbuf("slot_scales_" + pool, [P, T], U8) for pool in "ca"}
-        slot_words, part_words, part_scales, in_slots, in_tokens = {}, {}, {}, {}, {}
-        for pool in "ca":
-            for t in range(PACK):
-                part_scales[pool, t] = sbuf("part_scales_%s%d" % (pool, t), [P, EXPERTS[pool], P], U8)
+        slot_words, slot_scales, part_words, part_scales, in_tokens = {}, {}, {}, {}, {}
 
         def entries(pool, lo, hi):
             return lists[pool][:, lo // PER_COLUMN : hi // PER_COLUMN]
 
-        def gather_words(pool, lo, hi):
-            gathered = sbuf("slot_words_%s%d" % (pool, lo), [P, hi - lo], U32)
-            nc.vector.tensor_copy(gathered[:], x_w[:].bitcast(U32).indirect(entries(pool, lo, hi)))
+        def gather(table, dtype, into, place, pool, lo, hi):
+            gathered = sbuf(place, [P, hi - lo], dtype)
+            nc.vector.tensor_copy(gathered[:], table[:].bitcast(dtype).indirect(entries(pool, lo, hi)))
             for slot in range(lo, hi, P):
-                slot_words[pool, slot] = gathered[:, slot - lo :]
+                into[pool, slot] = gathered[:, slot - lo :]
 
-        def gather_scales(pool):
-            nc.vector.tensor_copy(slot_scales[pool][:], x_s[:].indirect(entries(pool, 0, T)))
-
-        def pick_words(copy, pool, t, place, lo=0, hi=None):
-            hi = hi or EXPERTS[pool]
-            picked = sbuf(place, [P, hi - lo, 2 * P], U8)
-            columns = raw_words[pool][:].bitcast(U16).rearrange("p e (m t) -> p e m t", t=PACK)
-            copy(picked[:].bitcast(U16), columns[:, lo:hi, :, t])
-            for e in range(lo, hi):
-                part_words[pool, t, e] = picked[:, e - lo, :]
-
-        def pick_scales(pool, t, experts=slice(None)):
-            columns = raw_scales[pool][:].rearrange("p e (m t) -> p e m t", t=PACK)
-            nc.gpsimd.tensor_copy(part_scales[pool, t][:, experts], columns[:, experts, :, t])
+        def pick(copy, raw, dtype, into, place, pool, first, parts):
+            count, n = raw.shape[1], parts.stop - parts.start
+            size = 2 if dtype == U16 else 1
+            picked = sbuf(place, [P, count, n, size * P], U8)
+            columns = raw.bitcast(dtype).rearrange("p e (m t) -> p e t m", t=PACK)
+            copy(picked[:].bitcast(dtype), columns[:, :, parts, :])
+            for e in range(count):
+                for t in range(n):
+                    into[pool, parts.start + t, first + e] = picked[:, e, t, :]
 
         def products(pool, t, lo, hi, n):
             acc = bank(n)
             width = SLOTS[pool]
-            for e in range(lo // width, (hi - 1) // width + 1):
-                slots = slice(max(lo, e * width), min(hi, (e + 1) * width))
+            for e in range(lo // width, hi // width):
                 nc.tensor.matmul_mx(
-                    out=acc[:, slots.start - lo : slots.stop - lo],
+                    out=acc[:, e * width - lo : (e + 1) * width - lo],
                     lhsT=part_words[pool, t, e].bitcast(FP4X4),
-                    lhsT_scale=part_scales[pool, t][:, e, :],
-                    rhs=slot_words[pool, slots.start][:, : slots.stop - slots.start].bitcast(FP8X4),
-                    rhs_scale=slot_scales[pool][:, slots],
+                    lhsT_scale=part_scales[pool, t, e],
+                    rhs=slot_words[pool, e * width][:, :width].bitcast(FP8X4),
+                    rhs_scale=slot_scales[pool, e * width][:, :width],
                     start=True,
                     stop=True,
                 )
             return acc[:, : hi - lo]
-
-        def in_two_banks(pool, t, banks, cuts=HALVES):
-            return [products(pool, t, lo, hi, n) for (lo, hi), n in zip(cuts, banks)]
-
-        def empty_piece(copy, sums, pool, t, lo, hi, place=None):
-            in_slots[pool, t, lo] = sbuf(place or "in_slots_%s%d_%d" % (pool, t, lo), [P, hi - lo], F32)[:]
-            copy(in_slots[pool, t, lo], sums)
-
-        def empty_whole(copies, sums, pool, t, cuts=HALVES):
-            in_slots[pool, t] = sbuf("in_slots_%s%d" % (pool, t), [P, T], F32)
-            for copy, (lo, hi), some in zip(copies, cuts, sums):
-                copy(in_slots[pool, t][:, lo:hi], some)
-
-        def scatter_whole(pool, t, place=None):
-            in_tokens[pool, t] = sbuf(place or "in_tokens_%s%d" % (pool, t), [P, WINDOW], F32)
-            nc.vector.tensor_copy(in_tokens[pool, t][:].indirect(entries(pool, 0, T)), in_slots[pool, t][:])
-
-        def scatter_piece(pool, t, lo, hi, place=None):
-            if lo == 0:
-                in_tokens[pool, t] = sbuf(place or "in_tokens_%s%d" % (pool, t), [P, T], F32)
-            window = in_tokens[pool, t][:].indirect(entries(pool, lo, hi))
-            nc.scalar.activation(window, in_slots[pool, t, lo], COPY)
 
         h_pairs = [sbuf("h_pairs%d" % j, [P, 2, hi - lo, 2], BF16) for j, (lo, hi) in enumerate(RANGES)]
         h_words = [sbuf("h_words%d" % j, [P, hi - lo, PACK], BF16) for j, (lo, hi) in enumerate(RANGES)]
@@ -155,89 +125,94 @@ def tile_moe_pool_none_kernel(
                     mybir.AluOpType.mult,
                 )
 
-        on_scalar, on_vector = nc.scalar.copy, nc.vector.tensor_copy
+        def scatter_v(pool, t, values, place=None):
+            in_tokens[pool, t] = sbuf(place or "in_tokens_%s%d" % (pool, t), [P, WINDOW], F32)
+            nc.vector.tensor_copy(in_tokens[pool, t][:].indirect(entries(pool, 0, T)), values)
+
+        def scatter_s(pool, t, lo, hi, values, columns=None, place=None):
+            if columns:
+                in_tokens[pool, t] = sbuf(place or "in_tokens_%s%d" % (pool, t), [P, columns], F32)
+            nc.scalar.activation(in_tokens[pool, t][:].indirect(entries(pool, lo, hi)), values, COPY, scale=ones[:])
+
+        on_scalar, on_vector, on_gpsimd = nc.scalar.copy, nc.vector.tensor_copy, nc.gpsimd.tensor_copy
         t0, t1, t2, t3 = ORDER
-        e0, e1, e2 = [(e * SLOTS["c"], (e + 1) * SLOTS["c"]) for e in range(EXPERTS["c"])]
-        first, second = HALVES
-        by_bank = ((0, BANK), (BANK, T))
-        width = SLOTS["c"]
+        first = SLOTS["c"]
+        low, high = slice(0, 2), slice(2, 4)
 
-        gather_scales("c")
-        gather_words("c", *e0)
-        gather_words("c", e0[1], T)
-        gather_words("a", 0, T)
-        gather_scales("a")
+        def one(t):
+            return slice(t, t + 1)
+
+        def staged(name, width, place=None):
+            return sbuf(place or name, [P, width], F32)
+
+        gather(x_s, U8, slot_scales, "slot_scales_c0", "c", 0, first)
+        gather(x_w, U32, slot_words, "slot_words_c0", "c", 0, first)
+        pick(on_scalar, raw_first[:], U16, part_words, "words_first_low", "c", 0, low)
         for t in (t0, t2):
-            pick_words(on_scalar, "c", t, "first_words_c%d" % t, 0, 1)
+            pick(on_gpsimd, raw_scales["c"][:, :1], U8, part_scales, "scales_first%d" % t, "c", 0, one(t))
+        pick(on_scalar, raw_first[:], U16, part_words, "words_first_high", "c", 0, high)
+        gather(x_w, U32, slot_words, "slot_words_c1", "c", first, T)
+        gather(x_s, U8, slot_scales, "raw_first", "c", first, T)
+        pick(on_gpsimd, raw_rest[:], U16, part_words, "words_rest_low", "c", 1, low)
+        pick(on_gpsimd, raw_scales["c"][:, 1:], U8, part_scales, "scales_rest_low", "c", 1, low)
+        pick(on_gpsimd, raw_rest[:], U16, part_words, "words_rest_high", "c", 1, high)
+        pick(on_gpsimd, raw_scales["c"][:], U8, part_scales, "scales_high", "c", 0, high)
+        for t in (t1, t0, t2, t3):
+            pick(on_gpsimd, raw_a[:], U16, part_words, "words_a%d" % t, "a", 0, one(t))
+            pick(on_gpsimd, raw_scales["a"][:], U8, part_scales, "scales_a%d" % t, "a", 0, one(t))
+
+        heads = {}
+        for n, t in enumerate((t0, t2)):
+            heads[t] = staged("head_c%d" % t, first)
+            on_scalar(heads[t][:], products("c", t, 0, first, n))
+        gather(x_w, U32, slot_words, "words_first_low", "a", 0, T)
+        gather(x_s, U8, slot_scales, "scales_first%d" % t2, "a", 0, T)
         for t in (t0, t2):
-            pick_words(on_scalar, "c", t, "part_words_c%d" % t, 1)
-        pick_scales("c", t0, slice(0, 1))
-        pick_scales("c", t2, slice(0, 1))
-        pick_scales("c", t0, slice(1, None))
-        words_place = {
-            t1: "part_words_a%d" % t1,
-            t0: "part_words_a%d" % t0,
-            t2: "first_words_c%d" % t2,
-            t3: "part_scales_c%d" % t3,
-        }
+            scatter_s("c", t, 0, first, heads[t][:], WINDOW)
 
-        def pick_a(t):
-            pick_words(nc.gpsimd.tensor_copy, "a", t, words_place[t])
-            pick_scales("a", t)
+        def in_two(pool, t, banks):
+            return products(pool, t, 0, BANK, banks[0]), products(pool, t, BANK, T, banks[1])
 
-        empty_piece(on_scalar, products("c", t0, *e0, 0), "c", t0, *e0)
-        empty_piece(on_scalar, products("c", t2, *e0, 1), "c", t2, *e0)
-        pick_scales("c", t1)
-        pick_words(nc.gpsimd.tensor_copy, "c", t1, "first_words_c%d" % t0)
-        pick_scales("c", t2, slice(1, None))
-        pick_scales("c", t3)
-        pick_words(nc.gpsimd.tensor_copy, "c", t3, "first_words_c%d" % t2)
-        pick_a(t1)
-        pick_a(t0)
-        scatter_piece("c", t0, *e0)
-        rest_t0 = products("c", t0, e1[0], T, 0)
-        empty_piece(on_scalar, rest_t0[:, :width], "c", t0, *e1)
-        empty_whole([on_vector, on_vector], in_two_banks("c", t1, (3, 4), by_bank), "c", t1, by_bank)
-        rest_t2 = products("c", t2, e1[0], T, 7)
-        empty_piece(on_vector, rest_t2[:, :width], "c", t2, *e1)
-        scatter_piece("c", t2, *e0)
-        scatter_piece("c", t0, *e1)
-        scatter_piece("c", t2, *e1)
-        empty_whole([on_vector, on_scalar], in_two_banks("c", t3, (5, 6), by_bank), "c", t3, by_bank)
-        for lo, hi in HALVES:
-            in_slots["c", t3, lo] = in_slots["c", t3][:, lo:hi]
-        scatter_whole("c", t1)
-        pick_a(t2)
-        pick_a(t3)
+        sums_t0 = products("c", t0, first, T, 2)
+        sums_t2 = products("c", t2, first, T, 3)
+        sums_t1 = in_two("c", t1, (4, 5))
+        sums_t3 = in_two("c", t3, (6, 7))
+        rest_t0 = staged("rest_c%d" % t0, BANK)
+        on_scalar(rest_t0[:], sums_t0)
+        slots_c1, slots_c3 = staged("slots_c1", T), staged("slots_c3", T)
+        on_scalar(slots_c3[:, BANK:], sums_t3[1])
+        scatter_s("c", t0, first, T, rest_t0[:])
+        on_vector(slots_c1[:, :BANK], sums_t1[0])
+        on_vector(slots_c1[:, BANK:], sums_t1[1])
+        on_vector(slots_c3[:, :BANK], sums_t3[0])
+        scatter_v("c", t1, slots_c1[:])
 
-        empty_whole([on_scalar, on_scalar], in_two_banks("a", t1, (2, 1)), "a", t1)
-        scatter_whole("a", t1)
+        slots_a = {t: staged("slots_a%d" % t, T) for t in ORDER}
+
+        def empty_a(t, sums, which=(0, 1)):
+            for n in which:
+                on_scalar(slots_a[t][:, n * BANK : min(T, (n + 1) * BANK)], sums[n])
+
+        empty_a(t1, in_two("a", t1, (0, 1)))
+        scatter_v("a", t1, slots_a[t1][:])
         multiply(nc.gpsimd, t1)
-
-        halves_t0 = in_two_banks("a", t0, (3, 4))
-        empty_piece(on_scalar, halves_t0[0], "a", t0, *first)
-        empty_piece(on_scalar, rest_t0[:, width:], "c", t0, *e2, words_place[t0])
-        scatter_piece("a", t0, *first)
-        scatter_piece("c", t0, *e2)
-
-        halves = in_two_banks("a", t2, (5, 6))
-        empty_piece(on_scalar, halves_t0[1], "a", t0, *second, words_place[t2])
-        empty_whole([on_scalar, on_scalar], halves, "a", t2)
-        scatter_piece("a", t0, *second)
-        w2_s = sbuf(words_place[t2], [P, N], U8)
+        sums = in_two("a", t0, (2, 5))
+        empty_a(t0, sums, (0,))
+        rest_t2 = staged("rest_c%d" % t2, BANK, "words_a%d" % t0)
+        on_scalar(rest_t2[:], sums_t2)
+        empty_a(t0, sums, (1,))
+        scatter_s("c", t2, first, T, rest_t2[:])
+        empty_a(t2, in_two("a", t2, (4, 7)))
+        empty_a(t3, in_two("a", t3, (0, 1)))
+        scatter_s("a", t0, 0, T, slots_a[t0][:], 2 * T, "words_a%d" % t3)
+        w2_s = sbuf("scales_a%d" % t1, [P, N], U8)
         nc.gpsimd.memset(w2_s[:].bitcast(I32), 0)
         load_scales(w2_s, w2_scales[0])
-        multiply(nc.gpsimd, t0)
-        scatter_whole("a", t2)
-
-        halves = in_two_banks("a", t3, (0, 1))
-        empty_piece(on_scalar, rest_t2[:, width:], "c", t2, *e2, "part_scales_a%d" % t3)
-        empty_whole([on_scalar, on_scalar], halves, "a", t3)
-        scatter_piece("c", t3, *first, words_place[t3])
-        scatter_piece("c", t2, *e2)
+        scatter_v("a", t2, slots_a[t2][:])
         multiply(nc.gpsimd, t2)
-        scatter_whole("a", t3, "in_tokens_a%d" % t1)
-        scatter_piece("c", t3, *second)
+        multiply(nc.gpsimd, t0)
+        scatter_s("c", t3, 0, T, slots_c3[:], 2 * T, "scales_a%d" % t3)
+        scatter_v("a", t3, slots_a[t3][:], "in_tokens_a%d" % t1)
 
         def weave(j, copy, word, tokens=slice(None)):
             copy(

@@ -98,19 +98,23 @@ def tile_moe_pool_none_kernel(
                 for t in range(n):
                     into[pool, parts.start + t, first + e] = picked[:, e, t, :]
 
+        def one_pass(sums, pool, t, e):
+            width = SLOTS[pool]
+            nc.tensor.matmul_mx(
+                out=sums,
+                lhsT=part_words[pool, t, e].bitcast(FP4X4),
+                lhsT_scale=part_scales[pool, t, e],
+                rhs=slot_words[pool, e * width][:, :width].bitcast(FP8X4),
+                rhs_scale=slot_scales[pool, e * width][:, :width],
+                start=True,
+                stop=True,
+            )
+
         def products(pool, t, lo, hi, n):
             acc = bank(n)
             width = SLOTS[pool]
             for e in range(lo // width, hi // width):
-                nc.tensor.matmul_mx(
-                    out=acc[:, e * width - lo : (e + 1) * width - lo],
-                    lhsT=part_words[pool, t, e].bitcast(FP4X4),
-                    lhsT_scale=part_scales[pool, t, e],
-                    rhs=slot_words[pool, e * width][:, :width].bitcast(FP8X4),
-                    rhs_scale=slot_scales[pool, e * width][:, :width],
-                    start=True,
-                    stop=True,
-                )
+                one_pass(acc[:, e * width - lo : (e + 1) * width - lo], pool, t, e)
             return acc[:, : hi - lo]
 
         h_pairs = [sbuf("h_pairs%d" % j, [P, 2, hi - lo, 2], BF16) for j, (lo, hi) in enumerate(RANGES)]
@@ -157,7 +161,7 @@ def tile_moe_pool_none_kernel(
         pick(on_gpsimd, raw_scales["c"][:, 1:], U8, part_scales, "scales_rest_low", "c", 1, low)
         pick(on_gpsimd, raw_rest[:], U16, part_words, "words_rest_high", "c", 1, high)
         pick(on_gpsimd, raw_scales["c"][:], U8, part_scales, "scales_high", "c", 0, high)
-        for t in (t1, t0, t2, t3):
+        for t in (t1, t2, t0, t3):
             pick(on_gpsimd, raw_a[:], U16, part_words, "words_a%d" % t, "a", 0, one(t))
             pick(on_gpsimd, raw_scales["a"][:], U8, part_scales, "scales_a%d" % t, "a", 0, one(t))
 
@@ -170,49 +174,53 @@ def tile_moe_pool_none_kernel(
         for t in (t0, t2):
             scatter_s("c", t, 0, first, heads[t][:], WINDOW)
 
-        def in_two(pool, t, banks):
-            return products(pool, t, 0, BANK, banks[0]), products(pool, t, BANK, T, banks[1])
+        def in_three(pool, parts, banks):
+            sums = []
+            for n, bank_number in enumerate(banks):
+                acc = bank(bank_number)
+                width = SLOTS[pool]
+                for column in range(n * BANK, (n + 1) * BANK, width):
+                    one_pass(acc[:, column - n * BANK : column - n * BANK + width], pool, parts[column // T], column % T // width)
+                sums.append(acc[:])
+            return sums
+
+        def empty(copy, staging, sums, n):
+            copy(staging[:, n * BANK : (n + 1) * BANK], sums[n])
 
         sums_t0 = products("c", t0, first, T, 2)
         sums_t2 = products("c", t2, first, T, 3)
-        sums_t1 = in_two("c", t1, (4, 5))
-        sums_t3 = in_two("c", t3, (6, 7))
+        sums_c = in_three("c", (t1, t3), (4, 5, 6))
         rest_t0 = staged("rest_c%d" % t0, BANK)
         on_scalar(rest_t0[:], sums_t0)
-        slots_c1, slots_c3 = staged("slots_c1", T), staged("slots_c3", T)
-        on_scalar(slots_c3[:, BANK:], sums_t3[1])
+        slots_c = staged("slots_c", 2 * T)
+        empty(on_scalar, slots_c, sums_c, 2)
         scatter_s("c", t0, first, T, rest_t0[:])
-        on_vector(slots_c1[:, :BANK], sums_t1[0])
-        on_vector(slots_c1[:, BANK:], sums_t1[1])
-        on_vector(slots_c3[:, :BANK], sums_t3[0])
-        scatter_v("c", t1, slots_c1[:])
+        empty(on_vector, slots_c, sums_c, 0)
+        empty(on_vector, slots_c, sums_c, 1)
+        scatter_v("c", t1, slots_c[:, :T])
 
-        slots_a = {t: staged("slots_a%d" % t, T) for t in ORDER}
-
-        def empty_a(t, sums, which=(0, 1)):
-            for n in which:
-                on_scalar(slots_a[t][:, n * BANK : min(T, (n + 1) * BANK)], sums[n])
-
-        empty_a(t1, in_two("a", t1, (0, 1)))
-        scatter_v("a", t1, slots_a[t1][:])
-        multiply(nc.gpsimd, t1)
-        sums = in_two("a", t0, (2, 5))
-        empty_a(t0, sums, (0,))
-        rest_t2 = staged("rest_c%d" % t2, BANK, "words_a%d" % t0)
+        early, late = staged("slots_a_early", 2 * T), staged("slots_a_late", 2 * T)
+        sums = in_three("a", (t1, t2), (0, 1, 7))
+        empty(on_scalar, early, sums, 0)
+        empty(on_scalar, early, sums, 1)
+        rest_t2 = staged("rest_c%d" % t2, BANK, "words_a%d" % t2)
         on_scalar(rest_t2[:], sums_t2)
-        empty_a(t0, sums, (1,))
+        empty(on_scalar, early, sums, 2)
+        scatter_v("a", t1, early[:, :T])
+        multiply(nc.gpsimd, t1)
         scatter_s("c", t2, first, T, rest_t2[:])
-        empty_a(t2, in_two("a", t2, (4, 7)))
-        empty_a(t3, in_two("a", t3, (0, 1)))
-        scatter_s("a", t0, 0, T, slots_a[t0][:], 2 * T, "words_a%d" % t3)
+        sums = in_three("a", (t0, t3), (2, 4, 5))
+        for n in range(3):
+            empty(on_scalar, late, sums, n)
+        scatter_s("a", t0, 0, T, late[:, :T], 2 * T, "words_a%d" % t3)
         w2_s = sbuf("scales_a%d" % t1, [P, N], U8)
         nc.gpsimd.memset(w2_s[:].bitcast(I32), 0)
         load_scales(w2_s, w2_scales[0])
-        scatter_v("a", t2, slots_a[t2][:])
+        scatter_v("a", t2, early[:, T:])
         multiply(nc.gpsimd, t2)
         multiply(nc.gpsimd, t0)
-        scatter_s("c", t3, 0, T, slots_c3[:], 2 * T, "scales_a%d" % t3)
-        scatter_v("a", t3, slots_a[t3][:], "in_tokens_a%d" % t1)
+        scatter_s("c", t3, 0, T, slots_c[:, T:], 2 * T, "scales_a%d" % t3)
+        scatter_v("a", t3, late[:, T:], "in_tokens_a%d" % t1)
 
         def weave(j, copy, word, tokens=slice(None)):
             copy(

@@ -89,14 +89,15 @@ def tile_moe_pool_none_kernel(
                 into[pool, slot] = gathered[:, slot - lo :]
 
         def pick(copy, raw, dtype, into, place, pool, first, parts):
-            count, n = raw.shape[1], parts.stop - parts.start
+            chosen = range(PACK)[parts]
+            count, n = raw.shape[1], len(chosen)
             size = 2 if dtype == U16 else 1
             picked = sbuf(place, [P, count, n, size * P], U8)
             columns = raw.bitcast(dtype).rearrange("p e (m t) -> p e t m", t=PACK)
             copy(picked[:].bitcast(dtype), columns[:, :, parts, :])
             for e in range(count):
-                for t in range(n):
-                    into[pool, parts.start + t, first + e] = picked[:, e, t, :]
+                for row, t in enumerate(chosen):
+                    into[pool, t, first + e] = picked[:, e, row, :]
 
         def one_pass(sums, pool, t, e):
             width = SLOTS[pool]
@@ -161,9 +162,10 @@ def tile_moe_pool_none_kernel(
         pick(on_gpsimd, raw_scales["c"][:, 1:], U8, part_scales, "scales_rest_low", "c", 1, low)
         pick(on_gpsimd, raw_rest[:], U16, part_words, "words_rest_high", "c", 1, high)
         pick(on_gpsimd, raw_scales["c"][:], U8, part_scales, "scales_high", "c", 0, high)
-        for t in (t1, t2, t0, t3):
-            pick(on_gpsimd, raw_a[:], U16, part_words, "words_a%d" % t, "a", 0, one(t))
-            pick(on_gpsimd, raw_scales["a"][:], U8, part_scales, "scales_a%d" % t, "a", 0, one(t))
+        inner, outer = slice(1, 3), slice(0, 4, 3)
+        pick(on_gpsimd, raw_scales["a"][:], U8, part_scales, "scales_early", "a", 0, inner)
+        pick(on_gpsimd, raw_a[:], U16, part_words, "words_early", "a", 0, inner)
+        pick(on_gpsimd, raw_a[:], U16, part_words, "words_late", "a", 0, outer)
 
         heads = {}
         for n, t in enumerate((t0, t2)):
@@ -203,23 +205,24 @@ def tile_moe_pool_none_kernel(
         sums = in_three("a", (t1, t2), (0, 1, 7))
         empty(on_scalar, early, sums, 0)
         empty(on_scalar, early, sums, 1)
-        rest_t2 = staged("rest_c%d" % t2, BANK, "words_a%d" % t2)
+        rest_t2 = staged("rest_c%d" % t2, BANK, "scales_early")
         on_scalar(rest_t2[:], sums_t2)
         empty(on_scalar, early, sums, 2)
+        pick(on_gpsimd, raw_scales["a"][:], U8, part_scales, "words_early", "a", 0, outer)
         scatter_v("a", t1, early[:, :T])
         multiply(nc.gpsimd, t1)
         scatter_s("c", t2, first, T, rest_t2[:])
         sums = in_three("a", (t0, t3), (2, 4, 5))
         for n in range(3):
             empty(on_scalar, late, sums, n)
-        scatter_s("a", t0, 0, T, late[:, :T], 2 * T, "words_a%d" % t3)
-        w2_s = sbuf("scales_a%d" % t1, [P, N], U8)
+        scatter_s("a", t0, 0, T, late[:, :T], 2 * T, "words_late")
+        w2_s = sbuf("scales_early", [P, N], U8)
         nc.gpsimd.memset(w2_s[:].bitcast(I32), 0)
         load_scales(w2_s, w2_scales[0])
         scatter_v("a", t2, early[:, T:])
         multiply(nc.gpsimd, t2)
         multiply(nc.gpsimd, t0)
-        scatter_s("c", t3, 0, T, slots_c[:, T:], 2 * T, "scales_a%d" % t3)
+        scatter_s("c", t3, 0, T, slots_c[:, T:], 2 * T, "words_early")
         scatter_v("a", t3, late[:, T:], "in_tokens_a%d" % t1)
 
         def weave(j, copy, word, tokens=slice(None)):

@@ -189,20 +189,26 @@ def tile_moe_pool_none_kernel(
         def empty(copy, staging, sums, n):
             copy(staging[:, n * BANK : (n + 1) * BANK], sums[n])
 
-        sums_t0 = products("c", t0, first, T, 2)
+        slots_c = staged("slots_c", 8 * first)
+        in_row = [(t3, 0), (t3, 1), (t3, 2), (t0, 1), (t0, 2), (t1, 0), (t1, 1), (t1, 2)]
+
+        def pieces(n, lowest, order):
+            acc = bank(n)
+            for k in order:
+                one_pass(acc[:, (k - lowest) * first : (k - lowest + 1) * first], "c", *in_row[k])
+            return slots_c[:, lowest * first : (lowest + len(order)) * first], acc[:, : len(order) * first]
+
         sums_t2 = products("c", t2, first, T, 3)
-        sums_c = in_three("c", (t1, t3), (4, 5, 6))
-        rest_t0 = staged("rest_c%d" % t0, BANK)
-        on_scalar(rest_t0[:], sums_t0)
-        slots_c = staged("slots_c", 2 * T)
-        empty(on_scalar, slots_c, sums_c, 2)
-        scatter_s("c", t0, first, T, rest_t0[:])
-        empty(on_vector, slots_c, sums_c, 0)
-        empty(on_vector, slots_c, sums_c, 1)
-        scatter_v("c", t1, slots_c[:, :T])
+        on_scalar(*pieces(2, 4, (4, 5)))
+        on_scalar(*pieces(4, 2, (3, 2)))
+        scatter_s("c", t0, first, T, slots_c[:, 3 * first : 5 * first])
+        on_vector(*pieces(5, 6, (6, 7)))
+        on_vector(*pieces(6, 0, (0,)))
+        on_scalar(*pieces(7, 1, (1,)))
+        scatter_v("c", t1, slots_c[:, 5 * first :])
 
         early, late = staged("slots_a_early", 2 * T), staged("slots_a_late", 2 * T)
-        sums = in_three("a", (t1, t2), (0, 1, 7))
+        sums = in_three("a", (t1, t2), (0, 1, 2))
         empty(on_scalar, early, sums, 0)
         empty(on_scalar, early, sums, 1)
         rest_t2 = staged("rest_c%d" % t2, BANK, "scales_early")
@@ -212,7 +218,7 @@ def tile_moe_pool_none_kernel(
         scatter_v("a", t1, early[:, :T])
         multiply(nc.gpsimd, t1)
         scatter_s("c", t2, first, T, rest_t2[:])
-        sums = in_three("a", (t0, t3), (2, 4, 5))
+        sums = in_three("a", (t0, t3), (4, 5, 6))
         for n in range(3):
             empty(on_scalar, late, sums, n)
         scatter_s("a", t0, 0, T, late[:, :T], 2 * T, "words_late")
@@ -222,7 +228,7 @@ def tile_moe_pool_none_kernel(
         scatter_v("a", t2, early[:, T:])
         multiply(nc.gpsimd, t2)
         multiply(nc.gpsimd, t0)
-        scatter_s("c", t3, 0, T, slots_c[:, T:], 2 * T, "words_early")
+        scatter_s("c", t3, 0, T, slots_c[:, :T], 2 * T, "words_early")
         scatter_v("a", t3, late[:, T:], "in_tokens_a%d" % t1)
 
         def weave(j, copy, word, tokens=slice(None)):

@@ -200,11 +200,11 @@ def tile_moe_pool_none_kernel(
 
         sums_t2 = products("c", t2, first, T, 3)
         on_scalar(*pieces(2, 4, (4, 5)))
-        on_scalar(*pieces(4, 2, (3, 2)))
+        on_scalar(*pieces(4, 3, (3,)))
+        on_scalar(*pieces(7, 2, (2,)))
         scatter_s("c", t0, first, T, slots_c[:, 3 * first : 5 * first])
         on_vector(*pieces(5, 6, (6, 7)))
-        on_vector(*pieces(6, 0, (0,)))
-        on_scalar(*pieces(7, 1, (1,)))
+        on_vector(*pieces(6, 0, (0, 1)))
         scatter_v("c", t1, slots_c[:, 5 * first :])
 
         early, late = staged("slots_a_early", 2 * T), staged("slots_a_late", 2 * T)

@@ -150,14 +150,14 @@ def tile_moe_pool_none_kernel(
         def staged(name, width, place=None):
             return sbuf(place or name, [P, width], F32)
 
-        gather(x_s, U8, slot_scales, "slot_scales_c0", "c", 0, first)
+        gather(x_s, U8, slot_scales, "slot_scales_c0", "c", 0, BANK)
         gather(x_w, U32, slot_words, "slot_words_c0", "c", 0, first)
         pick(on_scalar, raw_first[:], U16, part_words, "words_first_low", "c", 0, low)
         for t in (t0, t2):
             pick(on_gpsimd, raw_scales["c"][:, :1], U8, part_scales, "scales_first%d" % t, "c", 0, one(t))
         pick(on_scalar, raw_first[:], U16, part_words, "words_first_high", "c", 0, high)
         gather(x_w, U32, slot_words, "slot_words_c1", "c", first, T)
-        gather(x_s, U8, slot_scales, "raw_first", "c", first, T)
+        gather(x_s, U8, slot_scales, "raw_first", "c", BANK, T)
         pick(on_gpsimd, raw_rest[:], U16, part_words, "words_rest_low", "c", 1, low)
         pick(on_gpsimd, raw_scales["c"][:, 1:], U8, part_scales, "scales_rest_low", "c", 1, low)
         pick(on_gpsimd, raw_rest[:], U16, part_words, "words_rest_high", "c", 1, high)
@@ -189,23 +189,20 @@ def tile_moe_pool_none_kernel(
         def empty(copy, staging, sums, n):
             copy(staging[:, n * BANK : (n + 1) * BANK], sums[n])
 
-        slots_c = staged("slots_c", 8 * first)
-        in_row = [(t3, 0), (t3, 1), (t3, 2), (t0, 1), (t0, 2), (t1, 0), (t1, 1), (t1, 2)]
-
-        def pieces(n, lowest, order):
-            acc = bank(n)
-            for k in order:
-                one_pass(acc[:, (k - lowest) * first : (k - lowest + 1) * first], "c", *in_row[k])
-            return slots_c[:, lowest * first : (lowest + len(order)) * first], acc[:, : len(order) * first]
-
+        slots_c = staged("slots_c", 2 * T)
         sums_t2 = products("c", t2, first, T, 3)
-        on_scalar(*pieces(2, 4, (4, 5)))
-        on_scalar(*pieces(4, 3, (3,)))
-        on_scalar(*pieces(7, 2, (2,)))
-        scatter_s("c", t0, first, T, slots_c[:, 3 * first : 5 * first])
-        on_vector(*pieces(5, 6, (6, 7)))
-        on_vector(*pieces(6, 0, (0, 1)))
-        scatter_v("c", t1, slots_c[:, 5 * first :])
+        sums_t0 = products("c", t0, first, T, 2)
+        sums = [bank(n) for n in (4, 5, 6)]
+        for k in (0, 3, 2, 1, 4, 5):
+            one_pass(sums[k // 2][:, k % 2 * first : (k % 2 + 1) * first], "c", (t1, t3)[k // 3], k % 3)
+        sums = [acc[:] for acc in sums]
+        rest_t0 = staged("rest_c%d" % t0, BANK, "words_first_high")
+        on_scalar(rest_t0[:], sums_t0)
+        empty(on_scalar, slots_c, sums, 1)
+        scatter_s("c", t0, first, T, rest_t0[:])
+        empty(on_vector, slots_c, sums, 0)
+        empty(on_vector, slots_c, sums, 2)
+        scatter_v("c", t1, slots_c[:, :T])
 
         early, late = staged("slots_a_early", 2 * T), staged("slots_a_late", 2 * T)
         sums = in_three("a", (t1, t2), (0, 1, 2))
@@ -228,7 +225,7 @@ def tile_moe_pool_none_kernel(
         scatter_v("a", t2, early[:, T:])
         multiply(nc.gpsimd, t2)
         multiply(nc.gpsimd, t0)
-        scatter_s("c", t3, 0, T, slots_c[:, :T], 2 * T, "words_early")
+        scatter_s("c", t3, 0, T, slots_c[:, T:], 2 * T, "words_early")
         scatter_v("a", t3, late[:, T:], "in_tokens_a%d" % t1)
 
         def weave(j, copy, word, tokens=slice(None)):

from contextlib import ExitStack

import concourse.mybir as mybir

K, T, H, N = 512, 768, 512, 128
EXPERTS = {"a": 6, "c": 3}
SLOTS = {"a": 128, "c": 256}
FLOPS = 2 * (2 * K * H * T) + 2 * H * N * T

F32 = mybir.dt.float32
BF16 = mybir.dt.bfloat16
I32 = mybir.dt.int32
U32 = mybir.dt.uint32
U16 = mybir.dt.uint16
U8 = mybir.dt.uint8
FP8X4 = mybir.dt.float8_e4m3fn_x4
FP4X4 = mybir.dt.float4_e2m1fn_x4
COPY = mybir.ActivationFunctionType.Copy

P = 128
PACK = 4
PER_COLUMN = 16
BANK = 512
WINDOW = 1024
ORDER = (0, 2, 1, 3)
RANGES = [(0, 256), (256, 512), (512, 768)]


def tile_moe_pool_none_kernel(
    tc, x_words, x_scales, wa_words, wa_scales, wb_words, wb_scales, w2_words, w2_scales, offs, offs2, out
):
    nc = tc.nc
    with ExitStack() as ctx:
        keep = ctx.enter_context(tc.tile_pool(name="keep", bufs=1))
        psum = ctx.enter_context(tc.psum_pool(name="psum", bufs=1))

        def bank(n):
            return psum.tile([P, BANK], F32, name="bank%d" % n)

        def sbuf(place, shape, dtype):
            return keep.tile(shape, dtype, name=place, align_bytes=64)

        lists = {pool: keep.tile([P, T // PER_COLUMN], U16, name="list_" + pool) for pool in "ca"}
        x_w = sbuf("x_w", [P, WINDOW], I32)
        x_s = sbuf("x_s", [P, WINDOW], U8)
        raw_first = sbuf("raw_first", [P, 1, 2 * H], U8)
        raw_rest = sbuf("raw_rest", [P, EXPERTS["c"] - 1, 2 * H], U8)
        raw_a = sbuf("raw_a", [P, EXPERTS["a"], 2 * H], U8)
        raw_scales = {pool: sbuf("raw_scales_" + pool, [P, EXPERTS[pool], H], U8) for pool in "ca"}
        w2_w = sbuf("w2_w", [P, 2 * N], U8)
        ones = sbuf("ones", [P, 1], F32)

        for scale_tile in (raw_scales["c"], raw_scales["a"]):
            nc.gpsimd.memset(scale_tile[:].bitcast(I32), 0)
        nc.gpsimd.memset(ones[:], 1.0)

        def load_scales(scale_tile, rows):
            for r in range(4):
                nc.sync.dma_start(out=scale_tile[r:P:32].bitcast(I32), in_=rows[r:16:4].bitcast(I32))

        def load_token_scales(queue, q):
            rows = x_scales[0, 4 * q : 4 * q + 4].bitcast(I32)
            queue.dma_start(out=x_s[32 * q : 32 * q + 32, :T].bitcast(I32), in_=rows.partition_broadcast(8))

        def load_words(raw, words):
            nc.sync.dma_start(out=raw[:].bitcast(I32), in_=words[:, 0].rearrange("e p b -> p e b").bitcast(I32))

        nc.sync.dma_start(lists["c"][:], offs2)
        for q in range(4):
            load_token_scales(nc.sync if q < 2 else nc.scalar, q)
        nc.sync.dma_start(out=x_w[:, :T], in_=x_words[0].rearrange("p t d -> p (t d)").bitcast(I32))
        load_words(raw_first, wb_words[:1])
        load_scales(raw_scales["c"], wb_scales[:, 0].rearrange("e g i -> g e i"))
        load_words(raw_rest, wb_words[1:])
        nc.sync.dma_start(lists["a"][:], offs)
        load_scales(raw_scales["a"], wa_scales[:, 0].rearrange("e g i -> g e i"))
        load_words(raw_a, wa_words)
        nc.gpsimd.dma_start(out=w2_w[:].bitcast(I32), in_=w2_words[0].bitcast(I32))

        slot_words, slot_scales, part_words, part_scales, in_tokens = {}, {}, {}, {}, {}

        def entries(pool, lo, hi):
            return lists[pool][:, lo // PER_COLUMN : hi // PER_COLUMN]

        def gather(table, dtype, into, place, pool, lo, hi):
            gathered = sbuf(place, [P, hi - lo], dtype)
            nc.vector.tensor_copy(gathered[:], table[:].bitcast(dtype).indirect(entries(pool, lo, hi)))
            for slot in range(lo, hi, P):
                into[pool, slot] = gathered[:, slot - lo :]

        def pick(copy, raw, dtype, into, place, pool, first, parts):
            chosen = range(PACK)[parts]
            count, n = raw.shape[1], len(chosen)
            size = 2 if dtype == U16 else 1
            picked = sbuf(place, [P, count, n, size * P], U8)
            columns = raw.bitcast(dtype).rearrange("p e (m t) -> p e t m", t=PACK)
            copy(picked[:].bitcast(dtype), columns[:, :, parts, :])
            for e in range(count):
                for row, t in enumerate(chosen):
                    into[pool, t, first + e] = picked[:, e, row, :]

        def one_pass(sums, pool, t, e):
            width = SLOTS[pool]
            nc.tensor.matmul_mx(
                out=sums,
                lhsT=part_words[pool, t, e].bitcast(FP4X4),
                lhsT_scale=part_scales[pool, t, e],
                rhs=slot_words[pool, e * width][:, :width].bitcast(FP8X4),
                rhs_scale=slot_scales[pool, e * width][:, :width],
                start=True,
                stop=True,
            )

        def products(pool, t, lo, hi, n):
            acc = bank(n)
            width = SLOTS[pool]
            for e in range(lo // width, hi // width):
                one_pass(acc[:, e * width - lo : (e + 1) * width - lo], pool, t, e)
            return acc[:, : hi - lo]

        h_pairs = [sbuf("h_pairs%d" % j, [P, 2, hi - lo, 2], BF16) for j, (lo, hi) in enumerate(RANGES)]
        h_words = [sbuf("h_words%d" % j, [P, hi - lo, PACK], BF16) for j, (lo, hi) in enumerate(RANGES)]

        def multiply(engine, t):
            for j, (lo, hi) in enumerate(RANGES):
                engine.tensor_tensor(
                    h_pairs[j][:, t // 2, :, t % 2],
                    in_tokens["a", t][:, lo:hi],
                    in_tokens["c", t][:, lo:hi],
                    mybir.AluOpType.mult,
                )

        def scatter_v(pool, t, values, place=None):
            in_tokens[pool, t] = sbuf(place or "in_tokens_%s%d" % (pool, t), [P, WINDOW], F32)
            nc.vector.tensor_copy(in_tokens[pool, t][:].indirect(entries(pool, 0, T)), values)

        def scatter_s(pool, t, lo, hi, values, columns=None, place=None):
            if columns:
                in_tokens[pool, t] = sbuf(place or "in_tokens_%s%d" % (pool, t), [P, columns], F32)
            nc.scalar.activation(in_tokens[pool, t][:].indirect(entries(pool, lo, hi)), values, COPY, scale=ones[:])

        on_scalar, on_vector, on_gpsimd = nc.scalar.copy, nc.vector.tensor_copy, nc.gpsimd.tensor_copy
        t0, t1, t2, t3 = ORDER
        first = SLOTS["c"]
        low, high = slice(0, 2), slice(2, 4)

        def one(t):
            return slice(t, t + 1)

        def staged(name, width, place=None):
            return sbuf(place or name, [P, width], F32)

        gather(x_s, U8, slot_scales, "slot_scales_c0", "c", 0, BANK)
        gather(x_w, U32, slot_words, "slot_words_c0", "c", 0, first)
        pick(on_scalar, raw_first[:], U16, part_words, "words_first_low", "c", 0, low)
        for t in (t0, t2):
            pick(on_gpsimd, raw_scales["c"][:, :1], U8, part_scales, "scales_first%d" % t, "c", 0, one(t))
        pick(on_scalar, raw_first[:], U16, part_words, "words_first_high", "c", 0, high)
        gather(x_w, U32, slot_words, "slot_words_c1", "c", first, T)
        gather(x_s, U8, slot_scales, "raw_first", "c", BANK, T)
        pick(on_gpsimd, raw_rest[:], U16, part_words, "words_rest_low", "c", 1, low)
        pick(on_gpsimd, raw_scales["c"][:, 1:], U8, part_scales, "scales_rest_low", "c", 1, low)
        pick(on_gpsimd, raw_rest[:], U16, part_words, "words_rest_high", "c", 1, high)
        pick(on_gpsimd, raw_scales["c"][:], U8, part_scales, "scales_high", "c", 0, high)
        inner, outer = slice(1, 3), slice(0, 4, 3)
        pick(on_gpsimd, raw_scales["a"][:], U8, part_scales, "scales_early", "a", 0, inner)
        pick(on_gpsimd, raw_a[:], U16, part_words, "words_early", "a", 0, inner)
        pick(on_gpsimd, raw_a[:], U16, part_words, "words_late", "a", 0, outer)

        heads = {}
        for n, t in enumerate((t0, t2)):
            heads[t] = staged("head_c%d" % t, first)
            on_scalar(heads[t][:], products("c", t, 0, first, n))
        gather(x_w, U32, slot_words, "words_first_low", "a", 0, T)
        gather(x_s, U8, slot_scales, "scales_first%d" % t2, "a", 0, T)
        for t in (t0, t2):
            scatter_s("c", t, 0, first, heads[t][:], WINDOW)

        def in_three(pool, parts, banks):
            sums = []
            for n, bank_number in enumerate(banks):
                acc = bank(bank_number)
                width = SLOTS[pool]
                for column in range(n * BANK, (n + 1) * BANK, width):
                    one_pass(acc[:, column - n * BANK : column - n * BANK + width], pool, parts[column // T], column % T // width)
                sums.append(acc[:])
            return sums

        def empty(copy, staging, sums, n):
            copy(staging[:, n * BANK : (n + 1) * BANK], sums[n])

        slots_c = staged("slots_c", 2 * T)
        sums_t2 = products("c", t2, first, T, 3)
        sums_t0 = products("c", t0, first, T, 2)
        sums = [bank(n) for n in (4, 5, 6)]
        for k in (0, 3, 2, 1, 4, 5):
            one_pass(sums[k // 2][:, k % 2 * first : (k % 2 + 1) * first], "c", (t1, t3)[k // 3], k % 3)
        sums = [acc[:] for acc in sums]
        rest_t0 = staged("rest_c%d" % t0, BANK, "words_first_high")
        on_scalar(rest_t0[:], sums_t0)
        empty(on_scalar, slots_c, sums, 1)
        scatter_s("c", t0, first, T, rest_t0[:])
        empty(on_vector, slots_c, sums, 0)
        empty(on_vector, slots_c, sums, 2)
        scatter_v("c", t1, slots_c[:, :T])

        early, late = staged("slots_a_early", 2 * T), staged("slots_a_late", 2 * T)
        sums = in_three("a", (t1, t2), (0, 1, 2))
        empty(on_scalar, early, sums, 0)
        empty(on_scalar, early, sums, 1)
        rest_t2 = staged("rest_c%d" % t2, BANK, "scales_early")
        on_scalar(rest_t2[:], sums_t2)
        empty(on_scalar, early, sums, 2)
        pick(on_gpsimd, raw_scales["a"][:], U8, part_scales, "words_early", "a", 0, outer)
        scatter_v("a", t1, early[:, :T])
        multiply(nc.gpsimd, t1)
        scatter_s("c", t2, first, T, rest_t2[:])
        sums = in_three("a", (t0, t3), (4, 5, 6))
        for n in range(3):
            empty(on_scalar, late, sums, n)
        scatter_s("a", t0, 0, T, late[:, :T], 2 * T, "words_late")
        w2_s = sbuf("scales_early", [P, N], U8)
        nc.gpsimd.memset(w2_s[:].bitcast(I32), 0)
        load_scales(w2_s, w2_scales[0])
        scatter_v("a", t2, early[:, T:])
        multiply(nc.gpsimd, t2)
        multiply(nc.gpsimd, t0)
        scatter_s("c", t3, 0, T, slots_c[:, T:], 2 * T, "words_early")
        scatter_v("a", t3, late[:, T:], "in_tokens_a%d" % t1)

        def weave(j, copy, word, tokens=slice(None)):
            copy(
                h_words[j][:, tokens].rearrange("p c t -> p (c t)").bitcast(word).rearrange("p (c w) -> p c w", w=2),
                h_pairs[j][:, :, tokens].rearrange("p w c e -> p w (c e)").bitcast(word).rearrange("p w c -> p c w"),
            )

        result = sbuf("result", [P, T], F32)

        def store(queue, lo, hi):
            queue.dma_start(out=out[:, lo:hi], in_=result[:, lo:hi])

        def project(j, n, copy_out, tokens=slice(0, 2 * P)):
            lo, width = RANGES[j][0] + tokens.start, tokens.stop - tokens.start
            h_codes = sbuf("h_codes%d" % n, [P, width], U32)
            h_scales = sbuf("h_scales%d" % n, [P, width], U8)
            nc.vector.quantize_mx(
                out=h_codes[:].bitcast(FP8X4),
                scales=h_scales[:],
                in_=h_words[j][:, tokens].rearrange("p c t -> p (c t)"),
            )
            acc = bank(n)
            nc.tensor.matmul_mx(
                out=acc[:, :width],
                lhsT=w2_w[:].bitcast(FP4X4),
                lhsT_scale=w2_s[:],
                rhs=h_codes[:].bitcast(FP8X4),
                rhs_scale=h_scales[:],
                start=True,
                stop=True,
            )
            copy_out(result[:, lo : lo + width], acc[:, :width])

        multiply(nc.vector, t3)
        weave(0, on_scalar, U32)
        weave(1, on_vector, I32)
        weave(2, on_scalar, U32, slice(0, P))
        weave(2, on_scalar, U32, slice(P, 2 * P))
        project(0, 0, on_scalar)
        store(nc.sync, 0, 2 * P)
        project(1, 1, on_scalar)
        project(2, 2, on_scalar, slice(0, P))
        store(nc.scalar, 2 * P, T - P)
        project(2, 3, on_vector, slice(P, 2 * P))
        store(nc.sync, T - P, T)
